import numpy as np
import ml_dtypes


def mxq(x, axis, fmt="e4m3"):
    dtype, down = {"e4m3": (ml_dtypes.float8_e4m3fn, 7), "e5m2": (ml_dtypes.float8_e5m2, 14)}[fmt]
    v = np.moveaxis(np.asarray(x, np.float32).astype(ml_dtypes.bfloat16).astype(np.float64), axis, -1)
    blocks = v.reshape(v.shape[:-1] + (-1, 32))
    amax = np.abs(blocks).max(-1, keepdims=True)
    byte = np.maximum(np.where(amax > 0, np.frexp(amax)[1] - 1 + 127, 0) - down, 1)
    scale = np.exp2(byte - 127.0)
    codes = (blocks / scale).astype(np.float32).astype(dtype).astype(np.float64)
    return np.moveaxis((codes * scale).reshape(v.shape), -1, axis)


WIDE = False


def mx_kscale(k):
    if not WIDE:
        return np.ones(k)
    levels = np.array([10, -10, 5, -5, 0])
    if k % 512:
        return np.exp2(np.random.permutation(np.resize(levels, k // 32))).repeat(32)
    a = np.empty((k // 512, 16))
    for p in range(k // 512):
        a[p, :8] = np.random.permutation(np.resize(levels, 8))
        for g in range(8):
            far = levels[np.abs(levels - a[p, g]) >= 10]
            a[p, g + 8] = far[np.random.randint(len(far))]
    return np.exp2(a.ravel()).repeat(32)


def f64(x):
    return np.asarray(x).astype(np.float64)


def striped(idx):
    return np.tile(idx.reshape(-1, 16).T, (8, 1)).astype(np.uint16)


def unstriped(offs):
    return offs[:16].T.reshape(-1).astype(np.int64)


E2M1 = np.array([0.0, 0.5, 1.0, 1.5, 2.0, 3.0, 4.0, 6.0, -0.0, -0.5, -1.0, -1.5, -2.0, -3.0, -4.0, -6.0])


def pack_weight(w, fmt):
    k, n = w.shape
    w = f64(np.asarray(w, np.float32).astype(ml_dtypes.bfloat16)).reshape(k // 32, 32, n)
    amax = np.abs(w).max(1)
    if fmt == "e4m3":
        byte = np.frexp(amax)[1] - 1 + 127 - 7
    else:
        mant, ex = np.frexp(amax / 6.0)
        byte = np.where(mant > 0.5, ex, ex - 1) + 127
    byte = np.clip(np.where(amax > 0, byte, 1), 1, 254)
    scaled = (w * np.exp2(127.0 - byte)[:, None, :]).reshape(k, n).astype(np.float32)
    by_word = np.ascontiguousarray(scaled.reshape(k // 512, 128, 4, n).transpose(0, 1, 3, 2))
    if fmt == "e4m3":
        words = by_word.astype(ml_dtypes.float8_e4m3fn).view(np.uint8)
    else:
        c = by_word.astype(ml_dtypes.float4_e2m1fn).view(np.uint8) & 0xF
        words = (c[..., 0::2] | (c[..., 1::2] << 4)).reshape(k // 512, 128, 2 * n)
    return np.ascontiguousarray(words), np.ascontiguousarray(byte.astype(np.uint8).reshape(k // 512, 16, n))


def unpack_weight(words, scales, fmt):
    g, _, n = scales.shape
    words = np.ascontiguousarray(words).reshape(g, 128, n, -1)
    if fmt == "e4m3":
        vals = words.view(ml_dtypes.float8_e4m3fn).astype(np.float64)
    else:
        nib = np.empty((g, 128, n, 4), np.uint8)
        nib[..., 0::2] = words & 0xF
        nib[..., 1::2] = words >> 4
        vals = E2M1[nib]
    vals = vals * np.repeat(np.exp2(scales.astype(np.float64) - 127.0), 8, axis=1)[..., None]
    return vals.transpose(0, 1, 3, 2).reshape(g * 512, n)


def sigmoid(v):
    return 1.0 / (1.0 + np.exp(-np.maximum(v, -700.0)))


def d_sigmoid(v):
    s = 1.0 / (1.0 + np.exp(-np.maximum(v, -700.0)))
    return s * (1.0 - s)


K, T, E, C, H, N = 128, 1280, 15, 256, 512, 512
TOP = 3


def by_expert(wq, xq):
    return np.concatenate([wq[e].T @ xq[:, e * C:(e + 1) * C] for e in range(E)], axis=1)


def setup_inputs():
    n = np.random.standard_normal
    s = mx_kscale(N)[:, None]
    u = mx_kscale(H)
    deal = np.repeat(np.arange(E), C).reshape(TOP, T)[:, np.random.permutation(T)]
    deal = np.take_along_axis(deal, np.argsort(np.random.rand(TOP, T), axis=0), axis=0)
    for _ in range(8):
        s_, t_ = np.random.permutation(T).reshape(2, -1); r = np.random.randint(TOP, size=T // 2); x, y = deal[r, s_].copy(), deal[r, t_].copy()
        ok = ~((deal[:, s_] == y).any(0) | (deal[:, t_] == x).any(0)); deal[r[ok], s_[ok]] = y[ok]; deal[r[ok], t_[ok]] = x[ok]
    order = np.lexsort((np.random.rand(TOP * T), deal.reshape(-1)))
    slot_token = order % T; pos = np.empty(TOP * T, np.int64); pos[order] = np.arange(TOP * T); pos = pos.reshape(TOP, T)
    g = np.random.uniform(0.5, 1.5, (TOP, T)); g = g / g.sum(0)
    w_slot = np.empty(E * C)
    for r in range(TOP): w_slot[pos[r]] = g[r]
    w2 = [pack_weight(m, "e2m1") for m in n((E, N, H)) / np.sqrt(N) / s[None] * u[None, None, :]]
    w1 = [pack_weight(m, "e2m1") for m in n((E, H, K)) / np.sqrt(H) / u[None, :, None]]
    w3 = [pack_weight(m, "e2m1") for m in n((E, H, K)) / np.sqrt(H) / u[None, :, None]]
    return {
        "dyT": (n((N, T)) * s).astype(np.float32),
        "a1": n((H, E * C)).astype(np.float32),
        "a3": n((H, E * C)).astype(np.float32),
        "w2_words": np.stack([m[0] for m in w2]),
        "w2_scales": np.stack([m[1] for m in w2]),
        "w1_words": np.stack([m[0] for m in w1]),
        "w1_scales": np.stack([m[1] for m in w1]),
        "w3_words": np.stack([m[0] for m in w3]),
        "w3_scales": np.stack([m[1] for m in w3]),
        "gate": np.tile(w_slot, (N, 1)).astype(np.float32),
        "offs": striped(slot_token),
        "pos1": striped(pos[0]),
        "pos2": striped(pos[1]),
        "pos3": striped(pos[2]),
    }


def reference(dyT, a1, a3, w2_words, w2_scales, w1_words, w1_scales, w3_words, w3_scales, gate, offs, pos1, pos2, pos3):
    idx = unstriped(offs)
    w2 = np.stack([unpack_weight(w2_words[e], w2_scales[e], "e2m1") for e in range(E)])
    w1 = np.stack([unpack_weight(w1_words[e], w1_scales[e], "e2m1") for e in range(E)])
    w3 = np.stack([unpack_weight(w3_words[e], w3_scales[e], "e2m1") for e in range(E)])
    gq = mxq(f64(gate) * f64(dyT)[:, idx], 0, "e4m3")
    dh = by_expert(w2, gq)
    da1 = dh * f64(a3) * d_sigmoid(f64(a1))
    da3 = dh * sigmoid(f64(a1))
    dx = by_expert(w1, mxq(da1, 0, "e4m3")) + by_expert(w3, mxq(da3, 0, "e4m3"))
    return dx[:, unstriped(pos1)] + dx[:, unstriped(pos2)] + dx[:, unstriped(pos3)]

@@ -1,0 +1,302 @@
+from contextlib import ExitStack
+
+import concourse.mybir as mybir
+
+K, T, E, C, H, N = 128, 1280, 15, 256, 512, 512
+S = E * C
+P = 128
+PACK = 4
+GROUP = 128
+FLOPS = 2 * S * (N * H + 2 * H * K)
+BYTES = 4 * (N * T + 2 * H * S + S + K * T) + E * (N * H + 2 * H * K) * 17 // 32 + 2 * P * (S + 3 * T) // 16
+
+F32 = mybir.dt.float32
+BF16 = mybir.dt.bfloat16
+I32 = mybir.dt.int32
+U32 = mybir.dt.uint32
+U16 = mybir.dt.uint16
+U8 = mybir.dt.uint8
+FP8X4 = mybir.dt.float8_e4m3fn_x4
+FP4X4 = mybir.dt.float4_e2m1fn_x4
+ACT = mybir.ActivationFunctionType
+MULT = mybir.AluOpType.mult
+ADD = mybir.AluOpType.add
+
+UNITS = [1, 2, 2, 2, 2, 2, 2, 2]
+HEAD = 2
+U_ON_VECTOR = 2
+OUT_CUTS = [0, 768, 1280]
+SPAN = PACK * 2 * C
+OVERLAP = 16
+PAIR = 2
+
+
+def planes_by_pairs(ap):
+    return ap.rearrange("p t (c i) -> p c t i", i=PAIR)
+
+
+def words_by_pairs(ap):
+    return ap.rearrange("p (c i) t -> p c t i", i=PAIR)
+
+
+def tile_moe_bdx_glu_sigmoid_kernel(
+    tc, dyT, a1, a3, w2_words, w2_scales, w1_words, w1_scales, w3_words, w3_scales, gate, offs, pos1, pos2, pos3, out
+):
+    nc = tc.nc
+    first = [sum(UNITS[:k]) for k in range(len(UNITS))]
+    last = len(UNITS) - 1
+
+    with ExitStack() as ctx:
+        keep = ctx.enter_context(tc.tile_pool(name="keep", bufs=1))
+        ring2 = ctx.enter_context(tc.tile_pool(name="ring2", bufs=2))
+        ring3 = ctx.enter_context(tc.tile_pool(name="ring3", bufs=3))
+        psum_dh = ctx.enter_context(tc.psum_pool(name="psum_dh", bufs=6))
+        psum_dx = ctx.enter_context(tc.psum_pool(name="psum_dx", bufs=2))
+
+        offs_sb = keep.tile([P, S // 16], U16, name="offs_sb")
+        pos_sb = [keep.tile([P, T // 16], U16, name="pos_sb%d" % r) for r in range(3)]
+        dy = [keep.tile([P, T], F32, name="dy%d" % t) for t in range(PACK)]
+        dx = keep.tile([P, S], F32, name="dx")
+        s2_raw = keep.tile([P, E, H], U8, name="s2_raw", align_bytes=64)
+        s2 = keep.tile([P, E, H], U8, name="s2", align_bytes=64)
+        w13 = [keep.tile([P, E, 2 * K], U8, name="w13_%d" % m, align_bytes=64) for m in range(2)]
+        s13 = [keep.tile([P, E, K], U8, name="s13_%d" % m, align_bytes=64) for m in range(2)]
+        turn = [keep.tile([P, PACK * 2 * C], F32, name="turn%d" % r) for r in range(4)]
+        pair = [keep.tile([P, PACK * 2 * C], F32, name="pair%d" % r) for r in range(2)]
+        arena = [keep.tile([P, 2 * SPAN], F32, name="arena%d" % r, align_bytes=64) for r in range(3)]
+        raw = [keep.tile([P, SPAN], F32, name="raw%d" % r, align_bytes=64) for r in range(2)]
+        minus_half = keep.tile([P, 1], F32, name="minus_half")
+
+        nc.vector.memset(s2_raw[:].bitcast(I32), 0)
+        nc.vector.memset(minus_half[:], -0.5)
+        for plane in s13:
+            nc.gpsimd.memset(plane[:].bitcast(I32), 0)
+
+        gu, g_f32, g_bf, g_codes, g_scales = {}, {}, {}, {}, {}
+        sig, a3_sb, dsig, w2_raw, w2, dh, da, da_codes, da_scales = {}, {}, {}, {}, {}, {}, {}, {}, {}
+
+        def slots(k):
+            return slice(first[k] * C, (first[k] + UNITS[k]) * C)
+
+        def width(k):
+            return UNITS[k] * C
+
+        def planes(tiles, r, k):
+            return tiles[r % len(tiles)][:, : PACK * width(k)].rearrange("p (t s) -> p t s", t=PACK)
+
+        def load_scale_rows(plane, scales, experts):
+            for quad in range(4):
+                nc.sync.dma_start(
+                    plane[32 * quad : 32 * quad + 4, experts, :].bitcast(I32),
+                    scales[experts, 0, 4 * quad : 4 * quad + 4, :].rearrange("e f n -> f e n").bitcast(I32),
+                )
+
+        def gate_planes(k):
+            end = SPAN + OVERLAP
+            return arena[k % 3][:, end - PACK * width(k) : end].rearrange("p (t s) -> p t s", t=PACK)
+
+        def u_planes(k):
+            return arena[k % 3][:, SPAN : SPAN + PACK * width(k)].rearrange("p (t s) -> p t s", t=PACK)
+
+        def load_gate(k, t0=0, t1=PACK):
+            nc.sync.dma_start(gate_planes(k)[:, t0:t1, :], gate.rearrange("(p t) s -> p t s", t=PACK)[:, t0:t1, slots(k)])
+
+        def load_a1(k):
+            nc.sync.dma_start(planes(raw, k, k), a1.rearrange("(p t) s -> p t s", t=PACK)[:, :, slots(k)])
+
+        def load_a3(k):
+            a3_sb[k] = ring2.tile([P, PACK, width(k)], F32, name="a3_sb")
+            nc.sync.dma_start(a3_sb[k][:], a3.rearrange("(p t) s -> p t s", t=PACK)[:, :, slots(k)])
+
+        def load_w2(k):
+            w2_raw[k] = ring2.tile([P, UNITS[k], 2 * H], U8, name="w2_raw", align_bytes=64)
+            nc.sync.dma_start(
+                w2_raw[k][:].bitcast(I32),
+                w2_words[first[k] : first[k] + UNITS[k], 0, :, :].rearrange("e p b -> p e b").bitcast(I32),
+            )
+
+        def permute_w2(k):
+            w2[k] = ring2.tile([P, UNITS[k], 2 * H], U8, name="w2", align_bytes=64)
+            nc.vector.tensor_copy(
+                w2[k][:].bitcast(U16).rearrange("p e (t m) -> p e t m", t=PACK),
+                w2_raw[k][:].bitcast(U16).rearrange("p e (m t) -> p e t m", t=PACK),
+            )
+            experts = slice(first[k], first[k] + UNITS[k])
+            nc.vector.tensor_copy(
+                s2[:, experts, :].rearrange("p e (t m) -> p e t m", t=PACK),
+                s2_raw[:, experts, :].rearrange("p e (m t) -> p e t m", t=PACK),
+            )
+
+        def gather(k, t):
+            if t == 0:
+                g_f32[k] = planes(turn, k - 2, k) if k < HEAD else planes(pair, k, k)
+            cols = slice(first[k] * C // 16, (first[k] + UNITS[k]) * C // 16)
+            nc.vector.tensor_tensor(g_f32[k][:, t, :], dy[t][:].indirect(offs_sb[:, cols]), gate_planes(k)[:, (0 if k < HEAD else t), :], MULT)
+
+        def round_g(k):
+            home = arena[0] if k == 0 else raw[(k + 1) % 2]
+            g_bf[k] = home[:, : PACK * width(k) // 2].bitcast(BF16).rearrange("p (c t) -> p c t", t=PACK)
+            nc.scalar.activation(words_by_pairs(g_bf[k][:]), planes_by_pairs(g_f32[k][:]), ACT.Copy)
+
+        def quantize_g(k):
+            g_codes[k] = ring2.tile([P, width(k)], U32, name="g_codes", align_bytes=64)
+            g_scales[k] = ring2.tile([P, width(k)], U8, name="g_scales", align_bytes=64)
+            nc.vector.quantize_mx(
+                out=g_codes[k][:].bitcast(FP8X4), scales=g_scales[k][:], in_=g_bf[k][:].rearrange("p c t -> p (c t)")
+            )
+
+        def multiply_w2(k):
+            for j in range(width(k) // GROUP):
+                e = j * GROUP // C
+                cols = slice(j * GROUP, (j + 1) * GROUP)
+                dh[k, j] = psum_dh.tile([P, PACK, GROUP], F32, name="dh")
+                for t in range(PACK):
+                    nc.tensor.matmul_mx(
+                        out=dh[k, j][:, t, :],
+                        lhsT=w2[k][:, e, 2 * P * t : 2 * P * (t + 1)].bitcast(FP4X4),
+                        lhsT_scale=s2[:, first[k] + e, P * t : P * (t + 1)],
+                        rhs=g_codes[k][:, cols].bitcast(FP8X4),
+                        rhs_scale=g_scales[k][:, cols],
+                        start=True,
+                        stop=True,
+                    )
+
+        def sigmoids(k):
+            sig[k] = planes(turn, k, k)
+            nc.scalar.activation(sig[k][:], planes(raw, k, k), ACT.Sigmoid)
+            nc.scalar.activation(planes(pair, k, k), sig[k][:], ACT.Square, bias=minus_half[:])
+
+        def derivative(k):
+            dsig[k] = planes(pair, k, k) if k < HEAD else planes(turn, k - 2, k)
+            nc.scalar.activation(dsig[k][:], planes(pair, k, k), ACT.Copy, bias=0.25, scale=-1.0)
+
+        def factor_u(k):
+            if k < U_ON_VECTOR:
+                nc.vector.tensor_tensor(u_planes(k), dsig[k][:], a3_sb[k][:], MULT)
+            else:
+                nc.gpsimd.tensor_tensor(u_planes(k), dsig[k][:], a3_sb[k][:], MULT)
+
+        def make_da(k, j):
+            if j == 0:
+                groups = width(k) // GROUP
+                da[k] = arena[(k + 1) % 3][:, SPAN - PACK * width(k) : SPAN].bitcast(BF16).rearrange(
+                    "p (j m c t) -> p j m c t", m=2, c=GROUP, t=PACK
+                )
+                da_codes[k] = ring2.tile([P, groups, 2, GROUP], U32, name="da_codes", align_bytes=64)
+                da_scales[k] = ring2.tile([P, groups, 2, GROUP], U8, name="da_scales", align_bytes=64)
+            cols = slice(j * GROUP, (j + 1) * GROUP)
+            for m, factor in ((1, sig[k]), (0, u_planes(k))):
+                nc.vector.tensor_tensor(
+                    words_by_pairs(da[k][:, j, m, :, :]),
+                    planes_by_pairs(dh[k, j][:]),
+                    planes_by_pairs(factor[:, :, cols]),
+                    MULT,
+                )
+
+        def finish(k, j0, j1):
+            nc.vector.quantize_mx(
+                out=da_codes[k][:, j0:j1, :, :].rearrange("p j m c -> p (j m c)").bitcast(FP8X4),
+                scales=da_scales[k][:, j0:j1, :, :].rearrange("p j m c -> p (j m c)"),
+                in_=da[k][:, j0:j1, :, :, :].rearrange("p j m c t -> p (j m c t)"),
+            )
+            dx_ps = psum_dx.tile([P, (j1 - j0) * GROUP], F32, name="dx_ps")
+            for j in range(j0, j1):
+                e = first[k] + j * GROUP // C
+                for m in range(2):
+                    nc.tensor.matmul_mx(
+                        out=dx_ps[:, (j - j0) * GROUP : (j - j0 + 1) * GROUP],
+                        lhsT=w13[m][:, e, :].bitcast(FP4X4),
+                        lhsT_scale=s13[m][:, e, :],
+                        rhs=da_codes[k][:, j, m, :].bitcast(FP8X4),
+                        rhs_scale=da_scales[k][:, j, m, :],
+                        start=(m == 0),
+                        stop=(m == 1),
+                    )
+            base = first[k] * C
+            nc.scalar.copy(dx[:, base + j0 * GROUP : base + j1 * GROUP], dx_ps[:])
+
+        dy_rows = dyT.rearrange("(p t) c -> p t c", t=PACK)
+        load_a1(0)
+        nc.sync.dma_start(offs_sb[:], offs)
+        nc.sync.dma_start(dy[0][:], dy_rows[:, 0, :])
+        load_gate(0, 0, 0 + 1)
+        load_gate(1, 0, 0 + 1)
+        nc.sync.dma_start(dy[1][:], dy_rows[:, 1, :])
+        load_a1(1)
+        nc.sync.dma_start(dy[2][:], dy_rows[:, 2, :])
+        nc.sync.dma_start(dy[3][:], dy_rows[:, 3, :])
+        load_w2(0)
+        load_scale_rows(s2_raw, w2_scales, slice(0, first[2]))
+        load_a3(0)
+
+        sigmoids(0)
+        derivative(0)
+        load_a1(2)
+        load_gate(2)
+        load_w2(1)
+        load_a3(1)
+        for t in range(PACK):
+            for k in range(HEAD):
+                gather(k, t)
+        round_g(0)
+        sigmoids(1)
+        derivative(1)
+        factor_u(0)
+        permute_w2(0)
+        quantize_g(0)
+        multiply_w2(0)
+
+        for k in range(len(UNITS)):
+            groups = width(k) // GROUP
+            if k + 3 <= last:
+                load_a1(k + 3)
+            if k == 0:
+                load_w2(2)
+                load_a3(2)
+                load_scale_rows(s2_raw, w2_scales, slice(first[2], E))
+                for m, scales in enumerate((w1_scales, w3_scales)):
+                    load_scale_rows(s13[m], scales, slice(0, E))
+                for m, words in enumerate((w1_words, w3_words)):
+                    nc.sync.dma_start(w13[m][:].bitcast(I32), words[:, 0, :, :].rearrange("e p b -> p e b").bitcast(I32))
+            elif k + 2 <= last:
+                load_a3(k + 2)
+                load_w2(k + 2)
+            if k == 2:
+                for r, pos in enumerate((pos1, pos2, pos3)):
+                    nc.sync.dma_start(pos_sb[r][:], pos)
+            if k < last:
+                if k + 2 <= last:
+                    sigmoids(k + 2)
+                if k + 1 >= HEAD:
+                    for t in range(PACK):
+                        gather(k + 1, t)
+                round_g(k + 1)
+                if k + 1 >= U_ON_VECTOR:
+                    factor_u(k + 1)
+                for j in range(groups):
+                    make_da(k, j)
+                if k + 2 <= last:
+                    derivative(k + 2)
+                permute_w2(k + 1)
+                if k + 1 < U_ON_VECTOR:
+                    factor_u(k + 1)
+                finish(k, 0, groups)
+                if k + 3 <= last:
+                    load_gate(k + 3)
+                quantize_g(k + 1)
+                multiply_w2(k + 1)
+            else:
+                for j in range(groups):
+                    make_da(k, j)
+                    if j > 0:
+                        finish(k, j - 1, j)
+                finish(k, groups - 1, groups)
+
+        for c0, c1 in zip(OUT_CUTS[:-1], OUT_CUTS[1:]):
+            parts = [turn[r][:, c0:c1] for r in range(3)]
+            for r in range(3):
+                nc.vector.tensor_copy(parts[r][:], dx[:].indirect(pos_sb[r][:, c0 // 16 : c1 // 16]))
+                if r == 2:
+                    nc.vector.tensor_tensor(parts[0][:], parts[0][:], parts[1][:], ADD)
+            nc.vector.tensor_tensor(parts[0][:], parts[0][:], parts[2][:], ADD)
+            nc.sync.dma_start(out[:, c0:c1], parts[0][:])

@@ -23,9 +23,12 @@ MULT = mybir.AluOpType.mult
 ADD = mybir.AluOpType.add
 
 UNITS = [1, 2, 2, 2, 2, 2, 2, 2]
-HEAD = 2
+HEAD = 3
 U_ON_VECTOR = 2
-OUT_CUTS = [0, 768, 1280]
+OUT_CUTS = [0, 800, 1280]
+FREE = 3
+DIRECT = 3
+DECK = 3
 SPAN = PACK * 2 * C
 OVERLAP = 16
 PAIR = 2
@@ -49,7 +52,6 @@ def tile_moe_bdx_glu_sigmoid_kernel(
     with ExitStack() as ctx:
         keep = ctx.enter_context(tc.tile_pool(name="keep", bufs=1))
         ring2 = ctx.enter_context(tc.tile_pool(name="ring2", bufs=2))
-        ring3 = ctx.enter_context(tc.tile_pool(name="ring3", bufs=3))
         psum_dh = ctx.enter_context(tc.psum_pool(name="psum_dh", bufs=6))
         psum_dx = ctx.enter_context(tc.psum_pool(name="psum_dx", bufs=2))
 
@@ -62,13 +64,15 @@ def tile_moe_bdx_glu_sigmoid_kernel(
         w13 = [keep.tile([P, E, 2 * K], U8, name="w13_%d" % m, align_bytes=64) for m in range(2)]
         s13 = [keep.tile([P, E, K], U8, name="s13_%d" % m, align_bytes=64) for m in range(2)]
         turn = [keep.tile([P, PACK * 2 * C], F32, name="turn%d" % r) for r in range(4)]
-        pair = [keep.tile([P, PACK * 2 * C], F32, name="pair%d" % r) for r in range(2)]
-        arena = [keep.tile([P, 2 * SPAN], F32, name="arena%d" % r, align_bytes=64) for r in range(3)]
+        pair = [keep.tile([P, 2 * SPAN], F32, name="pair%d" % r, align_bytes=64) for r in range(2)]
+        arena = [keep.tile([P, SPAN // 2 + SPAN], F32, name="arena%d" % r) for r in range(3)]
         raw = [keep.tile([P, SPAN], F32, name="raw%d" % r, align_bytes=64) for r in range(2)]
+        spare = keep.tile([P, SPAN], F32, name="spare")
         minus_half = keep.tile([P, 1], F32, name="minus_half")
 
         nc.vector.memset(s2_raw[:].bitcast(I32), 0)
         nc.vector.memset(minus_half[:], -0.5)
+        nc.vector.memset(dx[:, 0:S:C], 0.25)
         for plane in s13:
             nc.gpsimd.memset(plane[:].bitcast(I32), 0)
 
@@ -92,13 +96,19 @@ def tile_moe_bdx_glu_sigmoid_kernel(
                 )
 
         def gate_planes(k):
-            end = SPAN + OVERLAP
-            return arena[k % 3][:, end - PACK * width(k) : end].rearrange("p (t s) -> p t s", t=PACK)
+            start = 0 if k < FREE else OVERLAP
+            return arena[k % 3][:, start : start + 2 * width(k)].rearrange("p (t s) -> p t s", t=2)
 
         def u_planes(k):
-            return arena[k % 3][:, SPAN : SPAN + PACK * width(k)].rearrange("p (t s) -> p t s", t=PACK)
+            return arena[k % 3][:, SPAN // 2 : SPAN // 2 + PACK * width(k)].rearrange("p (t s) -> p t s", t=PACK)
 
-        def load_gate(k, t0=0, t1=PACK):
+        def pieces(ap):
+            return ap.rearrange("p t (j c) -> p (t j) c", c=GROUP)
+
+        def square_pieces(k):
+            return pair[k % 2][:, : 2 * PACK * width(k)].rearrange("p (n c) -> p n c", c=2 * GROUP)[:, :, :GROUP]
+
+        def load_gate(k, t0=0, t1=2):
             nc.sync.dma_start(gate_planes(k)[:, t0:t1, :], gate.rearrange("(p t) s -> p t s", t=PACK)[:, t0:t1, slots(k)])
 
         def load_a1(k):
@@ -115,6 +125,13 @@ def tile_moe_bdx_glu_sigmoid_kernel(
                 w2_words[first[k] : first[k] + UNITS[k], 0, :, :].rearrange("e p b -> p e b").bitcast(I32),
             )
 
+        def load_w13(k):
+            experts = slice(first[k], first[k] + UNITS[k])
+            for m, words in enumerate((w1_words, w3_words)):
+                nc.sync.dma_start(
+                    w13[m][:, experts, :].bitcast(I32), words[experts, 0, :, :].rearrange("e p b -> p e b").bitcast(I32)
+                )
+
         def permute_w2(k):
             w2[k] = ring2.tile([P, UNITS[k], 2 * H], U8, name="w2", align_bytes=64)
             nc.vector.tensor_copy(
@@ -129,12 +146,12 @@ def tile_moe_bdx_glu_sigmoid_kernel(
 
         def gather(k, t):
             if t == 0:
-                g_f32[k] = planes(turn, k - 2, k) if k < HEAD else planes(pair, k, k)
+                g_f32[k] = planes((turn[2], turn[3], spare), k, k) if k < FREE else planes(pair, k, k)
             cols = slice(first[k] * C // 16, (first[k] + UNITS[k]) * C // 16)
-            nc.vector.tensor_tensor(g_f32[k][:, t, :], dy[t][:].indirect(offs_sb[:, cols]), gate_planes(k)[:, (0 if k < HEAD else t), :], MULT)
+            nc.vector.tensor_tensor(g_f32[k][:, t, :], dy[t][:].indirect(offs_sb[:, cols]), gate_planes(k)[:, (0 if k < FREE or t == PACK - 1 else 1), :], MULT)
 
         def round_g(k):
-            home = arena[0] if k == 0 else raw[(k + 1) % 2]
+            home = pair[0][:, SPAN:] if k == 0 else raw[(k + 1) % 2]
             g_bf[k] = home[:, : PACK * width(k) // 2].bitcast(BF16).rearrange("p (c t) -> p c t", t=PACK)
             nc.scalar.activation(words_by_pairs(g_bf[k][:]), planes_by_pairs(g_f32[k][:]), ACT.Copy)
 
@@ -164,11 +181,17 @@ def tile_moe_bdx_glu_sigmoid_kernel(
         def sigmoids(k):
             sig[k] = planes(turn, k, k)
             nc.scalar.activation(sig[k][:], planes(raw, k, k), ACT.Sigmoid)
-            nc.scalar.activation(planes(pair, k, k), sig[k][:], ACT.Square, bias=minus_half[:])
+            nc.scalar.activation(square_pieces(k), pieces(sig[k]), ACT.Square, bias=minus_half[:])
 
         def derivative(k):
-            dsig[k] = planes(pair, k, k) if k < HEAD else planes(turn, k - 2, k)
-            nc.scalar.activation(dsig[k][:], planes(pair, k, k), ACT.Copy, bias=0.25, scale=-1.0)
+            dsig[k] = u_planes(k) if k < 2 else planes(turn, k - 2, k)
+            col = first[max(k - 2, 0)] * C
+            quarter = dx[:, col : col + 1]
+            half = PACK * width(k) // GROUP // 2
+            for part in (slice(0, half), slice(half, 2 * half)):
+                nc.scalar.activation(
+                    pieces(dsig[k])[:, part, :], square_pieces(k)[:, part, :], ACT.Identity, bias=quarter, scale=-1.0
+                )
 
         def factor_u(k):
             if k < U_ON_VECTOR:
@@ -179,7 +202,7 @@ def tile_moe_bdx_glu_sigmoid_kernel(
         def make_da(k, j):
             if j == 0:
                 groups = width(k) // GROUP
-                da[k] = arena[(k + 1) % 3][:, SPAN - PACK * width(k) : SPAN].bitcast(BF16).rearrange(
+                da[k] = pair[(k + 1) % 2][:, SPAN : SPAN + PACK * width(k)].bitcast(BF16).rearrange(
                     "p (j m c t) -> p j m c t", m=2, c=GROUP, t=PACK
                 )
                 da_codes[k] = ring2.tile([P, groups, 2, GROUP], U32, name="da_codes", align_bytes=64)
@@ -217,22 +240,22 @@ def tile_moe_bdx_glu_sigmoid_kernel(
 
         dy_rows = dyT.rearrange("(p t) c -> p t c", t=PACK)
         load_a1(0)
-        nc.sync.dma_start(offs_sb[:], offs)
         nc.sync.dma_start(dy[0][:], dy_rows[:, 0, :])
-        load_gate(0, 0, 0 + 1)
-        load_gate(1, 0, 0 + 1)
+        nc.sync.dma_start(offs_sb[:], offs)
+        load_gate(0, 0, 1)
+        load_gate(1, 0, 1)
+        load_gate(2, 0, 1)
         nc.sync.dma_start(dy[1][:], dy_rows[:, 1, :])
         load_a1(1)
         nc.sync.dma_start(dy[2][:], dy_rows[:, 2, :])
-        nc.sync.dma_start(dy[3][:], dy_rows[:, 3, :])
-        load_w2(0)
-        load_scale_rows(s2_raw, w2_scales, slice(0, first[2]))
-        load_a3(0)
 
         sigmoids(0)
         derivative(0)
         load_a1(2)
-        load_gate(2)
+        nc.sync.dma_start(dy[3][:], dy_rows[:, 3, :])
+        load_a3(0)
+        load_w2(0)
+        load_scale_rows(s2_raw, w2_scales, slice(0, DIRECT))
         load_w2(1)
         load_a3(1)
         for t in range(PACK):
@@ -250,18 +273,12 @@ def tile_moe_bdx_glu_sigmoid_kernel(
             groups = width(k) // GROUP
             if k + 3 <= last:
                 load_a1(k + 3)
-            if k == 0:
-                load_w2(2)
-                load_a3(2)
-                load_scale_rows(s2_raw, w2_scales, slice(first[2], E))
-                for m, scales in enumerate((w1_scales, w3_scales)):
-                    load_scale_rows(s13[m], scales, slice(0, E))
-                for m, words in enumerate((w1_words, w3_words)):
-                    nc.sync.dma_start(w13[m][:].bitcast(I32), words[:, 0, :, :].rearrange("e p b -> p e b").bitcast(I32))
-            elif k + 2 <= last:
+            if k + 2 <= last:
                 load_a3(k + 2)
                 load_w2(k + 2)
-            if k == 2:
+            if k == 0:
+                load_scale_rows(s2_raw, w2_scales, slice(DIRECT, E))
+            if k == 3:
                 for r, pos in enumerate((pos1, pos2, pos3)):
                     nc.sync.dma_start(pos_sb[r][:], pos)
             if k < last:
@@ -277,12 +294,18 @@ def tile_moe_bdx_glu_sigmoid_kernel(
                     make_da(k, j)
                 if k + 2 <= last:
                     derivative(k + 2)
+                if k + 3 <= last:
+                    load_gate(k + 3)
+                if k == 0:
+                    for m, scales in enumerate((w1_scales, w3_scales)):
+                        load_scale_rows(s13[m], scales, slice(0, E))
+                if k == 0:
+                    load_w13(0)
+                load_w13(k + 1)
                 permute_w2(k + 1)
                 if k + 1 < U_ON_VECTOR:
                     factor_u(k + 1)
                 finish(k, 0, groups)
-                if k + 3 <= last:
-                    load_gate(k + 3)
                 quantize_g(k + 1)
                 multiply_w2(k + 1)
             else:

@@ -22,16 +22,16 @@ ACT = mybir.ActivationFunctionType
 MULT = mybir.AluOpType.mult
 ADD = mybir.AluOpType.add
 
-UNITS = [1, 2, 2, 2, 2, 2, 2, 2]
+UNITS = [2, 2, 2, 2, 2, 2, 2, 1]
 HEAD = 3
-U_ON_VECTOR = 2
+U_ON_VECTOR = 1
 OUT_CUTS = [0, 800, 1280]
 FREE = 3
-DIRECT = 3
+DIRECT = 4
 DECK = 3
 SPAN = PACK * 2 * C
 OVERLAP = 16
-PAIR = 2
+PAIR = 4
 
 
 def planes_by_pairs(ap):
@@ -65,9 +65,10 @@ def tile_moe_bdx_glu_sigmoid_kernel(
         s13 = [keep.tile([P, E, K], U8, name="s13_%d" % m, align_bytes=64) for m in range(2)]
         turn = [keep.tile([P, PACK * 2 * C], F32, name="turn%d" % r) for r in range(4)]
         pair = [keep.tile([P, 2 * SPAN], F32, name="pair%d" % r, align_bytes=64) for r in range(2)]
-        arena = [keep.tile([P, SPAN // 2 + SPAN], F32, name="arena%d" % r) for r in range(3)]
+        arena = [keep.tile([P, SPAN // 2 + SPAN], F32, name="arena%d" % r, align_bytes=64) for r in range(3)]
         raw = [keep.tile([P, SPAN], F32, name="raw%d" % r, align_bytes=64) for r in range(2)]
         spare = keep.tile([P, SPAN], F32, name="spare")
+        spare_d = keep.tile([P, SPAN], F32, name="spare_d")
         minus_half = keep.tile([P, 1], F32, name="minus_half")
 
         nc.vector.memset(s2_raw[:].bitcast(I32), 0)
@@ -151,7 +152,7 @@ def tile_moe_bdx_glu_sigmoid_kernel(
             nc.vector.tensor_tensor(g_f32[k][:, t, :], dy[t][:].indirect(offs_sb[:, cols]), gate_planes(k)[:, (0 if k < FREE or t == PACK - 1 else 1), :], MULT)
 
         def round_g(k):
-            home = pair[0][:, SPAN:] if k == 0 else raw[(k + 1) % 2]
+            home = arena[1][:, SPAN // 2 :] if k == 0 else raw[(k + 1) % 2]
             g_bf[k] = home[:, : PACK * width(k) // 2].bitcast(BF16).rearrange("p (c t) -> p c t", t=PACK)
             nc.scalar.activation(words_by_pairs(g_bf[k][:]), planes_by_pairs(g_f32[k][:]), ACT.Copy)
 
@@ -184,7 +185,7 @@ def tile_moe_bdx_glu_sigmoid_kernel(
             nc.scalar.activation(square_pieces(k), pieces(sig[k]), ACT.Square, bias=minus_half[:])
 
         def derivative(k):
-            dsig[k] = u_planes(k) if k < 2 else planes(turn, k - 2, k)
+            dsig[k] = (u_planes(0), planes((spare_d,), 0, 1))[k] if k < 2 else planes(turn, k - 2, k)
             col = first[max(k - 2, 0)] * C
             quarter = dx[:, col : col + 1]
             half = PACK * width(k) // GROUP // 2
@@ -239,25 +240,25 @@ def tile_moe_bdx_glu_sigmoid_kernel(
             nc.scalar.copy(dx[:, base + j0 * GROUP : base + j1 * GROUP], dx_ps[:])
 
         dy_rows = dyT.rearrange("(p t) c -> p t c", t=PACK)
-        load_a1(0)
         nc.sync.dma_start(dy[0][:], dy_rows[:, 0, :])
         nc.sync.dma_start(offs_sb[:], offs)
         load_gate(0, 0, 1)
         load_gate(1, 0, 1)
         load_gate(2, 0, 1)
+        load_a1(0)
         nc.sync.dma_start(dy[1][:], dy_rows[:, 1, :])
-        load_a1(1)
         nc.sync.dma_start(dy[2][:], dy_rows[:, 2, :])
-
-        sigmoids(0)
-        derivative(0)
-        load_a1(2)
+        load_a1(1)
         nc.sync.dma_start(dy[3][:], dy_rows[:, 3, :])
         load_a3(0)
         load_w2(0)
         load_scale_rows(s2_raw, w2_scales, slice(0, DIRECT))
-        load_w2(1)
+
+        sigmoids(0)
+        derivative(0)
+        load_a1(2)
         load_a3(1)
+        load_w2(1)
         for t in range(PACK):
             for k in range(HEAD):
                 gather(k, t)
@@ -305,9 +306,9 @@ def tile_moe_bdx_glu_sigmoid_kernel(
                 permute_w2(k + 1)
                 if k + 1 < U_ON_VECTOR:
                     factor_u(k + 1)
-                finish(k, 0, groups)
                 quantize_g(k + 1)
                 multiply_w2(k + 1)
+                finish(k, 0, groups)
             else:
                 for j in range(groups):
                     make_da(k, j)

@@ -317,10 +317,10 @@ def tile_moe_bdx_glu_sigmoid_kernel(
                 finish(k, groups - 1, groups)
 
         for c0, c1 in zip(OUT_CUTS[:-1], OUT_CUTS[1:]):
+            adder = nc.vector if c1 == T else nc.gpsimd
             parts = [turn[r][:, c0:c1] for r in range(3)]
             for r in range(3):
-                nc.vector.tensor_copy(parts[r][:], dx[:].indirect(pos_sb[r][:, c0 // 16 : c1 // 16]))
-                if r == 2:
-                    nc.vector.tensor_tensor(parts[0][:], parts[0][:], parts[1][:], ADD)
-            nc.vector.tensor_tensor(parts[0][:], parts[0][:], parts[2][:], ADD)
-            nc.sync.dma_start(out[:, c0:c1], parts[0][:])
+                nc.vector.tensor_copy(parts[r], dx[:].indirect(pos_sb[r][:, c0 // 16 : c1 // 16]))
+            adder.tensor_tensor(parts[0], parts[0], parts[1], ADD)
+            adder.tensor_tensor(parts[0], parts[0], parts[2], ADD)
+            nc.sync.dma_start(out[:, c0:c1], parts[0])

@@ -22,24 +22,22 @@ ACT = mybir.ActivationFunctionType
 MULT = mybir.AluOpType.mult
 ADD = mybir.AluOpType.add
 
-UNITS = [2, 2, 2, 2, 2, 2, 2, 1]
-HEAD = 3
-U_ON_VECTOR = 1
-OUT_CUTS = [0, 800, 1280]
-FREE = 3
-DIRECT = 4
-DECK = 3
-SPAN = PACK * 2 * C
-OVERLAP = 16
-PAIR = 4
+UNITS = [1, 1, 2, 2, 2, 2, 2, 2, 1]
+AHEAD = 3
+RING = 3
+LONG_RING = 4
+WIDE = 2 * C
+SPAN = PACK * WIDE
+OUT_CUTS = [0, 768, 1280]
+RUN = 4
 
 
-def planes_by_pairs(ap):
-    return ap.rearrange("p t (c i) -> p c t i", i=PAIR)
+def planes_by_runs(ap):
+    return ap.rearrange("p t (c i) -> p c t i", i=RUN)
 
 
-def words_by_pairs(ap):
-    return ap.rearrange("p (c i) t -> p c t i", i=PAIR)
+def words_by_runs(ap):
+    return ap.rearrange("p (c i) t -> p c t i", i=RUN)
 
 
 def tile_moe_bdx_glu_sigmoid_kernel(
@@ -51,7 +49,9 @@ def tile_moe_bdx_glu_sigmoid_kernel(
 
     with ExitStack() as ctx:
         keep = ctx.enter_context(tc.tile_pool(name="keep", bufs=1))
+        turns = ctx.enter_context(tc.tile_pool(name="turns", bufs=1))
         ring2 = ctx.enter_context(tc.tile_pool(name="ring2", bufs=2))
+        ring3 = ctx.enter_context(tc.tile_pool(name="ring3", bufs=3))
         psum_dh = ctx.enter_context(tc.psum_pool(name="psum_dh", bufs=6))
         psum_dx = ctx.enter_context(tc.psum_pool(name="psum_dx", bufs=2))
 
@@ -59,268 +59,295 @@ def tile_moe_bdx_glu_sigmoid_kernel(
         pos_sb = [keep.tile([P, T // 16], U16, name="pos_sb%d" % r) for r in range(3)]
         dy = [keep.tile([P, T], F32, name="dy%d" % t) for t in range(PACK)]
         dx = keep.tile([P, S], F32, name="dx")
-        s2_raw = keep.tile([P, E, H], U8, name="s2_raw", align_bytes=64)
-        s2 = keep.tile([P, E, H], U8, name="s2", align_bytes=64)
+        stacked = keep.tile([P, 2, H], U8, name="stacked", align_bytes=64)
+        s2 = [keep.tile([P, 2, H], U8, name="s2_%d" % a, align_bytes=64) for a in range(3)]
         w13 = [keep.tile([P, E, 2 * K], U8, name="w13_%d" % m, align_bytes=64) for m in range(2)]
         s13 = [keep.tile([P, E, K], U8, name="s13_%d" % m, align_bytes=64) for m in range(2)]
-        turn = [keep.tile([P, PACK * 2 * C], F32, name="turn%d" % r) for r in range(4)]
-        pair = [keep.tile([P, 2 * SPAN], F32, name="pair%d" % r, align_bytes=64) for r in range(2)]
-        arena = [keep.tile([P, SPAN // 2 + SPAN], F32, name="arena%d" % r, align_bytes=64) for r in range(3)]
-        raw = [keep.tile([P, SPAN], F32, name="raw%d" % r, align_bytes=64) for r in range(2)]
-        spare = keep.tile([P, SPAN], F32, name="spare")
-        spare_d = keep.tile([P, SPAN], F32, name="spare_d")
+        g_home = [keep.tile([P, SPAN], F32, name="g_home%d" % r, align_bytes=64) for r in range(LONG_RING)]
+        u_home = [keep.tile([P, GROUP + SPAN], F32, name="u_home%d" % r, align_bytes=64) for r in range(LONG_RING)]
+        s_home = [keep.tile([P, SPAN], F32, name="s_home%d" % r) for r in range(LONG_RING)]
         minus_half = keep.tile([P, 1], F32, name="minus_half")
 
-        nc.vector.memset(s2_raw[:].bitcast(I32), 0)
         nc.vector.memset(minus_half[:], -0.5)
         nc.vector.memset(dx[:, 0:S:C], 0.25)
+        nc.vector.memset(stacked[:, 1, :].bitcast(I32), 0)
         for plane in s13:
             nc.gpsimd.memset(plane[:].bitcast(I32), 0)
+        for plane in s2[1:]:
+            nc.gpsimd.memset(plane[:].bitcast(I32), 0)
 
-        gu, g_f32, g_bf, g_codes, g_scales = {}, {}, {}, {}, {}
-        sig, a3_sb, dsig, w2_raw, w2, dh, da, da_codes, da_scales = {}, {}, {}, {}, {}, {}, {}, {}, {}
-
-        def slots(k):
-            return slice(first[k] * C, (first[k] + UNITS[k]) * C)
+        a3_sb, dsig, w2_raw, mx, dh, da_mx, g_bf = {}, {}, {}, {}, {}, {}, {}
 
         def width(k):
             return UNITS[k] * C
 
-        def planes(tiles, r, k):
-            return tiles[r % len(tiles)][:, : PACK * width(k)].rearrange("p (t s) -> p t s", t=PACK)
+        def slots(k):
+            return slice(first[k] * C, (first[k] + UNITS[k]) * C)
 
-        def load_scale_rows(plane, scales, experts):
-            for quad in range(4):
-                nc.sync.dma_start(
-                    plane[32 * quad : 32 * quad + 4, experts, :].bitcast(I32),
-                    scales[experts, 0, 4 * quad : 4 * quad + 4, :].rearrange("e f n -> f e n").bitcast(I32),
-                )
+        def as_planes(ap):
+            return ap.rearrange("p (t s) -> p t s", t=PACK)
 
-        def gate_planes(k):
-            start = 0 if k < FREE else OVERLAP
-            return arena[k % 3][:, start : start + 2 * width(k)].rearrange("p (t s) -> p t s", t=2)
+        def s_planes(k):
+            return as_planes(s_home[k % LONG_RING][:, : PACK * width(k)])
+
+        def g_planes(k):
+            return as_planes(g_home[k % LONG_RING][:, : PACK * width(k)])
 
         def u_planes(k):
-            return arena[k % 3][:, SPAN // 2 : SPAN // 2 + PACK * width(k)].rearrange("p (t s) -> p t s", t=PACK)
+            if k + 2 > last:
+                return as_planes(g_home[(k - 2) % LONG_RING][:, : PACK * width(k)])
+            return as_planes(u_home[k % LONG_RING][:, GROUP : GROUP + PACK * width(k)])
 
-        def pieces(ap):
-            return ap.rearrange("p t (j c) -> p (t j) c", c=GROUP)
+        def gate_row(k):
+            if k < 2:
+                return u_home[1][:, WIDE + first[k] * C : WIDE + first[k] * C + width(k)]
+            return u_home[(k - 2) % LONG_RING][:, : width(k)]
 
-        def square_pieces(k):
-            return pair[k % 2][:, : 2 * PACK * width(k)].rearrange("p (n c) -> p n c", c=2 * GROUP)[:, :, :GROUP]
 
-        def load_gate(k, t0=0, t1=2):
-            nc.sync.dma_start(gate_planes(k)[:, t0:t1, :], gate.rearrange("(p t) s -> p t s", t=PACK)[:, t0:t1, slots(k)])
+        def da_words(k):
+            return g_home[k % LONG_RING][:, : PACK * width(k)].bitcast(BF16).rearrange(
+                "p (j m c t) -> p j m c t", m=2, c=GROUP, t=PACK
+            )
+
+        def load_dy(t):
+            nc.sync.dma_start(dy[t][:], dyT.rearrange("(p t) c -> p t c", t=PACK)[:, t, :])
+
+        def load_gate(k):
+            nc.sync.dma_start(gate_row(k), gate[:P, slots(k)])
 
         def load_a1(k):
-            nc.sync.dma_start(planes(raw, k, k), a1.rearrange("(p t) s -> p t s", t=PACK)[:, :, slots(k)])
+            nc.sync.dma_start(s_planes(k), a1.rearrange("(p t) s -> p t s", t=PACK)[:, :, slots(k)])
 
         def load_a3(k):
-            a3_sb[k] = ring2.tile([P, PACK, width(k)], F32, name="a3_sb")
+            a3_sb[k] = ring3.tile([P, PACK, width(k)], F32, name="a3_sb")
             nc.sync.dma_start(a3_sb[k][:], a3.rearrange("(p t) s -> p t s", t=PACK)[:, :, slots(k)])
 
         def load_w2(k):
-            w2_raw[k] = ring2.tile([P, UNITS[k], 2 * H], U8, name="w2_raw", align_bytes=64)
+            w2_raw[k] = ring3.tile([P, UNITS[k], 2 * H], U8, name="w2_raw", align_bytes=64)
             nc.sync.dma_start(
                 w2_raw[k][:].bitcast(I32),
                 w2_words[first[k] : first[k] + UNITS[k], 0, :, :].rearrange("e p b -> p e b").bitcast(I32),
             )
 
-        def load_w13(k):
-            experts = slice(first[k], first[k] + UNITS[k])
+        def load_w13():
             for m, words in enumerate((w1_words, w3_words)):
+                nc.sync.dma_start(w13[m][:].bitcast(I32), words[:, 0, :, :].rearrange("e p b -> p e b").bitcast(I32))
+
+        def load_s13():
+            for plane, scales in zip(s13, (w1_scales, w3_scales)):
+                for quad in range(4):
+                    nc.gpsimd.dma_start(
+                        plane[32 * quad : 32 * quad + 4, :, :].bitcast(I32),
+                        scales[:, 0, 4 * quad : 4 * quad + 4, :].rearrange("e f n -> f e n").bitcast(I32),
+                    )
+
+        def load_s2():
+            for b in range(2):
+                count = (E - b + 1) // 2
+                for quad in range(4):
+                    nc.sync.dma_start(
+                        stacked[32 * quad : 32 * quad + 4 * count, b, :].bitcast(I32),
+                        w2_scales[b::2, 0, 4 * quad : 4 * quad + 4, :].bitcast(I32),
+                    )
+
+        def reorder_s2():
+            nc.vector.tensor_copy(
+                s2[0][:].rearrange("p b (t m) -> p b t m", t=PACK),
+                stacked[:].rearrange("p b (m t) -> p b t m", t=PACK),
+            )
+
+        def unstack_s2(k):
+            a = first[k] // 2
+            for quad in range(4):
                 nc.sync.dma_start(
-                    w13[m][:, experts, :].bitcast(I32), words[experts, 0, :, :].rearrange("e p b -> p e b").bitcast(I32)
+                    s2[1 + k % 2][32 * quad : 32 * quad + 4, : UNITS[k], :].bitcast(I32),
+                    s2[0][32 * quad + 4 * a : 32 * quad + 4 * a + 4, : UNITS[k], :].bitcast(I32),
                 )
 
-        def permute_w2(k):
-            w2[k] = ring2.tile([P, UNITS[k], 2 * H], U8, name="w2", align_bytes=64)
-            nc.vector.tensor_copy(
-                w2[k][:].bitcast(U16).rearrange("p e (t m) -> p e t m", t=PACK),
-                w2_raw[k][:].bitcast(U16).rearrange("p e (m t) -> p e t m", t=PACK),
-            )
-            experts = slice(first[k], first[k] + UNITS[k])
-            nc.vector.tensor_copy(
-                s2[:, experts, :].rearrange("p e (t m) -> p e t m", t=PACK),
-                s2_raw[:, experts, :].rearrange("p e (m t) -> p e t m", t=PACK),
-            )
-
         def gather(k, t):
-            if t == 0:
-                g_f32[k] = planes((turn[2], turn[3], spare), k, k) if k < FREE else planes(pair, k, k)
-            cols = slice(first[k] * C // 16, (first[k] + UNITS[k]) * C // 16)
-            nc.vector.tensor_tensor(g_f32[k][:, t, :], dy[t][:].indirect(offs_sb[:, cols]), gate_planes(k)[:, (0 if k < FREE or t == PACK - 1 else 1), :], MULT)
+            pieces = [(GROUP, width(k)), (0, GROUP)] if t == PACK - 1 and k >= AHEAD else [(0, width(k))]
+            for c0, c1 in pieces:
+                base = first[k] * C
+                nc.vector.tensor_tensor(
+                    g_planes(k)[:, t, c0:c1],
+                    dy[t][:].indirect(offs_sb[:, (base + c0) // 16 : (base + c1) // 16]),
+                    gate_row(k)[:, c0:c1],
+                    MULT,
+                )
 
         def round_g(k):
-            home = arena[1][:, SPAN // 2 :] if k == 0 else raw[(k + 1) % 2]
-            g_bf[k] = home[:, : PACK * width(k) // 2].bitcast(BF16).rearrange("p (c t) -> p c t", t=PACK)
-            nc.scalar.activation(words_by_pairs(g_bf[k][:]), planes_by_pairs(g_f32[k][:]), ACT.Copy)
+            g_bf[k] = turns.tile([P, width(k), PACK], BF16, tag="swap%d" % (k % 2), name="g_bf", align_bytes=64)
+            nc.scalar.activation(words_by_runs(g_bf[k][:]), planes_by_runs(g_planes(k)), ACT.Copy)
 
-        def quantize_g(k):
-            g_codes[k] = ring2.tile([P, width(k)], U32, name="g_codes", align_bytes=64)
-            g_scales[k] = ring2.tile([P, width(k)], U8, name="g_scales", align_bytes=64)
+        def sigmoids(k):
+            dsig[k] = turns.tile([P, PACK, width(k)], F32, tag="turn%d" % (k % RING), name="dsig", align_bytes=64)
+            nc.scalar.activation(s_planes(k), s_planes(k), ACT.Sigmoid)
+            square = turns.tile([P, PACK, width(k)], F32, tag="swap%d" % (k % 2), name="square", align_bytes=64)
+            nc.scalar.activation(square[:], s_planes(k), ACT.Square, bias=minus_half[:])
+            col = first[max(k - 2, 0)] * C
+            nc.scalar.activation(dsig[k][:], square[:], ACT.Identity, bias=dx[:, col : col + 1], scale=-1.0)
+
+        def gpsimd_planes(k):
+            return 0 if k == 0 else PACK * min(width(k - 1), width(k)) // width(k)
+
+        def factor_u(engine, k, t0, t1):
+            if t1 > t0:
+                engine.tensor_tensor(u_planes(k)[:, t0:t1, :], dsig[k][:, t0:t1, :], a3_sb[k][:, t0:t1, :], MULT)
+
+        def w2_view(k):
+            return mx[k][:, : UNITS[k] * 2 * H].rearrange("p (e b) -> p e b", b=2 * H)
+
+        def g_codes(k):
+            return mx[k][:, 4 * H : 4 * H + 4 * width(k)].bitcast(U32)
+
+        def g_scales(k):
+            return mx[k][:, 4 * H + 4 * WIDE : 4 * H + 4 * WIDE + width(k)]
+
+        def first_product(k):
+            mx[k] = turns.tile([P, 4 * H + 5 * WIDE], U8, tag="turn%d" % (k % RING), name="mx", align_bytes=64)
             nc.vector.quantize_mx(
-                out=g_codes[k][:].bitcast(FP8X4), scales=g_scales[k][:], in_=g_bf[k][:].rearrange("p c t -> p (c t)")
+                out=g_codes(k).bitcast(FP8X4), scales=g_scales(k), in_=g_bf[k][:].rearrange("p c t -> p (c t)")
             )
-
-        def multiply_w2(k):
+            nc.vector.tensor_copy(
+                w2_view(k).bitcast(U16).rearrange("p e (t m) -> p e t m", t=PACK),
+                w2_raw[k][:].bitcast(U16).rearrange("p e (m t) -> p e t m", t=PACK),
+            )
             for j in range(width(k) // GROUP):
                 e = j * GROUP // C
+                expert = first[k] + e
                 cols = slice(j * GROUP, (j + 1) * GROUP)
                 dh[k, j] = psum_dh.tile([P, PACK, GROUP], F32, name="dh")
                 for t in range(PACK):
                     nc.tensor.matmul_mx(
                         out=dh[k, j][:, t, :],
-                        lhsT=w2[k][:, e, 2 * P * t : 2 * P * (t + 1)].bitcast(FP4X4),
-                        lhsT_scale=s2[:, first[k] + e, P * t : P * (t + 1)],
-                        rhs=g_codes[k][:, cols].bitcast(FP8X4),
-                        rhs_scale=g_scales[k][:, cols],
+                        lhsT=w2_view(k)[:, e, 2 * P * t : 2 * P * (t + 1)].bitcast(FP4X4),
+                        lhsT_scale=s2[0 if expert < 2 else 1 + k % 2][:, expert % 2, P * t : P * (t + 1)],
+                        rhs=g_codes(k)[:, cols].bitcast(FP8X4),
+                        rhs_scale=g_scales(k)[:, cols],
                         start=True,
                         stop=True,
                     )
 
-        def sigmoids(k):
-            sig[k] = planes(turn, k, k)
-            nc.scalar.activation(sig[k][:], planes(raw, k, k), ACT.Sigmoid)
-            nc.scalar.activation(square_pieces(k), pieces(sig[k]), ACT.Square, bias=minus_half[:])
-
-        def derivative(k):
-            dsig[k] = (u_planes(0), planes((spare_d,), 0, 1))[k] if k < 2 else planes(turn, k - 2, k)
-            col = first[max(k - 2, 0)] * C
-            quarter = dx[:, col : col + 1]
-            half = PACK * width(k) // GROUP // 2
-            for part in (slice(0, half), slice(half, 2 * half)):
-                nc.scalar.activation(
-                    pieces(dsig[k])[:, part, :], square_pieces(k)[:, part, :], ACT.Identity, bias=quarter, scale=-1.0
-                )
-
-        def factor_u(k):
-            if k < U_ON_VECTOR:
-                nc.vector.tensor_tensor(u_planes(k), dsig[k][:], a3_sb[k][:], MULT)
-            else:
-                nc.gpsimd.tensor_tensor(u_planes(k), dsig[k][:], a3_sb[k][:], MULT)
-
-        def make_da(k, j):
-            if j == 0:
-                groups = width(k) // GROUP
-                da[k] = pair[(k + 1) % 2][:, SPAN : SPAN + PACK * width(k)].bitcast(BF16).rearrange(
-                    "p (j m c t) -> p j m c t", m=2, c=GROUP, t=PACK
-                )
-                da_codes[k] = ring2.tile([P, groups, 2, GROUP], U32, name="da_codes", align_bytes=64)
-                da_scales[k] = ring2.tile([P, groups, 2, GROUP], U8, name="da_scales", align_bytes=64)
-            cols = slice(j * GROUP, (j + 1) * GROUP)
-            for m, factor in ((1, sig[k]), (0, u_planes(k))):
-                nc.vector.tensor_tensor(
-                    words_by_pairs(da[k][:, j, m, :, :]),
-                    planes_by_pairs(dh[k, j][:]),
-                    planes_by_pairs(factor[:, :, cols]),
-                    MULT,
-                )
-
-        def finish(k, j0, j1):
-            nc.vector.quantize_mx(
-                out=da_codes[k][:, j0:j1, :, :].rearrange("p j m c -> p (j m c)").bitcast(FP8X4),
-                scales=da_scales[k][:, j0:j1, :, :].rearrange("p j m c -> p (j m c)"),
-                in_=da[k][:, j0:j1, :, :, :].rearrange("p j m c t -> p (j m c t)"),
-            )
-            dx_ps = psum_dx.tile([P, (j1 - j0) * GROUP], F32, name="dx_ps")
-            for j in range(j0, j1):
-                e = first[k] + j * GROUP // C
-                for m in range(2):
-                    nc.tensor.matmul_mx(
-                        out=dx_ps[:, (j - j0) * GROUP : (j - j0 + 1) * GROUP],
-                        lhsT=w13[m][:, e, :].bitcast(FP4X4),
-                        lhsT_scale=s13[m][:, e, :],
-                        rhs=da_codes[k][:, j, m, :].bitcast(FP8X4),
-                        rhs_scale=da_scales[k][:, j, m, :],
-                        start=(m == 0),
-                        stop=(m == 1),
+        def make_da(k):
+            for j in range(width(k) // GROUP):
+                cols = slice(j * GROUP, (j + 1) * GROUP)
+                for m, factor in ((1, s_planes(k)), (0, u_planes(k))):
+                    nc.vector.tensor_tensor(
+                        words_by_runs(da_words(k)[:, j, m, :, :]),
+                        planes_by_runs(dh[k, j][:]),
+                        planes_by_runs(factor[:, :, cols]),
+                        MULT,
                     )
-            base = first[k] * C
-            nc.scalar.copy(dx[:, base + j0 * GROUP : base + j1 * GROUP], dx_ps[:])
 
-        dy_rows = dyT.rearrange("(p t) c -> p t c", t=PACK)
-        nc.sync.dma_start(dy[0][:], dy_rows[:, 0, :])
+        def da_codes(k):
+            return da_mx[k][:, : 8 * width(k)].bitcast(U32).rearrange("p (j m c) -> p j m c", m=2, c=GROUP)
+
+        def da_scales(k):
+            return da_mx[k][:, 8 * WIDE : 8 * WIDE + 2 * width(k)].rearrange("p (j m c) -> p j m c", m=2, c=GROUP)
+
+        def second_product(k):
+            groups = width(k) // GROUP
+            da_mx[k] = turns.tile([P, 10 * WIDE], U8, tag="swap%d" % ((k + 1) % 2), name="da_mx", align_bytes=64)
+            halves = [(0, groups // 2), (groups // 2, groups)]
+            for j0, j1 in halves:
+                nc.vector.quantize_mx(
+                    out=da_codes(k)[:, j0:j1, :, :].rearrange("p j m c -> p (j m c)").bitcast(FP8X4),
+                    scales=da_scales(k)[:, j0:j1, :, :].rearrange("p j m c -> p (j m c)"),
+                    in_=da_words(k)[:, j0:j1, :, :, :].rearrange("p j m c t -> p (j m c t)"),
+                )
+            for j0, j1 in halves if k == last else [(0, groups)]:
+                dx_ps = psum_dx.tile([P, (j1 - j0) * GROUP], F32, name="dx_ps")
+                for j in range(j0, j1):
+                    e = first[k] + j * GROUP // C
+                    for m in range(2):
+                        nc.tensor.matmul_mx(
+                            out=dx_ps[:, (j - j0) * GROUP : (j - j0 + 1) * GROUP],
+                            lhsT=w13[m][:, e, :].bitcast(FP4X4),
+                            lhsT_scale=s13[m][:, e, :],
+                            rhs=da_codes(k)[:, j, m, :].bitcast(FP8X4),
+                            rhs_scale=da_scales(k)[:, j, m, :],
+                            start=(m == 0),
+                            stop=(m == 1),
+                        )
+                base = first[k] * C
+                nc.scalar.copy(dx[:, base + j0 * GROUP : base + j1 * GROUP], dx_ps[:])
+
+        load_s13()
+        load_dy(0)
         nc.sync.dma_start(offs_sb[:], offs)
-        load_gate(0, 0, 1)
-        load_gate(1, 0, 1)
-        load_gate(2, 0, 1)
+        nc.sync.dma_start(u_home[1][:, WIDE : 2 * WIDE], gate[:P, :WIDE])
+        load_gate(2)
+        load_gate(3)
+        load_dy(1)
         load_a1(0)
-        nc.sync.dma_start(dy[1][:], dy_rows[:, 1, :])
-        nc.sync.dma_start(dy[2][:], dy_rows[:, 2, :])
+        load_dy(2)
+        load_s2()
         load_a1(1)
-        nc.sync.dma_start(dy[3][:], dy_rows[:, 3, :])
+        load_dy(3)
         load_a3(0)
         load_w2(0)
-        load_scale_rows(s2_raw, w2_scales, slice(0, DIRECT))
+        load_a3(1)
+        load_a1(2)
+        load_w2(1)
 
         sigmoids(0)
-        derivative(0)
-        load_a1(2)
-        load_a3(1)
-        load_w2(1)
-        for t in range(PACK):
-            for k in range(HEAD):
-                gather(k, t)
-        round_g(0)
         sigmoids(1)
-        derivative(1)
-        factor_u(0)
-        permute_w2(0)
-        quantize_g(0)
-        multiply_w2(0)
+        for t in range(PACK):
+            for k in range(AHEAD + 1):
+                if (k, t) != (AHEAD, PACK - 1):
+                    gather(k, t)
+        reorder_s2()
+        load_gate(4)
+        load_w13()
+        load_a3(2)
+        load_a1(3)
+        load_gate(5)
+        load_w2(2)
+        unstack_s2(2)
+        round_g(0)
+        round_g(1)
+        factor_u(nc.vector, 0, 0, PACK)
+        first_product(0)
+        sigmoids(2)
+        gather(AHEAD, PACK - 1)
 
         for k in range(len(UNITS)):
-            groups = width(k) // GROUP
-            if k + 3 <= last:
-                load_a1(k + 3)
+            if 0 < k and k + AHEAD <= last:
+                for t in range(PACK - 1):
+                    gather(k + AHEAD, t)
+                factor_u(nc.vector, k + 1, gpsimd_planes(k + 1), PACK)
+                gather(k + AHEAD, PACK - 1)
+            if k < last:
+                factor_u(nc.gpsimd, k + 1, 0, gpsimd_planes(k + 1))
             if k + 2 <= last:
-                load_a3(k + 2)
-                load_w2(k + 2)
-            if k == 0:
-                load_scale_rows(s2_raw, w2_scales, slice(DIRECT, E))
+                round_g(k + 2)
+            make_da(k)
+            if k + 6 <= last:
+                load_gate(k + 6)
+            if k + 3 <= last:
+                load_a3(k + 3)
+            if k + 4 <= last:
+                load_a1(k + 4)
+            if k < last:
+                first_product(k + 1)
+            if k + 3 <= last:
+                load_w2(k + 3)
+            second_product(k)
+            if k + 3 <= last:
+                sigmoids(k + 3)
+            if k + 3 <= last:
+                unstack_s2(k + 3)
             if k == 3:
                 for r, pos in enumerate((pos1, pos2, pos3)):
                     nc.sync.dma_start(pos_sb[r][:], pos)
-            if k < last:
-                if k + 2 <= last:
-                    sigmoids(k + 2)
-                if k + 1 >= HEAD:
-                    for t in range(PACK):
-                        gather(k + 1, t)
-                round_g(k + 1)
-                if k + 1 >= U_ON_VECTOR:
-                    factor_u(k + 1)
-                for j in range(groups):
-                    make_da(k, j)
-                if k + 2 <= last:
-                    derivative(k + 2)
-                if k + 3 <= last:
-                    load_gate(k + 3)
-                if k == 0:
-                    for m, scales in enumerate((w1_scales, w3_scales)):
-                        load_scale_rows(s13[m], scales, slice(0, E))
-                if k == 0:
-                    load_w13(0)
-                load_w13(k + 1)
-                permute_w2(k + 1)
-                if k + 1 < U_ON_VECTOR:
-                    factor_u(k + 1)
-                quantize_g(k + 1)
-                multiply_w2(k + 1)
-                finish(k, 0, groups)
-            else:
-                for j in range(groups):
-                    make_da(k, j)
-                    if j > 0:
-                        finish(k, j - 1, j)
-                finish(k, groups - 1, groups)
 
-        for c0, c1 in zip(OUT_CUTS[:-1], OUT_CUTS[1:]):
-            adder = nc.vector if c1 == T else nc.gpsimd
-            parts = [turn[r][:, c0:c1] for r in range(3)]
-            for r in range(3):
-                nc.vector.tensor_copy(parts[r], dx[:].indirect(pos_sb[r][:, c0 // 16 : c1 // 16]))
-            adder.tensor_tensor(parts[0], parts[0], parts[1], ADD)
-            adder.tensor_tensor(parts[0], parts[0], parts[2], ADD)
-            nc.sync.dma_start(out[:, c0:c1], parts[0])
+        chunks = list(zip(OUT_CUTS[:-1], OUT_CUTS[1:]))
+        for r in range(3):
+            for c0, c1 in chunks:
+                picked = dx[:].indirect(pos_sb[r][:, c0 // 16 : c1 // 16])
+                if r == 0:
+                    nc.vector.tensor_copy(s_home[0][:, c0:c1], picked)
+                else:
+                    nc.vector.tensor_tensor(s_home[r][:, c0:c1], picked, s_home[r - 1][:, c0:c1], ADD)
+                if r == 2:
+                    nc.sync.dma_start(out[:, c0:c1], s_home[r][:, c0:c1])

@@ -28,8 +28,9 @@ RING = 3
 LONG_RING = 4
 WIDE = 2 * C
 SPAN = PACK * WIDE
-OUT_CUTS = [0, 768, 1280]
+OUT_CUTS = [0, 800, 1280]
 RUN = 4
+EARLY = 4
 
 
 def planes_by_runs(ap):
@@ -129,26 +130,27 @@ def tile_moe_bdx_glu_sigmoid_kernel(
                 w2_words[first[k] : first[k] + UNITS[k], 0, :, :].rearrange("e p b -> p e b").bitcast(I32),
             )
 
-        def load_w13():
+        def load_w13(e0, e1):
             for m, words in enumerate((w1_words, w3_words)):
-                nc.sync.dma_start(w13[m][:].bitcast(I32), words[:, 0, :, :].rearrange("e p b -> p e b").bitcast(I32))
+                nc.sync.dma_start(
+                    w13[m][:, e0:e1, :].bitcast(I32), words[e0:e1, 0, :, :].rearrange("e p b -> p e b").bitcast(I32)
+                )
 
         def load_s13():
             for plane, scales in zip(s13, (w1_scales, w3_scales)):
                 for quad in range(4):
-                    nc.gpsimd.dma_start(
+                    nc.sync.dma_start(
                         plane[32 * quad : 32 * quad + 4, :, :].bitcast(I32),
                         scales[:, 0, 4 * quad : 4 * quad + 4, :].rearrange("e f n -> f e n").bitcast(I32),
                     )
 
-        def load_s2():
+        def load_s2(quad):
             for b in range(2):
                 count = (E - b + 1) // 2
-                for quad in range(4):
-                    nc.sync.dma_start(
-                        stacked[32 * quad : 32 * quad + 4 * count, b, :].bitcast(I32),
-                        w2_scales[b::2, 0, 4 * quad : 4 * quad + 4, :].bitcast(I32),
-                    )
+                nc.sync.dma_start(
+                    stacked[32 * quad : 32 * quad + 4 * count, b, :].bitcast(I32),
+                    w2_scales[b::2, 0, 4 * quad : 4 * quad + 4, :].bitcast(I32),
+                )
 
         def reorder_s2():
             nc.vector.tensor_copy(
@@ -176,13 +178,13 @@ def tile_moe_bdx_glu_sigmoid_kernel(
                 )
 
         def round_g(k):
-            g_bf[k] = turns.tile([P, width(k), PACK], BF16, tag="swap%d" % (k % 2), name="g_bf", align_bytes=64)
+            g_bf[k] = turns.tile([P, width(k), PACK], BF16, tag="swap%d" % (k % RING), name="g_bf", align_bytes=64)
             nc.scalar.activation(words_by_runs(g_bf[k][:]), planes_by_runs(g_planes(k)), ACT.Copy)
 
         def sigmoids(k):
             dsig[k] = turns.tile([P, PACK, width(k)], F32, tag="turn%d" % (k % RING), name="dsig", align_bytes=64)
             nc.scalar.activation(s_planes(k), s_planes(k), ACT.Sigmoid)
-            square = turns.tile([P, PACK, width(k)], F32, tag="swap%d" % (k % 2), name="square", align_bytes=64)
+            square = turns.tile([P, PACK, width(k)], F32, tag="swap%d" % (k % RING), name="square", align_bytes=64)
             nc.scalar.activation(square[:], s_planes(k), ACT.Square, bias=minus_half[:])
             col = first[max(k - 2, 0)] * C
             nc.scalar.activation(dsig[k][:], square[:], ACT.Identity, bias=dx[:, col : col + 1], scale=-1.0)
@@ -247,7 +249,7 @@ def tile_moe_bdx_glu_sigmoid_kernel(
 
         def second_product(k):
             groups = width(k) // GROUP
-            da_mx[k] = turns.tile([P, 10 * WIDE], U8, tag="swap%d" % ((k + 1) % 2), name="da_mx", align_bytes=64)
+            da_mx[k] = turns.tile([P, 10 * WIDE], U8, tag="swap%d" % ((k + 1) % RING), name="da_mx", align_bytes=64)
             halves = [(0, groups // 2), (groups // 2, groups)]
             for j0, j1 in halves:
                 nc.vector.quantize_mx(
@@ -272,7 +274,6 @@ def tile_moe_bdx_glu_sigmoid_kernel(
                 base = first[k] * C
                 nc.scalar.copy(dx[:, base + j0 * GROUP : base + j1 * GROUP], dx_ps[:])
 
-        load_s13()
         load_dy(0)
         nc.sync.dma_start(offs_sb[:], offs)
         nc.sync.dma_start(u_home[1][:, WIDE : 2 * WIDE], gate[:P, :WIDE])
@@ -280,10 +281,13 @@ def tile_moe_bdx_glu_sigmoid_kernel(
         load_gate(3)
         load_dy(1)
         load_a1(0)
+        load_s2(0)
         load_dy(2)
-        load_s2()
+        load_s2(1)
         load_a1(1)
+        load_s2(2)
         load_dy(3)
+        load_s2(3)
         load_a3(0)
         load_w2(0)
         load_a3(1)
@@ -298,11 +302,12 @@ def tile_moe_bdx_glu_sigmoid_kernel(
                     gather(k, t)
         reorder_s2()
         load_gate(4)
-        load_w13()
         load_a3(2)
         load_a1(3)
         load_gate(5)
         load_w2(2)
+        load_w13(0, EARLY)
+        load_s13()
         unstack_s2(2)
         round_g(0)
         round_g(1)
@@ -337,17 +342,17 @@ def tile_moe_bdx_glu_sigmoid_kernel(
                 sigmoids(k + 3)
             if k + 3 <= last:
                 unstack_s2(k + 3)
+            if k == 1:
+                load_w13(EARLY, E)
             if k == 3:
                 for r, pos in enumerate((pos1, pos2, pos3)):
                     nc.sync.dma_start(pos_sb[r][:], pos)
 
-        chunks = list(zip(OUT_CUTS[:-1], OUT_CUTS[1:]))
-        for r in range(3):
-            for c0, c1 in chunks:
-                picked = dx[:].indirect(pos_sb[r][:, c0 // 16 : c1 // 16])
-                if r == 0:
-                    nc.vector.tensor_copy(s_home[0][:, c0:c1], picked)
-                else:
-                    nc.vector.tensor_tensor(s_home[r][:, c0:c1], picked, s_home[r - 1][:, c0:c1], ADD)
-                if r == 2:
-                    nc.sync.dma_start(out[:, c0:c1], s_home[r][:, c0:c1])
+        for c0, c1 in zip(OUT_CUTS[:-1], OUT_CUTS[1:]):
+            adder = nc.vector if c1 == T else nc.gpsimd
+            parts = [s_home[r][:, c0:c1] for r in range(3)]
+            for r in range(3):
+                nc.vector.tensor_copy(parts[r], dx[:].indirect(pos_sb[r][:, c0 // 16 : c1 // 16]))
+            adder.tensor_tensor(parts[0], parts[0], parts[1], ADD)
+            adder.tensor_tensor(parts[0], parts[0], parts[2], ADD)
+            nc.sync.dma_start(out[:, c0:c1], parts[0])

@@ -22,12 +22,13 @@ ACT = mybir.ActivationFunctionType
 MULT = mybir.AluOpType.mult
 ADD = mybir.AluOpType.add
 
-UNITS = [1, 1, 2, 2, 2, 2, 2, 2, 1]
+UNITS = [2, 2, 2, 2, 2, 2, 2, 1]
 AHEAD = 3
 RING = 3
 LONG_RING = 4
 WIDE = 2 * C
 SPAN = PACK * WIDE
+COVER = WIDE - GROUP
 OUT_CUTS = [0, 800, 1280]
 RUN = 4
 EARLY = 4
@@ -65,7 +66,7 @@ def tile_moe_bdx_glu_sigmoid_kernel(
         w13 = [keep.tile([P, E, 2 * K], U8, name="w13_%d" % m, align_bytes=64) for m in range(2)]
         s13 = [keep.tile([P, E, K], U8, name="s13_%d" % m, align_bytes=64) for m in range(2)]
         g_home = [keep.tile([P, SPAN], F32, name="g_home%d" % r, align_bytes=64) for r in range(LONG_RING)]
-        u_home = [keep.tile([P, GROUP + SPAN], F32, name="u_home%d" % r, align_bytes=64) for r in range(LONG_RING)]
+        u_home = [keep.tile([P, COVER + SPAN], F32, name="u_home%d" % r, align_bytes=64) for r in range(LONG_RING)]
         s_home = [keep.tile([P, SPAN], F32, name="s_home%d" % r) for r in range(LONG_RING)]
         minus_half = keep.tile([P, 1], F32, name="minus_half")
 
@@ -97,12 +98,10 @@ def tile_moe_bdx_glu_sigmoid_kernel(
         def u_planes(k):
             if k + 2 > last:
                 return as_planes(g_home[(k - 2) % LONG_RING][:, : PACK * width(k)])
-            return as_planes(u_home[k % LONG_RING][:, GROUP : GROUP + PACK * width(k)])
+            return as_planes(u_home[k % LONG_RING][:, COVER : COVER + PACK * width(k)])
 
         def gate_row(k):
-            if k < 2:
-                return u_home[1][:, WIDE + first[k] * C : WIDE + first[k] * C + width(k)]
-            return u_home[(k - 2) % LONG_RING][:, : width(k)]
+            return u_home[(k - 2) % LONG_RING][:, WIDE - width(k) : WIDE]
 
 
         def da_words(k):
@@ -124,7 +123,7 @@ def tile_moe_bdx_glu_sigmoid_kernel(
             nc.sync.dma_start(a3_sb[k][:], a3.rearrange("(p t) s -> p t s", t=PACK)[:, :, slots(k)])
 
         def load_w2(k):
-            w2_raw[k] = ring3.tile([P, UNITS[k], 2 * H], U8, name="w2_raw", align_bytes=64)
+            w2_raw[k] = turns.tile([P, UNITS[k], 2 * H], U8, tag="raw%d" % (k % RING), name="w2_raw", align_bytes=64)
             nc.sync.dma_start(
                 w2_raw[k][:].bitcast(I32),
                 w2_words[first[k] : first[k] + UNITS[k], 0, :, :].rearrange("e p b -> p e b").bitcast(I32),
@@ -167,7 +166,7 @@ def tile_moe_bdx_glu_sigmoid_kernel(
                 )
 
         def gather(k, t):
-            pieces = [(GROUP, width(k)), (0, GROUP)] if t == PACK - 1 and k >= AHEAD else [(0, width(k))]
+            pieces = [(width(k) - GROUP, width(k)), (0, width(k) - GROUP)] if t == PACK - 1 and k >= AHEAD else [(0, width(k))]
             for c0, c1 in pieces:
                 base = first[k] * C
                 nc.vector.tensor_tensor(
@@ -178,7 +177,10 @@ def tile_moe_bdx_glu_sigmoid_kernel(
                 )
 
         def round_g(k):
-            g_bf[k] = turns.tile([P, width(k), PACK], BF16, tag="swap%d" % (k % RING), name="g_bf", align_bytes=64)
+            if k == 0:
+                g_bf[k] = g_home[AHEAD][:, SPAN // 2 :].bitcast(BF16).rearrange("p (c t) -> p c t", t=PACK)
+            else:
+                g_bf[k] = turns.tile([P, width(k), PACK], BF16, tag="swap%d" % (k % RING), name="g_bf", align_bytes=64)
             nc.scalar.activation(words_by_runs(g_bf[k][:]), planes_by_runs(g_planes(k)), ACT.Copy)
 
         def sigmoids(k):
@@ -186,15 +188,11 @@ def tile_moe_bdx_glu_sigmoid_kernel(
             nc.scalar.activation(s_planes(k), s_planes(k), ACT.Sigmoid)
             square = turns.tile([P, PACK, width(k)], F32, tag="swap%d" % (k % RING), name="square", align_bytes=64)
             nc.scalar.activation(square[:], s_planes(k), ACT.Square, bias=minus_half[:])
-            col = first[max(k - 2, 0)] * C
+            col = first[max(k - 3, 0)] * C
             nc.scalar.activation(dsig[k][:], square[:], ACT.Identity, bias=dx[:, col : col + 1], scale=-1.0)
 
-        def gpsimd_planes(k):
-            return 0 if k == 0 else PACK * min(width(k - 1), width(k)) // width(k)
-
         def factor_u(engine, k, t0, t1):
-            if t1 > t0:
-                engine.tensor_tensor(u_planes(k)[:, t0:t1, :], dsig[k][:, t0:t1, :], a3_sb[k][:, t0:t1, :], MULT)
+            engine.tensor_tensor(u_planes(k)[:, t0:t1, :], dsig[k][:, t0:t1, :], a3_sb[k][:, t0:t1, :], MULT)
 
         def w2_view(k):
             return mx[k][:, : UNITS[k] * 2 * H].rearrange("p (e b) -> p e b", b=2 * H)
@@ -207,12 +205,12 @@ def tile_moe_bdx_glu_sigmoid_kernel(
 
         def first_product(k):
             mx[k] = turns.tile([P, 4 * H + 5 * WIDE], U8, tag="turn%d" % (k % RING), name="mx", align_bytes=64)
-            nc.vector.quantize_mx(
-                out=g_codes(k).bitcast(FP8X4), scales=g_scales(k), in_=g_bf[k][:].rearrange("p c t -> p (c t)")
-            )
             nc.vector.tensor_copy(
                 w2_view(k).bitcast(U16).rearrange("p e (t m) -> p e t m", t=PACK),
                 w2_raw[k][:].bitcast(U16).rearrange("p e (m t) -> p e t m", t=PACK),
+            )
+            nc.vector.quantize_mx(
+                out=g_codes(k).bitcast(FP8X4), scales=g_scales(k), in_=g_bf[k][:].rearrange("p c t -> p (c t)")
             )
             for j in range(width(k) // GROUP):
                 e = j * GROUP // C
@@ -223,7 +221,7 @@ def tile_moe_bdx_glu_sigmoid_kernel(
                     nc.tensor.matmul_mx(
                         out=dh[k, j][:, t, :],
                         lhsT=w2_view(k)[:, e, 2 * P * t : 2 * P * (t + 1)].bitcast(FP4X4),
-                        lhsT_scale=s2[0 if expert < 2 else 1 + k % 2][:, expert % 2, P * t : P * (t + 1)],
+                        lhsT_scale=s2[0 if k == 0 else 1 + k % 2][:, expert % 2, P * t : P * (t + 1)],
                         rhs=g_codes(k)[:, cols].bitcast(FP8X4),
                         rhs_scale=g_scales(k)[:, cols],
                         start=True,
@@ -241,23 +239,24 @@ def tile_moe_bdx_glu_sigmoid_kernel(
                         MULT,
                     )
 
-        def da_codes(k):
-            return da_mx[k][:, : 8 * width(k)].bitcast(U32).rearrange("p (j m c) -> p j m c", m=2, c=GROUP)
+        def da_codes(k, half):
+            return da_mx[k, half][:, : 4 * width(k)].bitcast(U32).rearrange("p (j m c) -> p j m c", m=2, c=GROUP)
 
-        def da_scales(k):
-            return da_mx[k][:, 8 * WIDE : 8 * WIDE + 2 * width(k)].rearrange("p (j m c) -> p j m c", m=2, c=GROUP)
+        def da_scales(k, half):
+            return da_mx[k, half][:, 4 * WIDE : 4 * WIDE + width(k)].rearrange("p (j m c) -> p j m c", m=2, c=GROUP)
 
         def second_product(k):
-            groups = width(k) // GROUP
-            da_mx[k] = turns.tile([P, 10 * WIDE], U8, tag="swap%d" % ((k + 1) % RING), name="da_mx", align_bytes=64)
-            halves = [(0, groups // 2), (groups // 2, groups)]
-            for j0, j1 in halves:
-                nc.vector.quantize_mx(
-                    out=da_codes(k)[:, j0:j1, :, :].rearrange("p j m c -> p (j m c)").bitcast(FP8X4),
-                    scales=da_scales(k)[:, j0:j1, :, :].rearrange("p j m c -> p (j m c)"),
-                    in_=da_words(k)[:, j0:j1, :, :, :].rearrange("p j m c t -> p (j m c t)"),
+            count = width(k) // GROUP // 2
+            for half, slot in enumerate(("raw", "swap")):
+                da_mx[k, half] = turns.tile(
+                    [P, 5 * WIDE], U8, tag="%s%d" % (slot, (k + 1) % RING), name="da_mx", align_bytes=64
                 )
-            for j0, j1 in halves if k == last else [(0, groups)]:
+                nc.vector.quantize_mx(
+                    out=da_codes(k, half).rearrange("p j m c -> p (j m c)").bitcast(FP8X4),
+                    scales=da_scales(k, half).rearrange("p j m c -> p (j m c)"),
+                    in_=da_words(k)[:, half * count : (half + 1) * count, :, :, :].rearrange("p j m c t -> p (j m c t)"),
+                )
+            for j0, j1 in [(0, count), (count, 2 * count)] if k == last else [(0, 2 * count)]:
                 dx_ps = psum_dx.tile([P, (j1 - j0) * GROUP], F32, name="dx_ps")
                 for j in range(j0, j1):
                     e = first[k] + j * GROUP // C
@@ -266,8 +265,8 @@ def tile_moe_bdx_glu_sigmoid_kernel(
                             out=dx_ps[:, (j - j0) * GROUP : (j - j0 + 1) * GROUP],
                             lhsT=w13[m][:, e, :].bitcast(FP4X4),
                             lhsT_scale=s13[m][:, e, :],
-                            rhs=da_codes(k)[:, j, m, :].bitcast(FP8X4),
-                            rhs_scale=da_scales(k)[:, j, m, :],
+                            rhs=da_codes(k, j // count)[:, j % count, m, :].bitcast(FP8X4),
+                            rhs_scale=da_scales(k, j // count)[:, j % count, m, :],
                             start=(m == 0),
                             stop=(m == 1),
                         )
@@ -276,9 +275,8 @@ def tile_moe_bdx_glu_sigmoid_kernel(
 
         load_dy(0)
         nc.sync.dma_start(offs_sb[:], offs)
-        nc.sync.dma_start(u_home[1][:, WIDE : 2 * WIDE], gate[:P, :WIDE])
-        load_gate(2)
-        load_gate(3)
+        for k in range(AHEAD + 1):
+            load_gate(k)
         load_dy(1)
         load_a1(0)
         load_s2(0)
@@ -292,40 +290,46 @@ def tile_moe_bdx_glu_sigmoid_kernel(
         load_w2(0)
         load_a3(1)
         load_a1(2)
-        load_w2(1)
 
         sigmoids(0)
-        sigmoids(1)
         for t in range(PACK):
             for k in range(AHEAD + 1):
-                if (k, t) != (AHEAD, PACK - 1):
+                if k < AHEAD or t < PACK // 2:
                     gather(k, t)
         reorder_s2()
         load_gate(4)
+        load_w2(1)
+        unstack_s2(1)
+        load_w13(0, EARLY)
+        load_s13()
         load_a3(2)
         load_a1(3)
         load_gate(5)
         load_w2(2)
-        load_w13(0, EARLY)
-        load_s13()
         unstack_s2(2)
         round_g(0)
+        sigmoids(1)
         round_g(1)
         factor_u(nc.vector, 0, 0, PACK)
         first_product(0)
+        load_w2(3)
         sigmoids(2)
-        gather(AHEAD, PACK - 1)
+        for t in range(PACK // 2, PACK):
+            gather(AHEAD, t)
 
         for k in range(len(UNITS)):
             if 0 < k and k + AHEAD <= last:
-                for t in range(PACK - 1):
+                for t in range(PACK):
                     gather(k + AHEAD, t)
-                factor_u(nc.vector, k + 1, gpsimd_planes(k + 1), PACK)
-                gather(k + AHEAD, PACK - 1)
-            if k < last:
-                factor_u(nc.gpsimd, k + 1, 0, gpsimd_planes(k + 1))
+            if k + 1 == last - 1:
+                factor_u(nc.gpsimd, k + 1, 0, PACK // 2)
+                factor_u(nc.gpsimd, k + 1, PACK // 2, PACK)
+            elif k < last:
+                factor_u(nc.gpsimd, k + 1, 0, PACK)
             if k + 2 <= last:
                 round_g(k + 2)
+            if k + 3 <= last:
+                sigmoids(k + 3)
             make_da(k)
             if k + 6 <= last:
                 load_gate(k + 6)
@@ -335,11 +339,9 @@ def tile_moe_bdx_glu_sigmoid_kernel(
                 load_a1(k + 4)
             if k < last:
                 first_product(k + 1)
-            if k + 3 <= last:
-                load_w2(k + 3)
             second_product(k)
-            if k + 3 <= last:
-                sigmoids(k + 3)
+            if k + 4 <= last:
+                load_w2(k + 4)
             if k + 3 <= last:
                 unstack_s2(k + 3)
             if k == 1:

@@ -54,8 +54,8 @@ def tile_moe_bdx_glu_sigmoid_kernel(
         turns = ctx.enter_context(tc.tile_pool(name="turns", bufs=1))
         ring2 = ctx.enter_context(tc.tile_pool(name="ring2", bufs=2))
         ring3 = ctx.enter_context(tc.tile_pool(name="ring3", bufs=3))
-        psum_dh = ctx.enter_context(tc.psum_pool(name="psum_dh", bufs=6))
-        psum_dx = ctx.enter_context(tc.psum_pool(name="psum_dx", bufs=2))
+        psum_dh = ctx.enter_context(tc.psum_pool(name="psum_dh", bufs=4))
+        psum_dx = ctx.enter_context(tc.psum_pool(name="psum_dx", bufs=4))
 
         offs_sb = keep.tile([P, S // 16], U16, name="offs_sb")
         pos_sb = [keep.tile([P, T // 16], U16, name="pos_sb%d" % r) for r in range(3)]
@@ -335,6 +335,8 @@ def tile_moe_bdx_glu_sigmoid_kernel(
                 load_gate(k + 6)
             if k + 3 <= last:
                 load_a3(k + 3)
+            if k == 0:
+                load_w13(EARLY, E)
             if k + 4 <= last:
                 load_a1(k + 4)
             if k < last:
@@ -344,8 +346,6 @@ def tile_moe_bdx_glu_sigmoid_kernel(
                 load_w2(k + 4)
             if k + 3 <= last:
                 unstack_s2(k + 3)
-            if k == 1:
-                load_w13(EARLY, E)
             if k == 3:
                 for r, pos in enumerate((pos1, pos2, pos3)):
                     nc.sync.dma_start(pos_sb[r][:], pos)

@@ -29,7 +29,7 @@ LONG_RING = 4
 WIDE = 2 * C
 SPAN = PACK * WIDE
 COVER = WIDE - GROUP
-OUT_CUTS = [0, 800, 1280]
+OUT_CUTS = [0, 768, 1280]
 RUN = 4
 EARLY = 4
 
@@ -239,23 +239,28 @@ def tile_moe_bdx_glu_sigmoid_kernel(
                         MULT,
                     )
 
+        def gathers_follow(k):
+            return k + 1 + AHEAD <= last
+
         def da_codes(k, half):
             return da_mx[k, half][:, : 4 * width(k)].bitcast(U32).rearrange("p (j m c) -> p j m c", m=2, c=GROUP)
 
         def da_scales(k, half):
             return da_mx[k, half][:, 4 * WIDE : 4 * WIDE + width(k)].rearrange("p (j m c) -> p j m c", m=2, c=GROUP)
 
-        def second_product(k):
+        def quantize_da(k):
             count = width(k) // GROUP // 2
             for half, slot in enumerate(("raw", "swap")):
-                da_mx[k, half] = turns.tile(
-                    [P, 5 * WIDE], U8, tag="%s%d" % (slot, (k + 1) % RING), name="da_mx", align_bytes=64
-                )
+                tag = "codes%d" % half if gathers_follow(k) else "%s%d" % (slot, (k + 1) % RING)
+                da_mx[k, half] = turns.tile([P, 5 * WIDE], U8, tag=tag, name="da_mx", align_bytes=64)
                 nc.vector.quantize_mx(
                     out=da_codes(k, half).rearrange("p j m c -> p (j m c)").bitcast(FP8X4),
                     scales=da_scales(k, half).rearrange("p j m c -> p (j m c)"),
                     in_=da_words(k)[:, half * count : (half + 1) * count, :, :, :].rearrange("p j m c t -> p (j m c t)"),
                 )
+
+        def second_product(k):
+            count = width(k) // GROUP // 2
             for j0, j1 in [(0, count), (count, 2 * count)] if k == last else [(0, 2 * count)]:
                 dx_ps = psum_dx.tile([P, (j1 - j0) * GROUP], F32, name="dx_ps")
                 for j in range(j0, j1):
@@ -339,8 +344,12 @@ def tile_moe_bdx_glu_sigmoid_kernel(
                 load_w13(EARLY, E)
             if k + 4 <= last:
                 load_a1(k + 4)
+            if gathers_follow(k):
+                quantize_da(k)
             if k < last:
                 first_product(k + 1)
+            if not gathers_follow(k):
+                quantize_da(k)
             second_product(k)
             if k + 4 <= last:
                 load_w2(k + 4)
@@ -350,11 +359,13 @@ def tile_moe_bdx_glu_sigmoid_kernel(
                 for r, pos in enumerate((pos1, pos2, pos3)):
                     nc.sync.dma_start(pos_sb[r][:], pos)
 
-        for c0, c1 in zip(OUT_CUTS[:-1], OUT_CUTS[1:]):
-            adder = nc.vector if c1 == T else nc.gpsimd
-            parts = [s_home[r][:, c0:c1] for r in range(3)]
-            for r in range(3):
-                nc.vector.tensor_copy(parts[r], dx[:].indirect(pos_sb[r][:, c0 // 16 : c1 // 16]))
-            adder.tensor_tensor(parts[0], parts[0], parts[1], ADD)
-            adder.tensor_tensor(parts[0], parts[0], parts[2], ADD)
-            nc.sync.dma_start(out[:, c0:c1], parts[0])
+        chunks = list(zip(OUT_CUTS[:-1], OUT_CUTS[1:]))
+        for r in range(3):
+            for c0, c1 in chunks:
+                picked = dx[:].indirect(pos_sb[r][:, c0 // 16 : c1 // 16])
+                if r == 0:
+                    nc.vector.tensor_copy(s_home[0][:, c0:c1], picked)
+                else:
+                    nc.vector.tensor_tensor(s_home[r][:, c0:c1], picked, s_home[r - 1][:, c0:c1], ADD)
+                if r == 2:
+                    nc.sync.dma_start(out[:, c0:c1], s_home[r][:, c0:c1])

@@ -25,11 +25,14 @@ ADD = mybir.AluOpType.add
 UNITS = [2, 2, 2, 2, 2, 2, 2, 1]
 AHEAD = 3
 RING = 3
+HALVED = len(UNITS) - 2
 LONG_RING = 4
 WIDE = 2 * C
 SPAN = PACK * WIDE
 COVER = WIDE - GROUP
-OUT_CUTS = [0, 768, 1280]
+OUT_CUTS = [0, 640, 1280]
+LAST_CUTS = [0, 640, 1088, 1280]
+ROUNDS = {0: (2,), 1: (3,), 2: (4,), 3: (5,), 4: (6,), 6: (7,)}
 RUN = 4
 EARLY = 4
 
@@ -78,7 +81,7 @@ def tile_moe_bdx_glu_sigmoid_kernel(
         for plane in s2[1:]:
             nc.gpsimd.memset(plane[:].bitcast(I32), 0)
 
-        a3_sb, dsig, w2_raw, mx, dh, da_mx, g_bf = {}, {}, {}, {}, {}, {}, {}
+        a3_sb, dsig, w2_raw, mx, dh, da_mx, g_bf, g_pairs = {}, {}, {}, {}, {}, {}, {}, {}
 
         def width(k):
             return UNITS[k] * C
@@ -95,14 +98,24 @@ def tile_moe_bdx_glu_sigmoid_kernel(
         def g_planes(k):
             return as_planes(g_home[k % LONG_RING][:, : PACK * width(k)])
 
+        def g_pair(k, pair):
+            if (k, pair) in g_pairs:
+                return g_pairs[k, pair][:]
+            return g_planes(k)[:, 2 * pair : 2 * pair + 2, :]
+
         def u_planes(k):
-            if k + 2 > last:
-                return as_planes(g_home[(k - 2) % LONG_RING][:, : PACK * width(k)])
             return as_planes(u_home[k % LONG_RING][:, COVER : COVER + PACK * width(k)])
 
-        def gate_row(k):
-            return u_home[(k - 2) % LONG_RING][:, WIDE - width(k) : WIDE]
+        def gathers_of(step):
+            if step + AHEAD < HALVED:
+                return step + AHEAD, range(PACK)
+            turn = step + AHEAD - HALVED
+            return HALVED + turn // 2, range(turn % 2 * PACK // 2, (turn % 2 + 1) * PACK // 2)
 
+        def gate_row(step):
+            count = width(gathers_of(step)[0])
+            start = COVER - count * 3 // 4
+            return u_home[(step + 1) % LONG_RING][:, start : start + count]
 
         def da_words(k):
             return g_home[k % LONG_RING][:, : PACK * width(k)].bitcast(BF16).rearrange(
@@ -112,8 +125,8 @@ def tile_moe_bdx_glu_sigmoid_kernel(
         def load_dy(t):
             nc.sync.dma_start(dy[t][:], dyT.rearrange("(p t) c -> p t c", t=PACK)[:, t, :])
 
-        def load_gate(k):
-            nc.sync.dma_start(gate_row(k), gate[:P, slots(k)])
+        def load_gate(step):
+            nc.sync.dma_start(gate_row(step), gate[:P, slots(gathers_of(step)[0])])
 
         def load_a1(k):
             nc.sync.dma_start(s_planes(k), a1.rearrange("(p t) s -> p t s", t=PACK)[:, :, slots(k)])
@@ -123,7 +136,7 @@ def tile_moe_bdx_glu_sigmoid_kernel(
             nc.sync.dma_start(a3_sb[k][:], a3.rearrange("(p t) s -> p t s", t=PACK)[:, :, slots(k)])
 
         def load_w2(k):
-            w2_raw[k] = turns.tile([P, UNITS[k], 2 * H], U8, tag="raw%d" % (k % RING), name="w2_raw", align_bytes=64)
+            w2_raw[k] = ring3.tile([P, UNITS[k], 2 * H], U8, name="w2_raw", align_bytes=64)
             nc.sync.dma_start(
                 w2_raw[k][:].bitcast(I32),
                 w2_words[first[k] : first[k] + UNITS[k], 0, :, :].rearrange("e p b -> p e b").bitcast(I32),
@@ -165,23 +178,41 @@ def tile_moe_bdx_glu_sigmoid_kernel(
                     s2[0][32 * quad + 4 * a : 32 * quad + 4 * a + 4, : UNITS[k], :].bitcast(I32),
                 )
 
-        def gather(k, t):
-            pieces = [(width(k) - GROUP, width(k)), (0, width(k) - GROUP)] if t == PACK - 1 and k >= AHEAD else [(0, width(k))]
-            for c0, c1 in pieces:
-                base = first[k] * C
-                nc.vector.tensor_tensor(
-                    g_planes(k)[:, t, c0:c1],
-                    dy[t][:].indirect(offs_sb[:, (base + c0) // 16 : (base + c1) // 16]),
-                    gate_row(k)[:, c0:c1],
-                    MULT,
+        def gather(step, t, c0, c1):
+            k = gathers_of(step)[0]
+            base = first[k] * C
+            nc.vector.tensor_tensor(
+                g_pair(k, t // 2)[:, t % 2, c0:c1],
+                dy[t][:].indirect(offs_sb[:, (base + c0) // 16 : (base + c1) // 16]),
+                gate_row(step)[:, c0:c1],
+                MULT,
+            )
+
+        def gather_step(step, planes):
+            k = gathers_of(step)[0]
+            cut = width(k) * 3 // 4
+            split = planes[-(WIDE // width(k)) :]
+            if step > AHEAD:
+                g_pairs[k, planes[0] // 2] = turns.tile(
+                    [P, 2, width(k)], F32, tag="swap%d" % (step % RING), name="g_pair", align_bytes=64
                 )
+            for t in planes:
+                gather(step, t, cut if t in split else 0, width(k))
+            for t in split:
+                gather(step, t, 0, cut)
 
         def round_g(k):
             if k == 0:
                 g_bf[k] = g_home[AHEAD][:, SPAN // 2 :].bitcast(BF16).rearrange("p (c t) -> p c t", t=PACK)
             else:
                 g_bf[k] = turns.tile([P, width(k), PACK], BF16, tag="swap%d" % (k % RING), name="g_bf", align_bytes=64)
-            nc.scalar.activation(words_by_runs(g_bf[k][:]), planes_by_runs(g_planes(k)), ACT.Copy)
+            if k < HALVED:
+                nc.scalar.activation(words_by_runs(g_bf[k][:]), planes_by_runs(g_planes(k)), ACT.Copy)
+            else:
+                for pair in range(2):
+                    nc.scalar.activation(
+                        words_by_runs(g_bf[k][:, :, 2 * pair : 2 * pair + 2]), planes_by_runs(g_pair(k, pair)), ACT.Copy
+                    )
 
         def sigmoids(k):
             dsig[k] = turns.tile([P, PACK, width(k)], F32, tag="turn%d" % (k % RING), name="dsig", align_bytes=64)
@@ -239,9 +270,6 @@ def tile_moe_bdx_glu_sigmoid_kernel(
                         MULT,
                     )
 
-        def gathers_follow(k):
-            return k + 1 + AHEAD <= last
-
         def da_codes(k, half):
             return da_mx[k, half][:, : 4 * width(k)].bitcast(U32).rearrange("p (j m c) -> p j m c", m=2, c=GROUP)
 
@@ -250,9 +278,8 @@ def tile_moe_bdx_glu_sigmoid_kernel(
 
         def quantize_da(k):
             count = width(k) // GROUP // 2
-            for half, slot in enumerate(("raw", "swap")):
-                tag = "codes%d" % half if gathers_follow(k) else "%s%d" % (slot, (k + 1) % RING)
-                da_mx[k, half] = turns.tile([P, 5 * WIDE], U8, tag=tag, name="da_mx", align_bytes=64)
+            for half in range(2):
+                da_mx[k, half] = turns.tile([P, 5 * WIDE], U8, tag="codes%d" % half, name="da_mx", align_bytes=64)
                 nc.vector.quantize_mx(
                     out=da_codes(k, half).rearrange("p j m c -> p (j m c)").bitcast(FP8X4),
                     scales=da_scales(k, half).rearrange("p j m c -> p (j m c)"),
@@ -280,8 +307,10 @@ def tile_moe_bdx_glu_sigmoid_kernel(
 
         load_dy(0)
         nc.sync.dma_start(offs_sb[:], offs)
-        for k in range(AHEAD + 1):
-            load_gate(k)
+        for c0 in (0, C):
+            nc.sync.dma_start(gate_row(-AHEAD)[:, c0 : c0 + C], gate[:P, c0 : c0 + C])
+        for step in range(1 - AHEAD, 1):
+            load_gate(step)
         load_dy(1)
         load_a1(0)
         load_s2(0)
@@ -298,18 +327,21 @@ def tile_moe_bdx_glu_sigmoid_kernel(
 
         sigmoids(0)
         for t in range(PACK):
-            for k in range(AHEAD + 1):
-                if k < AHEAD or t < PACK // 2:
-                    gather(k, t)
+            for step in range(-AHEAD, 1):
+                if (step, t) == (-AHEAD, 0):
+                    gather(step, t, 0, C)
+                    gather(step, t, C, WIDE)
+                elif step < 0 or t < PACK // 2:
+                    gather(step, t, 0, WIDE)
         reorder_s2()
-        load_gate(4)
+        load_gate(1)
         load_w2(1)
         unstack_s2(1)
         load_w13(0, EARLY)
         load_s13()
         load_a3(2)
         load_a1(3)
-        load_gate(5)
+        load_gate(2)
         load_w2(2)
         unstack_s2(2)
         round_g(0)
@@ -319,37 +351,31 @@ def tile_moe_bdx_glu_sigmoid_kernel(
         first_product(0)
         load_w2(3)
         sigmoids(2)
-        for t in range(PACK // 2, PACK):
-            gather(AHEAD, t)
+        gather_step(0, range(PACK // 2, PACK))
 
         for k in range(len(UNITS)):
-            if 0 < k and k + AHEAD <= last:
-                for t in range(PACK):
-                    gather(k + AHEAD, t)
-            if k + 1 == last - 1:
-                factor_u(nc.gpsimd, k + 1, 0, PACK // 2)
-                factor_u(nc.gpsimd, k + 1, PACK // 2, PACK)
-            elif k < last:
+            if 0 < k < last:
+                gather_step(k, gathers_of(k)[1])
+            if k < last:
                 factor_u(nc.gpsimd, k + 1, 0, PACK)
-            if k + 2 <= last:
-                round_g(k + 2)
+            for unit in ROUNDS.get(k, ()):
+                round_g(unit)
             if k + 3 <= last:
                 sigmoids(k + 3)
             make_da(k)
-            if k + 6 <= last:
-                load_gate(k + 6)
+            if k + 3 < last:
+                load_gate(k + 3)
             if k + 3 <= last:
                 load_a3(k + 3)
             if k == 0:
                 load_w13(EARLY, E)
             if k + 4 <= last:
                 load_a1(k + 4)
-            if gathers_follow(k):
-                quantize_da(k)
-            if k < last:
+            if k + 1 == last:
+                first_product(last)
+            quantize_da(k)
+            if k + 1 < last:
                 first_product(k + 1)
-            if not gathers_follow(k):
-                quantize_da(k)
             second_product(k)
             if k + 4 <= last:
                 load_w2(k + 4)
@@ -359,9 +385,9 @@ def tile_moe_bdx_glu_sigmoid_kernel(
                 for r, pos in enumerate((pos1, pos2, pos3)):
                     nc.sync.dma_start(pos_sb[r][:], pos)
 
-        chunks = list(zip(OUT_CUTS[:-1], OUT_CUTS[1:]))
         for r in range(3):
-            for c0, c1 in chunks:
+            cuts = LAST_CUTS if r == 2 else OUT_CUTS
+            for c0, c1 in zip(cuts[:-1], cuts[1:]):
                 picked = dx[:].indirect(pos_sb[r][:, c0 // 16 : c1 // 16])
                 if r == 0:
                     nc.vector.tensor_copy(s_home[0][:, c0:c1], picked)

@@ -235,7 +235,8 @@ def tile_moe_bdx_glu_sigmoid_kernel(
             return mx[k][:, 4 * H + 4 * WIDE : 4 * H + 4 * WIDE + width(k)]
 
         def first_product(k):
-            mx[k] = turns.tile([P, 4 * H + 5 * WIDE], U8, tag="turn%d" % (k % RING), name="mx", align_bytes=64)
+            slot = "swap0" if k == 0 else "turn%d" % (k % RING)
+            mx[k] = turns.tile([P, 4 * H + 5 * WIDE], U8, tag=slot, name="mx", align_bytes=64)
             nc.vector.tensor_copy(
                 w2_view(k).bitcast(U16).rearrange("p e (t m) -> p e t m", t=PACK),
                 w2_raw[k][:].bitcast(U16).rearrange("p e (m t) -> p e t m", t=PACK),
@@ -303,7 +304,10 @@ def tile_moe_bdx_glu_sigmoid_kernel(
                             stop=(m == 1),
                         )
                 base = first[k] * C
-                nc.scalar.copy(dx[:, base + j0 * GROUP : base + j1 * GROUP], dx_ps[:])
+                if base + j1 * GROUP == S:
+                    nc.vector.tensor_copy(dx[:, base + j0 * GROUP :], dx_ps[:])
+                else:
+                    nc.scalar.copy(dx[:, base + j0 * GROUP : base + j1 * GROUP], dx_ps[:])
 
         load_dy(0)
         nc.sync.dma_start(offs_sb[:], offs)

@@ -34,6 +34,7 @@ OUT_CUTS = [0, 640, 1280]
 LAST_CUTS = [0, 640, 1088, 1280]
 ROUNDS = {0: (2,), 1: (3,), 2: (4,), 3: (5,), 4: (6,), 6: (7,)}
 RUN = 4
+LINE = 8
 EARLY = 4
 
 
@@ -238,8 +239,8 @@ def tile_moe_bdx_glu_sigmoid_kernel(
             slot = "swap0" if k == 0 else "turn%d" % (k % RING)
             mx[k] = turns.tile([P, 4 * H + 5 * WIDE], U8, tag=slot, name="mx", align_bytes=64)
             nc.vector.tensor_copy(
-                w2_view(k).bitcast(U16).rearrange("p e (t m) -> p e t m", t=PACK),
-                w2_raw[k][:].bitcast(U16).rearrange("p e (m t) -> p e t m", t=PACK),
+                w2_view(k).bitcast(U16).rearrange("p e (t c i) -> p e c t i", t=PACK, i=LINE),
+                w2_raw[k][:].bitcast(U16).rearrange("p e (c i t) -> p e c t i", t=PACK, i=LINE),
             )
             nc.vector.quantize_mx(
                 out=g_codes(k).bitcast(FP8X4), scales=g_scales(k), in_=g_bf[k][:].rearrange("p c t -> p (c t)")

@@ -1,6 +1,7 @@
 from contextlib import ExitStack
 
 import concourse.mybir as mybir
+from concourse.masks import make_identity
 
 K, T, E, C, H, N = 128, 1280, 15, 256, 512, 512
 S = E * C
@@ -21,21 +22,22 @@ FP4X4 = mybir.dt.float4_e2m1fn_x4
 ACT = mybir.ActivationFunctionType
 MULT = mybir.AluOpType.mult
 ADD = mybir.AluOpType.add
+SUB = mybir.AluOpType.subtract
 
 UNITS = [2, 2, 2, 2, 2, 2, 2, 1]
+SHARED = [1, 2, 2, 2, 1, 0, 0, 0]
 AHEAD = 3
-RING = 3
-HALVED = len(UNITS) - 2
-LONG_RING = 4
+RING = 4
+HOMES = 5
 WIDE = 2 * C
 SPAN = PACK * WIDE
-COVER = WIDE - GROUP
+BLOCK = PACK * GROUP
 OUT_CUTS = [0, 640, 1280]
 LAST_CUTS = [0, 640, 1088, 1280]
-ROUNDS = {0: (2,), 1: (3,), 2: (4,), 3: (5,), 4: (6,), 6: (7,)}
 RUN = 4
 LINE = 8
 EARLY = 4
+LIVE = 100
 
 
 def planes_by_runs(ap):
@@ -46,119 +48,141 @@ def words_by_runs(ap):
     return ap.rearrange("p (c i) t -> p c t i", i=RUN)
 
 
+def as_planes(ap):
+    return ap.rearrange("p (t s) -> p t s", t=PACK)
+
+
+def as_words(ap):
+    return ap.rearrange("p (s t) -> p s t", t=PACK)
+
+
 def tile_moe_bdx_glu_sigmoid_kernel(
     tc, dyT, a1, a3, w2_words, w2_scales, w1_words, w1_scales, w3_words, w3_scales, gate, offs, pos1, pos2, pos3, out
 ):
     nc = tc.nc
     first = [sum(UNITS[:k]) for k in range(len(UNITS))]
     last = len(UNITS) - 1
+    skipped = UNITS[0] * C // GROUP
+    turned = S // GROUP - skipped
 
     with ExitStack() as ctx:
         keep = ctx.enter_context(tc.tile_pool(name="keep", bufs=1))
         turns = ctx.enter_context(tc.tile_pool(name="turns", bufs=1))
-        ring2 = ctx.enter_context(tc.tile_pool(name="ring2", bufs=2))
         ring3 = ctx.enter_context(tc.tile_pool(name="ring3", bufs=3))
+        ring4 = ctx.enter_context(tc.tile_pool(name="ring4", bufs=4))
         psum_dh = ctx.enter_context(tc.psum_pool(name="psum_dh", bufs=4))
-        psum_dx = ctx.enter_context(tc.psum_pool(name="psum_dx", bufs=4))
+        psum_turn = ctx.enter_context(tc.psum_pool(name="psum_turn", bufs=1))
+        psum_back = ctx.enter_context(tc.psum_pool(name="psum_back", bufs=2))
 
         offs_sb = keep.tile([P, S // 16], U16, name="offs_sb")
         pos_sb = [keep.tile([P, T // 16], U16, name="pos_sb%d" % r) for r in range(3)]
         dy = [keep.tile([P, T], F32, name="dy%d" % t) for t in range(PACK)]
         dx = keep.tile([P, S], F32, name="dx")
         stacked = keep.tile([P, 2, H], U8, name="stacked", align_bytes=64)
-        s2 = [keep.tile([P, 2, H], U8, name="s2_%d" % a, align_bytes=64) for a in range(3)]
+        s2_all = keep.tile([P, E * H], U8, name="s2_all", align_bytes=64)
+        s2_first = keep.tile([P, 2, H], U8, name="s2_first", align_bytes=64)
         w13 = [keep.tile([P, E, 2 * K], U8, name="w13_%d" % m, align_bytes=64) for m in range(2)]
         s13 = [keep.tile([P, E, K], U8, name="s13_%d" % m, align_bytes=64) for m in range(2)]
-        g_home = [keep.tile([P, SPAN], F32, name="g_home%d" % r, align_bytes=64) for r in range(LONG_RING)]
-        u_home = [keep.tile([P, COVER + SPAN], F32, name="u_home%d" % r, align_bytes=64) for r in range(LONG_RING)]
-        s_home = [keep.tile([P, SPAN], F32, name="s_home%d" % r) for r in range(LONG_RING)]
+        sm_home = [keep.tile([P, SPAN // 2], F32, name="sm_home%d" % r, align_bytes=64) for r in range(RING)]
+        home = [keep.tile([P, SPAN], F32, name="home%d" % r, align_bytes=64) for r in range(HOMES)]
+        head = dx[:, :SPAN]
+        da3_exact = keep.tile([P, 2 * BLOCK], F32, name="da3_exact", align_bytes=64)
+        ident = keep.tile([P, P], F32, name="ident")
+        gate_rows = keep.tile([P, GROUP], F32, name="gate_rows")
+        gate_cols = keep.tile([P, turned], F32, name="gate_cols")
         minus_half = keep.tile([P, 1], F32, name="minus_half")
+        quarter = keep.tile([P, 1], F32, name="quarter")
 
         nc.vector.memset(minus_half[:], -0.5)
-        nc.vector.memset(dx[:, 0:S:C], 0.25)
+        nc.vector.memset(quarter[:], 0.25)
+        nc.vector.memset(gate_rows[:], 0.0)
         nc.vector.memset(stacked[:, 1, :].bitcast(I32), 0)
+        nc.vector.memset(s2_all[96:, 2 * H :].bitcast(I32), 0)
         for plane in s13:
-            nc.gpsimd.memset(plane[:].bitcast(I32), 0)
-        for plane in s2[1:]:
-            nc.gpsimd.memset(plane[:].bitcast(I32), 0)
+            nc.vector.memset(plane[:].bitcast(I32), 0)
+        make_identity(nc, ident[:])
 
-        a3_sb, dsig, w2_raw, mx, dh, da_mx, g_bf, g_pairs = {}, {}, {}, {}, {}, {}, {}, {}
+        a1_sb, a3_sb, s_sb, w2_raw, dh, da_mx, g_pairs, turned_g = {}, {}, {}, {}, {}, {}, {}, {}
+        w2_sb, g_codes, g_scales, dx_ps = {}, {}, {}, {}
 
         def width(k):
             return UNITS[k] * C
 
+        def groups(k):
+            return width(k) // GROUP
+
         def slots(k):
             return slice(first[k] * C, (first[k] + UNITS[k]) * C)
 
-        def as_planes(ap):
-            return ap.rearrange("p (t s) -> p t s", t=PACK)
+        def cut(k):
+            return SHARED[k] * GROUP
 
-        def s_planes(k):
-            return as_planes(s_home[k % LONG_RING][:, : PACK * width(k)])
+        def sm_words(k):
+            return as_words(sm_home[k % RING][:, WIDE - 2 * cut(k) : WIDE + 2 * cut(k)])
 
-        def g_planes(k):
-            return as_planes(g_home[k % LONG_RING][:, : PACK * width(k)])
+        def y_flat(k):
+            return home[(k - 2) % HOMES][:, : PACK * cut(k)]
 
-        def g_pair(k, pair):
-            if (k, pair) in g_pairs:
-                return g_pairs[k, pair][:]
-            return g_planes(k)[:, 2 * pair : 2 * pair + 2, :]
-
-        def u_planes(k):
-            return as_planes(u_home[k % LONG_RING][:, COVER : COVER + PACK * width(k)])
-
-        def gathers_of(step):
-            if step + AHEAD < HALVED:
-                return step + AHEAD, range(PACK)
-            turn = step + AHEAD - HALVED
-            return HALVED + turn // 2, range(turn % 2 * PACK // 2, (turn % 2 + 1) * PACK // 2)
-
-        def gate_row(step):
-            count = width(gathers_of(step)[0])
-            start = COVER - count * 3 // 4
-            return u_home[(step + 1) % LONG_RING][:, start : start + count]
+        def u_group(k, j0, j1):
+            if k == 0:
+                if j0 >= 2:
+                    return as_planes(home[-2 % HOMES][:, SPAN // 2 :])[:, :, (j0 - 2) * GROUP : (j1 - 2) * GROUP]
+                return as_planes(home[-2 % HOMES][:, BLOCK : 2 * BLOCK])
+            planes = as_planes(home[(k - 2) % HOMES][:, PACK * cut(k) : PACK * width(k)])
+            return planes[:, :, j0 * GROUP - cut(k) : j1 * GROUP - cut(k)]
 
         def da_words(k):
-            return g_home[k % LONG_RING][:, : PACK * width(k)].bitcast(BF16).rearrange(
-                "p (j m c t) -> p j m c t", m=2, c=GROUP, t=PACK
-            )
+            return home[k % HOMES][:, : PACK * width(k)].bitcast(BF16).rearrange("p (j m b) -> p j m b", m=2, b=BLOCK)
+
+        def gathered(k, t):
+            if k == 0 or (k, t) == (2, 2):
+                return head[:, t * WIDE : (t + 1) * WIDE]
+            if k < AHEAD:
+                return home[k][:, t * WIDE : (t + 1) * WIDE]
+            if t < 2:
+                return sm_home[(k - AHEAD) % RING][:, WIDE + (t - 1) * width(k) : WIDE + t * width(k)]
+            return home[(k - AHEAD - 2) % HOMES][:, SPAN // 2 + (t - 2) * width(k) : SPAN // 2 + (t - 1) * width(k)]
+
+        gate_first = home[-2 % HOMES][:, SPAN // 2 : SPAN // 2 + WIDE]
 
         def load_dy(t):
             nc.sync.dma_start(dy[t][:], dyT.rearrange("(p t) c -> p t c", t=PACK)[:, t, :])
 
-        def load_gate(step):
-            nc.sync.dma_start(gate_row(step), gate[:P, slots(gathers_of(step)[0])])
-
         def load_a1(k):
-            nc.sync.dma_start(s_planes(k), a1.rearrange("(p t) s -> p t s", t=PACK)[:, :, slots(k)])
+            a1_sb[k] = turns.tile([P, PACK, width(k)], F32, tag="a1_%d" % (k % RING), name="a1_sb", align_bytes=64)
+            nc.sync.dma_start(a1_sb[k][:], a1.rearrange("(p t) s -> p t s", t=PACK)[:, :, slots(k)])
 
         def load_a3(k):
-            a3_sb[k] = ring3.tile([P, PACK, width(k)], F32, name="a3_sb")
+            a3_sb[k] = ring4.tile([P, PACK, width(k)], F32, name="a3_sb")
             nc.sync.dma_start(a3_sb[k][:], a3.rearrange("(p t) s -> p t s", t=PACK)[:, :, slots(k)])
 
-        def load_w2(k):
-            w2_raw[k] = ring3.tile([P, UNITS[k], 2 * H], U8, name="w2_raw", align_bytes=64)
+        def load_w2(k, count):
+            if k == 0:
+                w2_raw[k] = turns.tile([P, count, 2 * H], U8, tag="pairs1", name="w2_raw", align_bytes=64)
+            else:
+                w2_raw[k] = ring3.tile([P, count, 2 * H], U8, name="w2_raw", align_bytes=64)
             nc.sync.dma_start(
                 w2_raw[k][:].bitcast(I32),
-                w2_words[first[k] : first[k] + UNITS[k], 0, :, :].rearrange("e p b -> p e b").bitcast(I32),
+                w2_words[first[k] : first[k] + count, 0, :, :].rearrange("e p b -> p e b").bitcast(I32),
             )
 
         def load_w13(e0, e1):
-            for m, words in enumerate((w1_words, w3_words)):
+            for m, packed in enumerate((w1_words, w3_words)):
                 nc.sync.dma_start(
-                    w13[m][:, e0:e1, :].bitcast(I32), words[e0:e1, 0, :, :].rearrange("e p b -> p e b").bitcast(I32)
+                    w13[m][:, e0:e1, :].bitcast(I32), packed[e0:e1, 0, :, :].rearrange("e p b -> p e b").bitcast(I32)
                 )
 
         def load_s13():
             for plane, scales in zip(s13, (w1_scales, w3_scales)):
                 for quad in range(4):
-                    nc.sync.dma_start(
+                    nc.gpsimd.dma_start(
                         plane[32 * quad : 32 * quad + 4, :, :].bitcast(I32),
                         scales[:, 0, 4 * quad : 4 * quad + 4, :].rearrange("e f n -> f e n").bitcast(I32),
                     )
 
-        def load_s2(quad):
-            for b in range(2):
+        def load_s2(parts):
+            for part in parts:
+                quad, b = divmod(part, 2)
                 count = (E - b + 1) // 2
                 nc.sync.dma_start(
                     stacked[32 * quad : 32 * quad + 4 * count, b, :].bitcast(I32),
@@ -167,236 +191,359 @@ def tile_moe_bdx_glu_sigmoid_kernel(
 
         def reorder_s2():
             nc.vector.tensor_copy(
-                s2[0][:].rearrange("p b (t m) -> p b t m", t=PACK),
+                s2_first[:].rearrange("p b (t m) -> p b t m", t=PACK),
                 stacked[:].rearrange("p b (m t) -> p b t m", t=PACK),
             )
 
-        def unstack_s2(k):
-            a = first[k] // 2
-            for quad in range(4):
-                nc.sync.dma_start(
-                    s2[1 + k % 2][32 * quad : 32 * quad + 4, : UNITS[k], :].bitcast(I32),
-                    s2[0][32 * quad + 4 * a : 32 * quad + 4 * a + 4, : UNITS[k], :].bitcast(I32),
-                )
+        def s2_plane(k):
+            if k == 0:
+                return s2_first[:]
+            return s2_all[:, first[k] * H : (first[k] + UNITS[k]) * H].rearrange("p (e n) -> p e n", n=H)
 
-        def gather(step, t, c0, c1):
-            k = gathers_of(step)[0]
-            base = first[k] * C
-            nc.vector.tensor_tensor(
-                g_pair(k, t // 2)[:, t % 2, c0:c1],
-                dy[t][:].indirect(offs_sb[:, (base + c0) // 16 : (base + c1) // 16]),
-                gate_row(step)[:, c0:c1],
-                MULT,
+        def unstack_s2(k):
+            nc.sync.dma_start(
+                s2_plane(k)[:LIVE].bitcast(I32), s2_first[4 * k : 4 * k + LIVE, : UNITS[k], :].bitcast(I32)
             )
 
-        def gather_step(step, planes):
-            k = gathers_of(step)[0]
-            cut = width(k) * 3 // 4
-            split = planes[-(WIDE // width(k)) :]
-            if step > AHEAD:
-                g_pairs[k, planes[0] // 2] = turns.tile(
-                    [P, 2, width(k)], F32, tag="swap%d" % (step % RING), name="g_pair", align_bytes=64
-                )
-            for t in planes:
-                gather(step, t, cut if t in split else 0, width(k))
-            for t in split:
-                gather(step, t, 0, cut)
+        def turn_gate():
+            bank = psum_back.tile([P, PACK, GROUP], F32, tag="dx", name="turn")
+            nc.tensor.transpose(bank[:, 0, :], gate_rows[:], ident[:])
+            for k in range(1, len(UNITS)):
+                col = first[k] * C // GROUP - skipped
+                for j0, j1, sign in ((0, SHARED[k], -1.0), (SHARED[k], groups(k), 1.0)):
+                    if j1 > j0:
+                        nc.scalar.activation(
+                            gate_cols[:, col + j0 : col + j1], bank[:, 0, col + j0 : col + j1], ACT.Copy, scale=sign
+                        )
 
-        def round_g(k):
+        def gather(k, t):
+            picked = dy[t][:].indirect(offs_sb[:, first[k] * C // 16 : (first[k] * C + width(k)) // 16])
             if k == 0:
-                g_bf[k] = g_home[AHEAD][:, SPAN // 2 :].bitcast(BF16).rearrange("p (c t) -> p c t", t=PACK)
+                nc.vector.tensor_tensor(gathered(k, t), picked, gate_first, MULT)
             else:
-                g_bf[k] = turns.tile([P, width(k), PACK], BF16, tag="swap%d" % (k % RING), name="g_bf", align_bytes=64)
-            if k < HALVED:
-                nc.scalar.activation(words_by_runs(g_bf[k][:]), planes_by_runs(g_planes(k)), ACT.Copy)
-            else:
-                for pair in range(2):
-                    nc.scalar.activation(
-                        words_by_runs(g_bf[k][:, :, 2 * pair : 2 * pair + 2]), planes_by_runs(g_pair(k, pair)), ACT.Copy
+                nc.vector.tensor_copy(gathered(k, t), picked)
+
+        def round_first():
+            g_pairs[0] = home[-2 % HOMES][:, : SPAN // 2]
+            planes = as_planes(head[:, :SPAN])
+            rounded = as_words(g_pairs[0][:].bitcast(BF16))
+            for c0, c1, sign in ((0, cut(0), -1.0), (cut(0), WIDE, 1.0)):
+                nc.scalar.activation(
+                    words_by_runs(rounded[:, c0:c1, :]), planes_by_runs(planes[:, :, c0:c1]), ACT.Copy, scale=sign
+                )
+
+        def apply_gate(k, j):
+            bank = psum_turn.tile([P, PACK, GROUP], F32, tag="turn%d" % (j % 2), name="turn")
+            for t in range(PACK):
+                nc.tensor.transpose(bank[:, t, :], gathered(k, t)[:, j * GROUP : (j + 1) * GROUP], ident[:])
+            turned_g[k, j] = turns.tile([P, N], BF16, tag="turned%d" % j, name="turned_g", align_bytes=64)
+            col = first[k] * C // GROUP - skipped + j
+            nc.scalar.activation(
+                turned_g[k, j][:].rearrange("s (u p e) -> s u p e", u=2, e=2),
+                bank[:].rearrange("s (u e) p -> s u p e", e=2),
+                ACT.Copy,
+                scale=gate_cols[:, col : col + 1],
+            )
+
+        def turn_back(k, half):
+            if half == 0:
+                g_pairs[k] = turns.tile(
+                    [P, 2 * width(k)], F32, tag="pairs%d" % (k % 2), name="g_pairs", align_bytes=64
+                )
+            bank = psum_turn.tile([P, 2, 2, GROUP], F32, tag="turn%d" % half, name="back")
+            for jj in range(2):
+                for u in range(2):
+                    nc.tensor.transpose(
+                        bank[:, jj, u, :], turned_g[k, 2 * half + jj][:].bitcast(F32)[:, u * P : (u + 1) * P], ident[:]
                     )
+            nc.scalar.copy(
+                g_pairs[k][:, half * BLOCK : (half + 1) * BLOCK].rearrange("p (j s u) -> p j s u", j=2, u=2),
+                bank[:].rearrange("p j u s -> p j s u"),
+            )
 
-        def sigmoids(k):
-            dsig[k] = turns.tile([P, PACK, width(k)], F32, tag="turn%d" % (k % RING), name="dsig", align_bytes=64)
-            nc.scalar.activation(s_planes(k), s_planes(k), ACT.Sigmoid)
-            square = turns.tile([P, PACK, width(k)], F32, tag="swap%d" % (k % RING), name="square", align_bytes=64)
-            nc.scalar.activation(square[:], s_planes(k), ACT.Square, bias=minus_half[:])
-            col = first[max(k - 3, 0)] * C
-            nc.scalar.activation(dsig[k][:], square[:], ACT.Identity, bias=dx[:, col : col + 1], scale=-1.0)
+        def sigmoid_minus(k):
+            if cut(k):
+                nc.scalar.activation(
+                    words_by_runs(sm_words(k)), planes_by_runs(a1_sb[k][:, :, : cut(k)]), ACT.Sigmoid, scale=-1.0
+                )
 
-        def factor_u(engine, k, t0, t1):
-            engine.tensor_tensor(u_planes(k)[:, t0:t1, :], dsig[k][:, t0:t1, :], a3_sb[k][:, t0:t1, :], MULT)
+        def sigmoid_plus(k):
+            s_sb[k] = turns.tile([P, PACK, width(k) - cut(k)], F32, tag="s%d" % (k % HOMES), name="s", align_bytes=64)
+            nc.scalar.activation(s_sb[k][:], a1_sb[k][:, :, cut(k) :], ACT.Sigmoid)
 
-        def w2_view(k):
-            return mx[k][:, : UNITS[k] * 2 * H].rearrange("p (e b) -> p e b", b=2 * H)
+        def square(k):
+            nc.scalar.activation(a1_sb[k][:, :, cut(k) :], s_sb[k][:], ACT.Square, bias=minus_half[:])
 
-        def g_codes(k):
-            return mx[k][:, 4 * H : 4 * H + 4 * width(k)].bitcast(U32)
+        def derivative(k):
+            own = a1_sb[k][:, :, cut(k) :]
+            nc.scalar.activation(own, own, ACT.Identity, bias=quarter[:], scale=-1.0)
 
-        def g_scales(k):
-            return mx[k][:, 4 * H + 4 * WIDE : 4 * H + 4 * WIDE + width(k)]
+        def copy_dx(k):
+            if k >= 0:
+                nc.scalar.copy(dx[:, slots(k)], dx_ps[k, 0][:])
 
-        def first_product(k):
-            slot = "swap0" if k == 0 else "turn%d" % (k % RING)
-            mx[k] = turns.tile([P, 4 * H + 5 * WIDE], U8, tag=slot, name="mx", align_bytes=64)
+        def scalar_step(k):
+            if k != 4:
+                round_da3(k)
+            if k == 4:
+                round_da3(k)
+                sigmoid_plus(k + 2)
+            if k < last:
+                for j in range(2, groups(k + 1)):
+                    apply_gate(k + 1, j)
+            if k + 2 <= last:
+                sigmoid_minus(k + 2)
+            if k >= 4:
+                copy_dx(k - 2)
+            if k < last:
+                for half in range(groups(k + 1) // 2):
+                    turn_back(k + 1, half)
+            if k == 5:
+                sigmoid_plus(k + 2)
+            if k + 2 <= last:
+                square(k + 2)
+                if k != 4:
+                    apply_gate(k + 2, 0)
+                if k != 3:
+                    derivative(k + 2)
+                if k == 4:
+                    apply_gate(k + 2, 0)
+                apply_gate(k + 2, 1)
+            if k < 4:
+                copy_dx(k - 2)
+            if k < 3:
+                sigmoid_plus(k + 3)
+
+        def factor_y(k):
+            if cut(k):
+                nc.gpsimd.tensor_tensor(
+                    as_words(y_flat(k)), a3_sb[k][:, :, : cut(k)].rearrange("p t c -> p c t"), sm_words(k), MULT
+                )
+
+        def factor_u(k, j0, j1):
+            cols = slice(j0 * GROUP, j1 * GROUP)
+            nc.gpsimd.tensor_tensor(u_group(k, j0, j1), a1_sb[k][:, :, cols], a3_sb[k][:, :, cols], MULT)
+
+        def reorder_w2(k, target):
             nc.vector.tensor_copy(
-                w2_view(k).bitcast(U16).rearrange("p e (t c i) -> p e c t i", t=PACK, i=LINE),
+                target.bitcast(U16).rearrange("p (e t c i) -> p e c t i", t=PACK, i=LINE, c=P // LINE),
                 w2_raw[k][:].bitcast(U16).rearrange("p e (c i t) -> p e c t i", t=PACK, i=LINE),
             )
+
+        def quantize_g(k):
             nc.vector.quantize_mx(
-                out=g_codes(k).bitcast(FP8X4), scales=g_scales(k), in_=g_bf[k][:].rearrange("p c t -> p (c t)")
+                out=g_codes[k].bitcast(U32).bitcast(FP8X4), scales=g_scales[k], in_=g_pairs[k][:].bitcast(BF16)
             )
-            for j in range(width(k) // GROUP):
+
+        def first_product(k):
+            for j in sorted(range(groups(k)), key=lambda g: (g - SHARED[k]) % groups(k) if SHARED[k] == 2 else g):
                 e = j * GROUP // C
-                expert = first[k] + e
-                cols = slice(j * GROUP, (j + 1) * GROUP)
                 dh[k, j] = psum_dh.tile([P, PACK, GROUP], F32, name="dh")
                 for t in range(PACK):
+                    start = e * 2 * H + 2 * P * t
                     nc.tensor.matmul_mx(
                         out=dh[k, j][:, t, :],
-                        lhsT=w2_view(k)[:, e, 2 * P * t : 2 * P * (t + 1)].bitcast(FP4X4),
-                        lhsT_scale=s2[0 if k == 0 else 1 + k % 2][:, expert % 2, P * t : P * (t + 1)],
-                        rhs=g_codes(k)[:, cols].bitcast(FP8X4),
-                        rhs_scale=g_scales(k)[:, cols],
+                        lhsT=w2_sb[k][:, start : start + 2 * P].bitcast(FP4X4),
+                        lhsT_scale=s2_plane(k)[:, e, P * t : P * (t + 1)],
+                        rhs=g_codes[k][:, j * BLOCK : (j + 1) * BLOCK].bitcast(U32).bitcast(FP8X4),
+                        rhs_scale=g_scales[k][:, j * GROUP : (j + 1) * GROUP],
                         start=True,
                         stop=True,
                     )
 
+        def halves(k):
+            return (1, 0) if SHARED[k] else (0, 1)
+
+        def exact_da3(k, j):
+            nc.vector.scalar_tensor_tensor(
+                as_words(da3_exact[:, j * BLOCK : (j + 1) * BLOCK]),
+                sm_words(k)[:, j * GROUP : (j + 1) * GROUP, :],
+                1.0,
+                dh[k, j][:].rearrange("p t c -> p c t"),
+                SUB,
+                MULT,
+            )
+
+        def product(k, j, m):
+            c0 = j * GROUP - cut(k)
+            nc.vector.tensor_tensor(
+                words_by_runs(as_words(da_words(k)[:, j, m, :])),
+                planes_by_runs(dh[k, j][:]),
+                planes_by_runs(s_sb[k][:, :, c0 : c0 + GROUP] if m else u_group(k, j, j + 1)),
+                MULT,
+            )
+
         def make_da(k):
-            for j in range(width(k) // GROUP):
-                cols = slice(j * GROUP, (j + 1) * GROUP)
-                for m, factor in ((1, s_planes(k)), (0, u_planes(k))):
-                    nc.vector.tensor_tensor(
-                        words_by_runs(da_words(k)[:, j, m, :, :]),
-                        planes_by_runs(dh[k, j][:]),
-                        planes_by_runs(factor[:, :, cols]),
-                        MULT,
-                    )
+            own = list(range(SHARED[k], groups(k)))
+            for j in own[:2]:
+                product(k, j, 1)
+            for j in range(SHARED[k]):
+                exact_da3(k, j)
+            for j in own[:2]:
+                product(k, j, 0)
+            for m in (1, 0):
+                for j in own[2:]:
+                    product(k, j, m)
 
-        def da_codes(k, half):
-            return da_mx[k, half][:, : 4 * width(k)].bitcast(U32).rearrange("p (j m c) -> p j m c", m=2, c=GROUP)
+        def exact(k):
+            return da3_exact[:, : PACK * cut(k)].rearrange("p (j b) -> p j b", b=BLOCK)
 
-        def da_scales(k, half):
-            return da_mx[k, half][:, 4 * WIDE : 4 * WIDE + width(k)].rearrange("p (j m c) -> p j m c", m=2, c=GROUP)
+        def round_da3(k):
+            if SHARED[k]:
+                nc.scalar.copy(da_words(k)[:, : SHARED[k], 1, :], exact(k))
 
-        def quantize_da(k):
-            count = width(k) // GROUP // 2
-            for half in range(2):
-                da_mx[k, half] = turns.tile([P, 5 * WIDE], U8, tag="codes%d" % half, name="da_mx", align_bytes=64)
-                nc.vector.quantize_mx(
-                    out=da_codes(k, half).rearrange("p j m c -> p (j m c)").bitcast(FP8X4),
-                    scales=da_scales(k, half).rearrange("p j m c -> p (j m c)"),
-                    in_=da_words(k)[:, half * count : (half + 1) * count, :, :, :].rearrange("p j m c t -> p (j m c t)"),
+        def finish_da1(k):
+            if SHARED[k]:
+                nc.gpsimd.tensor_tensor(
+                    da_words(k)[:, : SHARED[k], 0, :], exact(k), y_flat(k).rearrange("p (j b) -> p j b", b=BLOCK), MULT
                 )
 
-        def second_product(k):
-            count = width(k) // GROUP // 2
-            for j0, j1 in [(0, count), (count, 2 * count)] if k == last else [(0, 2 * count)]:
-                dx_ps = psum_dx.tile([P, (j1 - j0) * GROUP], F32, name="dx_ps")
-                for j in range(j0, j1):
-                    e = first[k] + j * GROUP // C
-                    for m in range(2):
-                        nc.tensor.matmul_mx(
-                            out=dx_ps[:, (j - j0) * GROUP : (j - j0 + 1) * GROUP],
-                            lhsT=w13[m][:, e, :].bitcast(FP4X4),
-                            lhsT_scale=s13[m][:, e, :],
-                            rhs=da_codes(k, j // count)[:, j % count, m, :].bitcast(FP8X4),
-                            rhs_scale=da_scales(k, j // count)[:, j % count, m, :],
-                            start=(m == 0),
-                            stop=(m == 1),
-                        )
-                base = first[k] * C
-                if base + j1 * GROUP == S:
-                    nc.vector.tensor_copy(dx[:, base + j0 * GROUP :], dx_ps[:])
-                else:
-                    nc.scalar.copy(dx[:, base + j0 * GROUP : base + j1 * GROUP], dx_ps[:])
+        def da_codes(k):
+            return da_mx[k][:, : 8 * width(k)].bitcast(U32).rearrange("p (j m c) -> p j m c", m=2, c=GROUP)
 
+        def da_scales(k):
+            return da_mx[k][:, 8 * WIDE : 8 * WIDE + 2 * width(k)].rearrange("p (j m c) -> p j m c", m=2, c=GROUP)
+
+        def quantize_da(k):
+            count = groups(k) // 2
+            for half in halves(k):
+                part = slice(half * count, (half + 1) * count)
+                nc.vector.quantize_mx(
+                    out=da_codes(k)[:, part, :, :].rearrange("p j m c -> p (j m c)").bitcast(FP8X4),
+                    scales=da_scales(k)[:, part, :, :].rearrange("p j m c -> p (j m c)"),
+                    in_=da_words(k)[:, part, :, :].rearrange("p j m b -> p (j m b)"),
+                )
+
+        def lodge(name, tag, size):
+            return turns.tile([P, size], U8, tag=tag, name=name, align_bytes=64)
+
+        def second_product(k, j0, j1):
+            count = groups(k) // 2
+            dx_ps[k, j0] = psum_back.tile([P, (j1 - j0) * GROUP], F32, tag="dx", name="dx_ps")
+            for j in sorted(range(j0, j1), key=lambda g: halves(k).index(g // count)):
+                e = first[k] + j * GROUP // C
+                for m in range(2):
+                    nc.tensor.matmul_mx(
+                        out=dx_ps[k, j0][:, (j - j0) * GROUP : (j - j0 + 1) * GROUP],
+                        lhsT=w13[m][:, e, :].bitcast(FP4X4),
+                        lhsT_scale=s13[m][:, e, :],
+                        rhs=da_codes(k)[:, j, m, :].bitcast(FP8X4),
+                        rhs_scale=da_scales(k)[:, j, m, :],
+                        start=(m == 0),
+                        stop=(m == 1),
+                    )
+
+        load_s13()
         load_dy(0)
         nc.sync.dma_start(offs_sb[:], offs)
-        for c0 in (0, C):
-            nc.sync.dma_start(gate_row(-AHEAD)[:, c0 : c0 + C], gate[:P, c0 : c0 + C])
-        for step in range(1 - AHEAD, 1):
-            load_gate(step)
-        load_dy(1)
         load_a1(0)
-        load_s2(0)
-        load_dy(2)
-        load_s2(1)
+        nc.sync.dma_start(gate_first, gate[:P, :WIDE])
+        load_dy(1)
+        load_s2(range(5))
+        load_w2(0, UNITS[0] + UNITS[1])
         load_a1(1)
-        load_s2(2)
+        load_s2(range(5, 8))
+        load_dy(2)
         load_dy(3)
-        load_s2(3)
         load_a3(0)
-        load_w2(0)
-        load_a3(1)
+        nc.sync.dma_start(gate_rows[:turned, :], gate[0, WIDE:].rearrange("(b s) -> b s", s=GROUP))
         load_a1(2)
+        load_a3(1)
 
-        sigmoids(0)
-        for t in range(PACK):
-            for step in range(-AHEAD, 1):
-                if (step, t) == (-AHEAD, 0):
-                    gather(step, t, 0, C)
-                    gather(step, t, C, WIDE)
-                elif step < 0 or t < PACK // 2:
-                    gather(step, t, 0, WIDE)
+        sigmoid_plus(0)
+        sigmoid_minus(0)
+        square(0)
+        derivative(0)
+        sigmoid_plus(1)
+        sigmoid_minus(1)
+        square(1)
+        derivative(1)
+        for k, t in ((1, 0), (2, 0), (0, 0), (0, 1), (1, 1), (2, 1)):
+            gather(k, t)
+        w2_head = lodge("w2_head", "pairs0", 8 * H)
+        w2_sb[0], w2_sb[1] = w2_head[:, : 4 * H], w2_head[:, 4 * H :]
+        reorder_w2(0, w2_head[:])
         reorder_s2()
-        load_gate(1)
-        load_w2(1)
         unstack_s2(1)
-        load_w13(0, EARLY)
-        load_s13()
-        load_a3(2)
+        load_w2(2, UNITS[2])
         load_a1(3)
-        load_gate(2)
-        load_w2(2)
+        load_a3(2)
         unstack_s2(2)
-        round_g(0)
-        sigmoids(1)
-        round_g(1)
-        factor_u(nc.vector, 0, 0, PACK)
+        load_w13(0, EARLY)
+        for k, t in ((0, 2), (0, 3), (1, 2), (1, 3), (2, 3)):
+            gather(k, t)
+        turn_gate()
+        round_first()
+        g_head = lodge("g_head", "s4", 5 * WIDE)
+        g_codes[0], g_scales[0] = g_head[:, : 4 * WIDE], g_head[:, 4 * WIDE :]
+        quantize_g(0)
         first_product(0)
-        load_w2(3)
-        sigmoids(2)
-        gather_step(0, range(PACK // 2, PACK))
+        gather(2, 2)
+        factor_u(0, 2, 4)
+        factor_y(0)
+        factor_u(0, 1, 2)
+        load_w2(3, UNITS[3])
+        load_a1(4)
+        load_a3(3)
+        unstack_s2(3)
+        load_w2(4, UNITS[4])
+        apply_gate(1, 0)
+        apply_gate(1, 1)
+        sigmoid_plus(2)
 
         for k in range(len(UNITS)):
-            if 0 < k < last:
-                gather_step(k, gathers_of(k)[1])
             if k < last:
-                factor_u(nc.gpsimd, k + 1, 0, PACK)
-            for unit in ROUNDS.get(k, ()):
-                round_g(unit)
-            if k + 3 <= last:
-                sigmoids(k + 3)
+                factor_y(k + 1)
             make_da(k)
-            if k + 3 < last:
-                load_gate(k + 3)
-            if k + 3 <= last:
-                load_a3(k + 3)
+            finish_da1(k)
+            if k < last:
+                factor_u(k + 1, SHARED[k + 1], groups(k + 1))
+            scalar_step(k)
+            if k + 4 <= last:
+                unstack_s2(k + 4)
+                load_a3(k + 4)
             if k == 0:
                 load_w13(EARLY, E)
-            if k + 4 <= last:
-                load_a1(k + 4)
-            if k + 1 == last:
-                first_product(last)
-            quantize_da(k)
-            if k + 1 < last:
+            if k + 5 <= last:
+                load_a1(k + 5)
+            if k + AHEAD <= last:
+                for t in range(PACK):
+                    gather(k + AHEAD, t)
+            if k < last:
+                codes = lodge("codes", "s%d" % (k % HOMES), 5 * WIDE + 4 * H)
+                g_codes[k + 1] = codes[:, : 4 * width(k + 1)]
+                g_scales[k + 1] = codes[:, 4 * WIDE : 4 * WIDE + width(k + 1)]
+                quantize_g(k + 1)
                 first_product(k + 1)
-            second_product(k)
-            if k + 4 <= last:
-                load_w2(k + 4)
-            if k + 3 <= last:
-                unstack_s2(k + 3)
+            da_mx[k] = lodge("da_mx", "pairs%d" % ((k + 1) % 2), 10 * WIDE + 4 * H)
+            if k + 2 <= last:
+                w2_sb[k + 2] = (codes[:, 5 * WIDE :] if k <= 3 else da_mx[k][:, 10 * WIDE :])[:, : UNITS[k + 2] * 2 * H]
+                reorder_w2(k + 2, w2_sb[k + 2])
+            if k == 3:
+                own = a1_sb[k + 2][:]
+                nc.vector.tensor_scalar(own, own, -1.0, 0.25, MULT, ADD)
+            quantize_da(k)
+            if k < last:
+                second_product(k, 0, groups(k))
+            if k + 5 <= last:
+                load_w2(k + 5, UNITS[k + 5])
             if k == 3:
                 for r, pos in enumerate((pos1, pos2, pos3)):
                     nc.sync.dma_start(pos_sb[r][:], pos)
+
+        copy_dx(last - 1)
+        second_product(last, 0, 1)
+        nc.scalar.copy(dx[:, S - 2 * GROUP : S - GROUP], dx_ps[last, 0][:])
+        second_product(last, 1, 2)
+        nc.vector.tensor_copy(dx[:, S - GROUP :], dx_ps[last, 1][:])
 
         for r in range(3):
             cuts = LAST_CUTS if r == 2 else OUT_CUTS
             for c0, c1 in zip(cuts[:-1], cuts[1:]):
                 picked = dx[:].indirect(pos_sb[r][:, c0 // 16 : c1 // 16])
                 if r == 0:
-                    nc.vector.tensor_copy(s_home[0][:, c0:c1], picked)
+                    nc.vector.tensor_copy(home[0][:, c0:c1], picked)
                 else:
-                    nc.vector.tensor_tensor(s_home[r][:, c0:c1], picked, s_home[r - 1][:, c0:c1], ADD)
+                    nc.vector.tensor_tensor(home[r][:, c0:c1], picked, home[r - 1][:, c0:c1], ADD)
                 if r == 2:
-                    nc.sync.dma_start(out[:, c0:c1], s_home[r][:, c0:c1])
+                    nc.sync.dma_start(out[:, c0:c1], home[r][:, c0:c1])

@@ -52,6 +52,10 @@ def as_planes(ap):
     return ap.rearrange("p (t s) -> p t s", t=PACK)
 
 
+def by_groups(ap):
+    return ap.rearrange("p (j t c) -> p j t c", t=PACK, c=GROUP)
+
+
 def as_words(ap):
     return ap.rearrange("p (s t) -> p s t", t=PACK)
 
@@ -117,8 +121,8 @@ def tile_moe_bdx_glu_sigmoid_kernel(
         def cut(k):
             return SHARED[k] * GROUP
 
-        def sm_words(k):
-            return as_words(sm_home[k % RING][:, WIDE - 2 * cut(k) : WIDE + 2 * cut(k)])
+        def sm_flat(k):
+            return (sm_home[k % RING][:, WIDE - 2 * cut(k) : WIDE + 2 * cut(k)])
 
         def y_flat(k):
             return home[(k - 2) % HOMES][:, : PACK * cut(k)]
@@ -175,7 +179,7 @@ def tile_moe_bdx_glu_sigmoid_kernel(
         def load_s13():
             for plane, scales in zip(s13, (w1_scales, w3_scales)):
                 for quad in range(4):
-                    nc.gpsimd.dma_start(
+                    nc.sync.dma_start(
                         plane[32 * quad : 32 * quad + 4, :, :].bitcast(I32),
                         scales[:, 0, 4 * quad : 4 * quad + 4, :].rearrange("e f n -> f e n").bitcast(I32),
                     )
@@ -264,11 +268,11 @@ def tile_moe_bdx_glu_sigmoid_kernel(
         def sigmoid_minus(k):
             if cut(k):
                 nc.scalar.activation(
-                    words_by_runs(sm_words(k)), planes_by_runs(a1_sb[k][:, :, : cut(k)]), ACT.Sigmoid, scale=-1.0
+                    by_groups(sm_flat(k)), a1_sb[k][:, :, : cut(k)].rearrange("p t (j c) -> p j t c", c=GROUP), ACT.Sigmoid, scale=-1.0
                 )
 
         def sigmoid_plus(k):
-            s_sb[k] = turns.tile([P, PACK, width(k) - cut(k)], F32, tag="s%d" % (k % HOMES), name="s", align_bytes=64)
+            s_sb[k] = turns.tile([P, PACK, width(k) - cut(k)], F32, tag="s%d" % (k % RING), name="s", align_bytes=64)
             nc.scalar.activation(s_sb[k][:], a1_sb[k][:, :, cut(k) :], ACT.Sigmoid)
 
         def square(k):
@@ -283,41 +287,48 @@ def tile_moe_bdx_glu_sigmoid_kernel(
                 nc.scalar.copy(dx[:, slots(k)], dx_ps[k, 0][:])
 
         def scalar_step(k):
-            if k != 4:
-                round_da3(k)
-            if k == 4:
-                round_da3(k)
-                sigmoid_plus(k + 2)
             if k < last:
                 for j in range(2, groups(k + 1)):
                     apply_gate(k + 1, j)
+            if k in (0, 5):
+                (derivative if k == 0 else square)(k + 2)
+            round_da3(k)
             if k + 2 <= last:
                 sigmoid_minus(k + 2)
-            if k >= 4:
+            if k >= 6:
                 copy_dx(k - 2)
             if k < last:
                 for half in range(groups(k + 1) // 2):
                     turn_back(k + 1, half)
-            if k == 5:
-                sigmoid_plus(k + 2)
-            if k + 2 <= last:
-                square(k + 2)
-                if k != 4:
-                    apply_gate(k + 2, 0)
-                if k != 3:
-                    derivative(k + 2)
-                if k == 4:
-                    apply_gate(k + 2, 0)
-                apply_gate(k + 2, 1)
-            if k < 4:
-                copy_dx(k - 2)
-            if k < 3:
+            if k <= 2:
                 sigmoid_plus(k + 3)
+                apply_gate(k + 2, 0)
+                square(k + 3)
+                apply_gate(k + 2, 1)
+                derivative(k + 3)
+                copy_dx(k - 2)
+            elif k == 3:
+                apply_gate(k + 2, 0)
+                apply_gate(k + 2, 1)
+                sigmoid_plus(k + 3)
+                copy_dx(k - 2)
+                square(k + 3)
+            elif k <= 5:
+                if k == 5:
+                    derivative(k + 2)
+                copy_dx(k - 2)
+                apply_gate(k + 2, 0)
+                apply_gate(k + 2, 1)
+                if k + 3 <= last:
+                    sigmoid_plus(k + 3)
 
         def factor_y(k):
             if cut(k):
                 nc.gpsimd.tensor_tensor(
-                    as_words(y_flat(k)), a3_sb[k][:, :, : cut(k)].rearrange("p t c -> p c t"), sm_words(k), MULT
+                    by_groups(y_flat(k)),
+                    a3_sb[k][:, :, : cut(k)].rearrange("p t (j c) -> p j t c", c=GROUP),
+                    by_groups(sm_flat(k)),
+                    MULT,
                 )
 
         def factor_u(k, j0, j1):
@@ -336,7 +347,7 @@ def tile_moe_bdx_glu_sigmoid_kernel(
             )
 
         def first_product(k):
-            for j in sorted(range(groups(k)), key=lambda g: (g - SHARED[k]) % groups(k) if SHARED[k] == 2 else g):
+            for j in sorted(range(groups(k)), key=lambda g: (g - SHARED[k]) % groups(k)):
                 e = j * GROUP // C
                 dh[k, j] = psum_dh.tile([P, PACK, GROUP], F32, name="dh")
                 for t in range(PACK):
@@ -356,10 +367,10 @@ def tile_moe_bdx_glu_sigmoid_kernel(
 
         def exact_da3(k, j):
             nc.vector.scalar_tensor_tensor(
-                as_words(da3_exact[:, j * BLOCK : (j + 1) * BLOCK]),
-                sm_words(k)[:, j * GROUP : (j + 1) * GROUP, :],
+                da3_exact[:, j * BLOCK : (j + 1) * BLOCK],
+                sm_flat(k)[:, j * BLOCK : (j + 1) * BLOCK],
                 1.0,
-                dh[k, j][:].rearrange("p t c -> p c t"),
+                dh[k, j][:].rearrange("p t c -> p (t c)"),
                 SUB,
                 MULT,
             )
@@ -374,28 +385,26 @@ def tile_moe_bdx_glu_sigmoid_kernel(
             )
 
         def make_da(k):
-            own = list(range(SHARED[k], groups(k)))
-            for j in own[:2]:
+            for j in range(SHARED[k], groups(k)):
                 product(k, j, 1)
+                product(k, j, 0)
             for j in range(SHARED[k]):
                 exact_da3(k, j)
-            for j in own[:2]:
-                product(k, j, 0)
-            for m in (1, 0):
-                for j in own[2:]:
-                    product(k, j, m)
-
-        def exact(k):
-            return da3_exact[:, : PACK * cut(k)].rearrange("p (j b) -> p j b", b=BLOCK)
 
         def round_da3(k):
             if SHARED[k]:
-                nc.scalar.copy(da_words(k)[:, : SHARED[k], 1, :], exact(k))
+                nc.scalar.copy(
+                    da_words(k)[:, : SHARED[k], 1, :].rearrange("p j (c i t) -> p j c t i", t=PACK, i=RUN),
+                    da3_exact[:, : PACK * cut(k)].rearrange("p (j t c i) -> p j c t i", t=PACK, c=GROUP // RUN, i=RUN),
+                )
 
         def finish_da1(k):
             if SHARED[k]:
                 nc.gpsimd.tensor_tensor(
-                    da_words(k)[:, : SHARED[k], 0, :], exact(k), y_flat(k).rearrange("p (j b) -> p j b", b=BLOCK), MULT
+                    da_words(k)[:, : SHARED[k], 0, :].rearrange("p j (c t) -> p j t c", t=PACK),
+                    by_groups(da3_exact[:, : PACK * cut(k)]),
+                    by_groups(y_flat(k)),
+                    MULT,
                 )
 
         def da_codes(k):
@@ -433,7 +442,6 @@ def tile_moe_bdx_glu_sigmoid_kernel(
                         stop=(m == 1),
                     )
 
-        load_s13()
         load_dy(0)
         nc.sync.dma_start(offs_sb[:], offs)
         load_a1(0)
@@ -444,8 +452,8 @@ def tile_moe_bdx_glu_sigmoid_kernel(
         load_a1(1)
         load_s2(range(5, 8))
         load_dy(2)
-        load_dy(3)
         load_a3(0)
+        load_dy(3)
         nc.sync.dma_start(gate_rows[:turned, :], gate[0, WIDE:].rearrange("(b s) -> b s", s=GROUP))
         load_a1(2)
         load_a3(1)
@@ -469,12 +477,11 @@ def tile_moe_bdx_glu_sigmoid_kernel(
         load_a1(3)
         load_a3(2)
         unstack_s2(2)
-        load_w13(0, EARLY)
         for k, t in ((0, 2), (0, 3), (1, 2), (1, 3), (2, 3)):
             gather(k, t)
         turn_gate()
         round_first()
-        g_head = lodge("g_head", "s4", 5 * WIDE)
+        g_head = lodge("g_head", "s3", 5 * WIDE)
         g_codes[0], g_scales[0] = g_head[:, : 4 * WIDE], g_head[:, 4 * WIDE :]
         quantize_g(0)
         first_product(0)
@@ -485,48 +492,49 @@ def tile_moe_bdx_glu_sigmoid_kernel(
         load_w2(3, UNITS[3])
         load_a1(4)
         load_a3(3)
-        unstack_s2(3)
-        load_w2(4, UNITS[4])
+        load_w13(0, EARLY)
+        load_s13()
         apply_gate(1, 0)
         apply_gate(1, 1)
         sigmoid_plus(2)
+        square(2)
 
         for k in range(len(UNITS)):
             if k < last:
                 factor_y(k + 1)
             make_da(k)
-            finish_da1(k)
             if k < last:
                 factor_u(k + 1, SHARED[k + 1], groups(k + 1))
+            finish_da1(k)
             scalar_step(k)
+            if k + 5 <= last:
+                load_a1(k + 5)
+            if k + 3 <= last:
+                unstack_s2(k + 3)
             if k + 4 <= last:
-                unstack_s2(k + 4)
+                load_w2(k + 4, UNITS[k + 4])
                 load_a3(k + 4)
             if k == 0:
                 load_w13(EARLY, E)
-            if k + 5 <= last:
-                load_a1(k + 5)
             if k + AHEAD <= last:
-                for t in range(PACK):
+                for t in (2, 3, 0, 1):
                     gather(k + AHEAD, t)
             if k < last:
-                codes = lodge("codes", "s%d" % (k % HOMES), 5 * WIDE + 4 * H)
+                codes = lodge("codes", "s%d" % (k % RING), 5 * WIDE)
                 g_codes[k + 1] = codes[:, : 4 * width(k + 1)]
                 g_scales[k + 1] = codes[:, 4 * WIDE : 4 * WIDE + width(k + 1)]
                 quantize_g(k + 1)
                 first_product(k + 1)
             da_mx[k] = lodge("da_mx", "pairs%d" % ((k + 1) % 2), 10 * WIDE + 4 * H)
             if k + 2 <= last:
-                w2_sb[k + 2] = (codes[:, 5 * WIDE :] if k <= 3 else da_mx[k][:, 10 * WIDE :])[:, : UNITS[k + 2] * 2 * H]
+                w2_sb[k + 2] = da_mx[k][:, 10 * WIDE : 10 * WIDE + UNITS[k + 2] * 2 * H]
                 reorder_w2(k + 2, w2_sb[k + 2])
-            if k == 3:
+            if k == 4:
                 own = a1_sb[k + 2][:]
                 nc.vector.tensor_scalar(own, own, -1.0, 0.25, MULT, ADD)
             quantize_da(k)
             if k < last:
                 second_product(k, 0, groups(k))
-            if k + 5 <= last:
-                load_w2(k + 5, UNITS[k + 5])
             if k == 3:
                 for r, pos in enumerate((pos1, pos2, pos3)):
                     nc.sync.dma_start(pos_sb[r][:], pos)

@@ -25,7 +25,7 @@ ADD = mybir.AluOpType.add
 SUB = mybir.AluOpType.subtract
 
 UNITS = [2, 2, 2, 2, 2, 2, 2, 1]
-SHARED = [1, 2, 2, 2, 1, 0, 0, 0]
+SHARED = [1, 2, 2, 2, 0, 0, 0, 0]
 AHEAD = 3
 RING = 4
 HOMES = 5
@@ -73,10 +73,9 @@ def tile_moe_bdx_glu_sigmoid_kernel(
         keep = ctx.enter_context(tc.tile_pool(name="keep", bufs=1))
         turns = ctx.enter_context(tc.tile_pool(name="turns", bufs=1))
         ring3 = ctx.enter_context(tc.tile_pool(name="ring3", bufs=3))
-        ring4 = ctx.enter_context(tc.tile_pool(name="ring4", bufs=4))
         psum_dh = ctx.enter_context(tc.psum_pool(name="psum_dh", bufs=4))
         psum_turn = ctx.enter_context(tc.psum_pool(name="psum_turn", bufs=1))
-        psum_back = ctx.enter_context(tc.psum_pool(name="psum_back", bufs=2))
+        psum_back = ctx.enter_context(tc.psum_pool(name="psum_back", bufs=1))
 
         offs_sb = keep.tile([P, S // 16], U16, name="offs_sb")
         pos_sb = [keep.tile([P, T // 16], U16, name="pos_sb%d" % r) for r in range(3)]
@@ -90,7 +89,6 @@ def tile_moe_bdx_glu_sigmoid_kernel(
         sm_home = [keep.tile([P, SPAN // 2], F32, name="sm_home%d" % r, align_bytes=64) for r in range(RING)]
         home = [keep.tile([P, SPAN], F32, name="home%d" % r, align_bytes=64) for r in range(HOMES)]
         head = dx[:, :SPAN]
-        da3_exact = keep.tile([P, 2 * BLOCK], F32, name="da3_exact", align_bytes=64)
         ident = keep.tile([P, P], F32, name="ident")
         gate_rows = keep.tile([P, GROUP], F32, name="gate_rows")
         gate_cols = keep.tile([P, turned], F32, name="gate_cols")
@@ -107,7 +105,7 @@ def tile_moe_bdx_glu_sigmoid_kernel(
         make_identity(nc, ident[:])
 
         a1_sb, a3_sb, s_sb, w2_raw, dh, da_mx, g_pairs, turned_g = {}, {}, {}, {}, {}, {}, {}, {}
-        w2_sb, g_codes, g_scales, dx_ps = {}, {}, {}, {}
+        w2_sb, g_codes, g_scales, dx_ps, da3_exact = {}, {}, {}, {}, {}
 
         def width(k):
             return UNITS[k] * C
@@ -125,14 +123,18 @@ def tile_moe_bdx_glu_sigmoid_kernel(
             return (sm_home[k % RING][:, WIDE - 2 * cut(k) : WIDE + 2 * cut(k)])
 
         def y_flat(k):
-            return home[(k - 2) % HOMES][:, : PACK * cut(k)]
+            return home[(k - 2) % HOMES][:, SPAN - PACK * cut(k) :]
 
         def u_group(k, j0, j1):
             if k == 0:
                 if j0 >= 2:
-                    return as_planes(home[-2 % HOMES][:, SPAN // 2 :])[:, :, (j0 - 2) * GROUP : (j1 - 2) * GROUP]
-                return as_planes(home[-2 % HOMES][:, BLOCK : 2 * BLOCK])
-            planes = as_planes(home[(k - 2) % HOMES][:, PACK * cut(k) : PACK * width(k)])
+                    return as_planes(home[-2 % HOMES][:, : SPAN // 2])[:, :, (j0 - 2) * GROUP : (j1 - 2) * GROUP]
+                return as_planes(home[-2 % HOMES][:, 2 * BLOCK : 3 * BLOCK])
+            if SHARED[k - 1] and not SHARED[k]:
+                start = SPAN // 2 if j0 < 2 else 0
+                part = as_planes(home[(k - 2) % HOMES][:, start : start + SPAN // 2])
+                return part[:, :, j0 % 2 * GROUP : (j0 % 2 + j1 - j0) * GROUP]
+            planes = as_planes(home[(k - 2) % HOMES][:, : PACK * (width(k) - cut(k))])
             return planes[:, :, j0 * GROUP - cut(k) : j1 * GROUP - cut(k)]
 
         def da_words(k):
@@ -143,11 +145,13 @@ def tile_moe_bdx_glu_sigmoid_kernel(
                 return head[:, t * WIDE : (t + 1) * WIDE]
             if k < AHEAD:
                 return home[k][:, t * WIDE : (t + 1) * WIDE]
+            if k == last:
+                return home[(k - AHEAD - 2) % HOMES][:, t * width(k) : (t + 1) * width(k)]
             if t < 2:
                 return sm_home[(k - AHEAD) % RING][:, WIDE + (t - 1) * width(k) : WIDE + t * width(k)]
-            return home[(k - AHEAD - 2) % HOMES][:, SPAN // 2 + (t - 2) * width(k) : SPAN // 2 + (t - 1) * width(k)]
+            return home[(k - AHEAD - 2) % HOMES][:, (t - 2) * width(k) : (t - 1) * width(k)]
 
-        gate_first = home[-2 % HOMES][:, SPAN // 2 : SPAN // 2 + WIDE]
+        gate_first = home[-2 % HOMES][:, :WIDE]
 
         def load_dy(t):
             nc.sync.dma_start(dy[t][:], dyT.rearrange("(p t) c -> p t c", t=PACK)[:, t, :])
@@ -157,7 +161,7 @@ def tile_moe_bdx_glu_sigmoid_kernel(
             nc.sync.dma_start(a1_sb[k][:], a1.rearrange("(p t) s -> p t s", t=PACK)[:, :, slots(k)])
 
         def load_a3(k):
-            a3_sb[k] = ring4.tile([P, PACK, width(k)], F32, name="a3_sb")
+            a3_sb[k] = turns.tile([P, PACK, width(k)], F32, tag="a3_%d" % (k % RING), name="a3_sb")
             nc.sync.dma_start(a3_sb[k][:], a3.rearrange("(p t) s -> p t s", t=PACK)[:, :, slots(k)])
 
         def load_w2(k, count):
@@ -179,7 +183,7 @@ def tile_moe_bdx_glu_sigmoid_kernel(
         def load_s13():
             for plane, scales in zip(s13, (w1_scales, w3_scales)):
                 for quad in range(4):
-                    nc.sync.dma_start(
+                    nc.gpsimd.dma_start(
                         plane[32 * quad : 32 * quad + 4, :, :].bitcast(I32),
                         scales[:, 0, 4 * quad : 4 * quad + 4, :].rearrange("e f n -> f e n").bitcast(I32),
                     )
@@ -212,13 +216,15 @@ def tile_moe_bdx_glu_sigmoid_kernel(
         def turn_gate():
             bank = psum_back.tile([P, PACK, GROUP], F32, tag="dx", name="turn")
             nc.tensor.transpose(bank[:, 0, :], gate_rows[:], ident[:])
-            for k in range(1, len(UNITS)):
-                col = first[k] * C // GROUP - skipped
-                for j0, j1, sign in ((0, SHARED[k], -1.0), (SHARED[k], groups(k), 1.0)):
-                    if j1 > j0:
-                        nc.scalar.activation(
-                            gate_cols[:, col + j0 : col + j1], bank[:, 0, col + j0 : col + j1], ACT.Copy, scale=sign
-                        )
+            paired = SHARED[1:].count(2) * PACK
+            for j0, sign in ((0, -1.0), (2, 1.0)):
+                nc.scalar.activation(
+                    gate_cols[:, :paired].rearrange("p (k j) -> p k j", j=PACK)[:, :, j0 : j0 + 2],
+                    bank[:, 0, :paired].rearrange("p (k j) -> p k j", j=PACK)[:, :, j0 : j0 + 2],
+                    ACT.Copy,
+                    scale=sign,
+                )
+            nc.scalar.copy(gate_cols[:, paired:], bank[:, 0, paired:turned])
 
         def gather(k, t):
             picked = dy[t][:].indirect(offs_sb[:, first[k] * C // 16 : (first[k] * C + width(k)) // 16])
@@ -228,7 +234,7 @@ def tile_moe_bdx_glu_sigmoid_kernel(
                 nc.vector.tensor_copy(gathered(k, t), picked)
 
         def round_first():
-            g_pairs[0] = home[-2 % HOMES][:, : SPAN // 2]
+            g_pairs[0] = home[-2 % HOMES][:, SPAN // 2 :]
             planes = as_planes(head[:, :SPAN])
             rounded = as_words(g_pairs[0][:].bitcast(BF16))
             for c0, c1, sign in ((0, cut(0), -1.0), (cut(0), WIDE, 1.0)):
@@ -237,7 +243,7 @@ def tile_moe_bdx_glu_sigmoid_kernel(
                 )
 
         def apply_gate(k, j):
-            bank = psum_turn.tile([P, PACK, GROUP], F32, tag="turn%d" % (j % 2), name="turn")
+            bank = psum_turn.tile([P, PACK, GROUP], F32, tag="turn%d" % (j % 3), name="turn")
             for t in range(PACK):
                 nc.tensor.transpose(bank[:, t, :], gathered(k, t)[:, j * GROUP : (j + 1) * GROUP], ident[:])
             turned_g[k, j] = turns.tile([P, N], BF16, tag="turned%d" % j, name="turned_g", align_bytes=64)
@@ -254,7 +260,7 @@ def tile_moe_bdx_glu_sigmoid_kernel(
                 g_pairs[k] = turns.tile(
                     [P, 2 * width(k)], F32, tag="pairs%d" % (k % 2), name="g_pairs", align_bytes=64
                 )
-            bank = psum_turn.tile([P, 2, 2, GROUP], F32, tag="turn%d" % half, name="back")
+            bank = psum_turn.tile([P, 2, 2, GROUP], F32, tag="turn%d" % (half + 1), name="back")
             for jj in range(2):
                 for u in range(2):
                     nc.tensor.transpose(
@@ -286,41 +292,59 @@ def tile_moe_bdx_glu_sigmoid_kernel(
             if k >= 0:
                 nc.scalar.copy(dx[:, slots(k)], dx_ps[k, 0][:])
 
+        def turn_backs(k):
+            for half in range(groups(k) // 2):
+                turn_back(k, half)
+
         def scalar_step(k):
-            if k < last:
-                for j in range(2, groups(k + 1)):
-                    apply_gate(k + 1, j)
-            if k in (0, 5):
-                (derivative if k == 0 else square)(k + 2)
-            round_da3(k)
-            if k + 2 <= last:
-                sigmoid_minus(k + 2)
-            if k >= 6:
-                copy_dx(k - 2)
-            if k < last:
-                for half in range(groups(k + 1) // 2):
-                    turn_back(k + 1, half)
             if k <= 2:
-                sigmoid_plus(k + 3)
+                round_da3(k)
                 apply_gate(k + 2, 0)
-                square(k + 3)
+                turn_backs(k + 1)
+                if k > 0:
+                    sigmoid_minus(k + 2)
+                copy_dx(k - 1)
+                sigmoid_plus(k + 3)
                 apply_gate(k + 2, 1)
-                derivative(k + 3)
-                copy_dx(k - 2)
+                if k < 2:
+                    square(k + 3)
+                apply_gate(k + 2, 2)
+                if k < 2:
+                    derivative(k + 3)
+                apply_gate(k + 2, 3)
+                if k == 2:
+                    square(k + 3)
             elif k == 3:
                 apply_gate(k + 2, 0)
+                turn_backs(k + 1)
+                round_da3(k)
+                derivative(k + 2)
+                copy_dx(k - 1)
                 apply_gate(k + 2, 1)
+                apply_gate(k + 2, 2)
                 sigmoid_plus(k + 3)
-                copy_dx(k - 2)
+                apply_gate(k + 2, 3)
                 square(k + 3)
-            elif k <= 5:
-                if k == 5:
-                    derivative(k + 2)
-                copy_dx(k - 2)
+            elif k == 4:
+                apply_gate(k + 2, 0)
+                turn_backs(k + 1)
+                round_da3(k)
+                derivative(k + 2)
+                copy_dx(k - 1)
+                for j in range(1, groups(k + 2)):
+                    apply_gate(k + 2, j)
+            elif k == 5:
+                sigmoid_plus(k + 2)
+                turn_backs(k + 1)
+                square(k + 2)
+                copy_dx(k - 1)
+                derivative(k + 2)
                 apply_gate(k + 2, 0)
                 apply_gate(k + 2, 1)
-                if k + 3 <= last:
-                    sigmoid_plus(k + 3)
+            else:
+                copy_dx(k - 1)
+                if k < last:
+                    turn_backs(k + 1)
 
         def factor_y(k):
             if cut(k):
@@ -347,7 +371,7 @@ def tile_moe_bdx_glu_sigmoid_kernel(
             )
 
         def first_product(k):
-            for j in sorted(range(groups(k)), key=lambda g: (g - SHARED[k]) % groups(k)):
+            for j in range(groups(k)):
                 e = j * GROUP // C
                 dh[k, j] = psum_dh.tile([P, PACK, GROUP], F32, name="dh")
                 for t in range(PACK):
@@ -367,7 +391,7 @@ def tile_moe_bdx_glu_sigmoid_kernel(
 
         def exact_da3(k, j):
             nc.vector.scalar_tensor_tensor(
-                da3_exact[:, j * BLOCK : (j + 1) * BLOCK],
+                da3_exact[k][:, j * BLOCK : (j + 1) * BLOCK],
                 sm_flat(k)[:, j * BLOCK : (j + 1) * BLOCK],
                 1.0,
                 dh[k, j][:].rearrange("p t c -> p (t c)"),
@@ -385,24 +409,27 @@ def tile_moe_bdx_glu_sigmoid_kernel(
             )
 
         def make_da(k):
-            for j in range(SHARED[k], groups(k)):
-                product(k, j, 1)
-                product(k, j, 0)
-            for j in range(SHARED[k]):
-                exact_da3(k, j)
+            if SHARED[k]:
+                da3_exact[k] = turns.tile([P, 2 * BLOCK], F32, tag="exact%d" % (k % 2), name="da3_exact", align_bytes=64)
+            for j in range(groups(k)):
+                if j < SHARED[k]:
+                    exact_da3(k, j)
+                else:
+                    product(k, j, 1)
+                    product(k, j, 0)
 
         def round_da3(k):
             if SHARED[k]:
                 nc.scalar.copy(
                     da_words(k)[:, : SHARED[k], 1, :].rearrange("p j (c i t) -> p j c t i", t=PACK, i=RUN),
-                    da3_exact[:, : PACK * cut(k)].rearrange("p (j t c i) -> p j c t i", t=PACK, c=GROUP // RUN, i=RUN),
+                    da3_exact[k][:, : PACK * cut(k)].rearrange("p (j t c i) -> p j c t i", t=PACK, c=GROUP // RUN, i=RUN),
                 )
 
         def finish_da1(k):
             if SHARED[k]:
                 nc.gpsimd.tensor_tensor(
                     da_words(k)[:, : SHARED[k], 0, :].rearrange("p j (c t) -> p j t c", t=PACK),
-                    by_groups(da3_exact[:, : PACK * cut(k)]),
+                    by_groups(da3_exact[k][:, : PACK * cut(k)]),
                     by_groups(y_flat(k)),
                     MULT,
                 )
@@ -428,7 +455,8 @@ def tile_moe_bdx_glu_sigmoid_kernel(
 
         def second_product(k, j0, j1):
             count = groups(k) // 2
-            dx_ps[k, j0] = psum_back.tile([P, (j1 - j0) * GROUP], F32, tag="dx", name="dx_ps")
+            pool, tag = (psum_turn, "turn%d" % (2 * j0)) if k == last else (psum_back, "dx")
+            dx_ps[k, j0] = pool.tile([P, (j1 - j0) * GROUP], F32, tag=tag, name="dx_ps")
             for j in sorted(range(j0, j1), key=lambda g: halves(k).index(g // count)):
                 e = first[k] + j * GROUP // C
                 for m in range(2):
@@ -442,22 +470,24 @@ def tile_moe_bdx_glu_sigmoid_kernel(
                         stop=(m == 1),
                     )
 
+        load_s13()
         load_dy(0)
         nc.sync.dma_start(offs_sb[:], offs)
+        nc.sync.dma_start(gate_rows[:turned, :], gate[0, WIDE:].rearrange("(b s) -> b s", s=GROUP))
         load_a1(0)
         nc.sync.dma_start(gate_first, gate[:P, :WIDE])
         load_dy(1)
-        load_s2(range(5))
+        load_s2(range(4))
         load_w2(0, UNITS[0] + UNITS[1])
         load_a1(1)
-        load_s2(range(5, 8))
+        load_s2(range(4, 8))
         load_dy(2)
-        load_a3(0)
         load_dy(3)
-        nc.sync.dma_start(gate_rows[:turned, :], gate[0, WIDE:].rearrange("(b s) -> b s", s=GROUP))
+        load_a3(0)
         load_a1(2)
         load_a3(1)
 
+        turn_gate()
         sigmoid_plus(0)
         sigmoid_minus(0)
         square(0)
@@ -479,7 +509,6 @@ def tile_moe_bdx_glu_sigmoid_kernel(
         unstack_s2(2)
         for k, t in ((0, 2), (0, 3), (1, 2), (1, 3), (2, 3)):
             gather(k, t)
-        turn_gate()
         round_first()
         g_head = lodge("g_head", "s3", 5 * WIDE)
         g_codes[0], g_scales[0] = g_head[:, : 4 * WIDE], g_head[:, 4 * WIDE :]
@@ -489,23 +518,28 @@ def tile_moe_bdx_glu_sigmoid_kernel(
         factor_u(0, 2, 4)
         factor_y(0)
         factor_u(0, 1, 2)
+        load_w13(0, EARLY)
         load_w2(3, UNITS[3])
         load_a1(4)
         load_a3(3)
-        load_w13(0, EARLY)
-        load_s13()
-        apply_gate(1, 0)
-        apply_gate(1, 1)
+        for j in range(3):
+            apply_gate(1, j)
         sigmoid_plus(2)
+        apply_gate(1, 3)
         square(2)
+        sigmoid_minus(2)
+        derivative(2)
 
         for k in range(len(UNITS)):
-            if k < last:
+            split = 2 if SHARED[k] else 0
+            if k < last and SHARED[k + 1]:
                 factor_y(k + 1)
+            elif split:
+                factor_u(k + 1, 0, split)
             make_da(k)
-            if k < last:
-                factor_u(k + 1, SHARED[k + 1], groups(k + 1))
             finish_da1(k)
+            if k < last:
+                factor_u(k + 1, split, groups(k + 1))
             scalar_step(k)
             if k + 5 <= last:
                 load_a1(k + 5)
@@ -520,18 +554,16 @@ def tile_moe_bdx_glu_sigmoid_kernel(
                 for t in (2, 3, 0, 1):
                     gather(k + AHEAD, t)
             if k < last:
-                codes = lodge("codes", "s%d" % (k % RING), 5 * WIDE)
+                after_s = lodge("after_s", "s%d" % (k % RING), 5 * WIDE)
+                codes = lodge("codes", "exact%d" % (k % 2), 4 * WIDE) if SHARED[k] else after_s
                 g_codes[k + 1] = codes[:, : 4 * width(k + 1)]
-                g_scales[k + 1] = codes[:, 4 * WIDE : 4 * WIDE + width(k + 1)]
+                g_scales[k + 1] = after_s[:, 4 * WIDE : 4 * WIDE + width(k + 1)]
                 quantize_g(k + 1)
                 first_product(k + 1)
             da_mx[k] = lodge("da_mx", "pairs%d" % ((k + 1) % 2), 10 * WIDE + 4 * H)
             if k + 2 <= last:
                 w2_sb[k + 2] = da_mx[k][:, 10 * WIDE : 10 * WIDE + UNITS[k + 2] * 2 * H]
                 reorder_w2(k + 2, w2_sb[k + 2])
-            if k == 4:
-                own = a1_sb[k + 2][:]
-                nc.vector.tensor_scalar(own, own, -1.0, 0.25, MULT, ADD)
             quantize_da(k)
             if k < last:
                 second_product(k, 0, groups(k))
@@ -539,7 +571,6 @@ def tile_moe_bdx_glu_sigmoid_kernel(
                 for r, pos in enumerate((pos1, pos2, pos3)):
                     nc.sync.dma_start(pos_sb[r][:], pos)
 
-        copy_dx(last - 1)
         second_product(last, 0, 1)
         nc.scalar.copy(dx[:, S - 2 * GROUP : S - GROUP], dx_ps[last, 0][:])
         second_product(last, 1, 2)

@@ -36,7 +36,7 @@ OUT_CUTS = [0, 640, 1280]
 LAST_CUTS = [0, 640, 1088, 1280]
 RUN = 4
 LINE = 8
-EARLY = 4
+EARLY = 6
 LIVE = 100
 
 
@@ -85,23 +85,18 @@ def tile_moe_bdx_glu_sigmoid_kernel(
         s2_all = keep.tile([P, E * H], U8, name="s2_all", align_bytes=64)
         s2_first = keep.tile([P, 2, H], U8, name="s2_first", align_bytes=64)
         w13 = [keep.tile([P, E, 2 * K], U8, name="w13_%d" % m, align_bytes=64) for m in range(2)]
-        s13 = [keep.tile([P, E, K], U8, name="s13_%d" % m, align_bytes=64) for m in range(2)]
+        s13 = keep.tile([P, E, 2, K], U8, name="s13", align_bytes=64)
         sm_home = [keep.tile([P, SPAN // 2], F32, name="sm_home%d" % r, align_bytes=64) for r in range(RING)]
         home = [keep.tile([P, SPAN], F32, name="home%d" % r, align_bytes=64) for r in range(HOMES)]
         head = dx[:, :SPAN]
         ident = keep.tile([P, P], F32, name="ident")
         gate_rows = keep.tile([P, GROUP], F32, name="gate_rows")
         gate_cols = keep.tile([P, turned], F32, name="gate_cols")
-        minus_half = keep.tile([P, 1], F32, name="minus_half")
-        quarter = keep.tile([P, 1], F32, name="quarter")
 
-        nc.vector.memset(minus_half[:], -0.5)
-        nc.vector.memset(quarter[:], 0.25)
         nc.vector.memset(gate_rows[:], 0.0)
         nc.vector.memset(stacked[:, 1, :].bitcast(I32), 0)
         nc.vector.memset(s2_all[96:, 2 * H :].bitcast(I32), 0)
-        for plane in s13:
-            nc.vector.memset(plane[:].bitcast(I32), 0)
+        nc.vector.memset(s13[:].bitcast(I32), 0)
         make_identity(nc, ident[:])
 
         a1_sb, a3_sb, s_sb, w2_raw, dh, da_mx, g_pairs, turned_g = {}, {}, {}, {}, {}, {}, {}, {}
@@ -180,13 +175,16 @@ def tile_moe_bdx_glu_sigmoid_kernel(
                     w13[m][:, e0:e1, :].bitcast(I32), packed[e0:e1, 0, :, :].rearrange("e p b -> p e b").bitcast(I32)
                 )
 
-        def load_s13():
-            for plane, scales in zip(s13, (w1_scales, w3_scales)):
-                for quad in range(4):
-                    nc.gpsimd.dma_start(
-                        plane[32 * quad : 32 * quad + 4, :, :].bitcast(I32),
-                        scales[:, 0, 4 * quad : 4 * quad + 4, :].rearrange("e f n -> f e n").bitcast(I32),
-                    )
+        def load_s13(e0, e1):
+            for m, scales in enumerate((w1_scales, w3_scales)):
+                nc.sync.dma_start(
+                    s13[:16, e0:e1, m, :].bitcast(I32), scales[e0:e1, 0, :, :].rearrange("e f n -> f e n").bitcast(I32)
+                )
+
+        def spread_s13(e0, e1):
+            rows = s13[:, e0:e1, :, :].rearrange("p e m n -> p (e m n)").bitcast(I32)
+            for quad in range(1, 4):
+                nc.sync.dma_start(rows[32 * quad : 32 * quad + 4, :], rows[4 * quad : 4 * quad + 4, :])
 
         def load_s2(parts):
             for part in parts:
@@ -216,15 +214,10 @@ def tile_moe_bdx_glu_sigmoid_kernel(
         def turn_gate():
             bank = psum_back.tile([P, PACK, GROUP], F32, tag="dx", name="turn")
             nc.tensor.transpose(bank[:, 0, :], gate_rows[:], ident[:])
-            paired = SHARED[1:].count(2) * PACK
-            for j0, sign in ((0, -1.0), (2, 1.0)):
-                nc.scalar.activation(
-                    gate_cols[:, :paired].rearrange("p (k j) -> p k j", j=PACK)[:, :, j0 : j0 + 2],
-                    bank[:, 0, :paired].rearrange("p (k j) -> p k j", j=PACK)[:, :, j0 : j0 + 2],
-                    ACT.Copy,
-                    scale=sign,
-                )
-            nc.scalar.copy(gate_cols[:, paired:], bank[:, 0, paired:turned])
+            signs = [-1.0 if j < SHARED[k] else 1.0 for k in range(1, len(UNITS)) for j in range(groups(k))]
+            edges = [c for c in range(turned) if c == 0 or signs[c] != signs[c - 1]] + [turned]
+            for c0, c1 in zip(edges[:-1], edges[1:]):
+                nc.scalar.activation(gate_cols[:, c0:c1], bank[:, 0, c0:c1], ACT.Copy, scale=signs[c0])
 
         def gather(k, t):
             picked = dy[t][:].indirect(offs_sb[:, first[k] * C // 16 : (first[k] * C + width(k)) // 16])
@@ -282,11 +275,11 @@ def tile_moe_bdx_glu_sigmoid_kernel(
             nc.scalar.activation(s_sb[k][:], a1_sb[k][:, :, cut(k) :], ACT.Sigmoid)
 
         def square(k):
-            nc.scalar.activation(a1_sb[k][:, :, cut(k) :], s_sb[k][:], ACT.Square, bias=minus_half[:])
+            nc.scalar.activation(a1_sb[k][:, :, cut(k) :], s_sb[k][:], ACT.Square, bias=-0.5)
 
         def derivative(k):
             own = a1_sb[k][:, :, cut(k) :]
-            nc.scalar.activation(own, own, ACT.Identity, bias=quarter[:], scale=-1.0)
+            nc.scalar.activation(own, own, ACT.Copy, bias=0.25, scale=-1.0)
 
         def copy_dx(k):
             if k >= 0:
@@ -299,11 +292,13 @@ def tile_moe_bdx_glu_sigmoid_kernel(
         def scalar_step(k):
             if k <= 2:
                 round_da3(k)
+                if k == 2:
+                    copy_dx(0)
                 apply_gate(k + 2, 0)
                 turn_backs(k + 1)
-                if k > 0:
-                    sigmoid_minus(k + 2)
-                copy_dx(k - 1)
+                (sigmoid_minus if k > 0 else derivative)(k + 2)
+                if k == 2:
+                    copy_dx(1)
                 sigmoid_plus(k + 3)
                 apply_gate(k + 2, 1)
                 if k < 2:
@@ -386,9 +381,6 @@ def tile_moe_bdx_glu_sigmoid_kernel(
                         stop=True,
                     )
 
-        def halves(k):
-            return (1, 0) if SHARED[k] else (0, 1)
-
         def exact_da3(k, j):
             nc.vector.scalar_tensor_tensor(
                 da3_exact[k][:, j * BLOCK : (j + 1) * BLOCK],
@@ -410,7 +402,7 @@ def tile_moe_bdx_glu_sigmoid_kernel(
 
         def make_da(k):
             if SHARED[k]:
-                da3_exact[k] = turns.tile([P, 2 * BLOCK], F32, tag="exact%d" % (k % 2), name="da3_exact", align_bytes=64)
+                da3_exact[k] = turns.tile([P, PACK * cut(k)], F32, tag="exact%d" % (k % 2), name="da3_exact", align_bytes=64)
             for j in range(groups(k)):
                 if j < SHARED[k]:
                     exact_da3(k, j)
@@ -441,9 +433,7 @@ def tile_moe_bdx_glu_sigmoid_kernel(
             return da_mx[k][:, 8 * WIDE : 8 * WIDE + 2 * width(k)].rearrange("p (j m c) -> p j m c", m=2, c=GROUP)
 
         def quantize_da(k):
-            count = groups(k) // 2
-            for half in halves(k):
-                part = slice(half * count, (half + 1) * count)
+            for part in (slice(0, 1), slice(1, 2)) if k == last else (slice(0, groups(k)),):
                 nc.vector.quantize_mx(
                     out=da_codes(k)[:, part, :, :].rearrange("p j m c -> p (j m c)").bitcast(FP8X4),
                     scales=da_scales(k)[:, part, :, :].rearrange("p j m c -> p (j m c)"),
@@ -454,23 +444,21 @@ def tile_moe_bdx_glu_sigmoid_kernel(
             return turns.tile([P, size], U8, tag=tag, name=name, align_bytes=64)
 
         def second_product(k, j0, j1):
-            count = groups(k) // 2
             pool, tag = (psum_turn, "turn%d" % (2 * j0)) if k == last else (psum_back, "dx")
             dx_ps[k, j0] = pool.tile([P, (j1 - j0) * GROUP], F32, tag=tag, name="dx_ps")
-            for j in sorted(range(j0, j1), key=lambda g: halves(k).index(g // count)):
+            for j in range(j0, j1):
                 e = first[k] + j * GROUP // C
                 for m in range(2):
                     nc.tensor.matmul_mx(
                         out=dx_ps[k, j0][:, (j - j0) * GROUP : (j - j0 + 1) * GROUP],
                         lhsT=w13[m][:, e, :].bitcast(FP4X4),
-                        lhsT_scale=s13[m][:, e, :],
+                        lhsT_scale=s13[:, e, m, :],
                         rhs=da_codes(k)[:, j, m, :].bitcast(FP8X4),
                         rhs_scale=da_scales(k)[:, j, m, :],
                         start=(m == 0),
                         stop=(m == 1),
                     )
 
-        load_s13()
         load_dy(0)
         nc.sync.dma_start(offs_sb[:], offs)
         nc.sync.dma_start(gate_rows[:turned, :], gate[0, WIDE:].rearrange("(b s) -> b s", s=GROUP))
@@ -506,7 +494,7 @@ def tile_moe_bdx_glu_sigmoid_kernel(
         load_w2(2, UNITS[2])
         load_a1(3)
         load_a3(2)
-        unstack_s2(2)
+        load_s13(0, EARLY)
         for k, t in ((0, 2), (0, 3), (1, 2), (1, 3), (2, 3)):
             gather(k, t)
         round_first()
@@ -518,20 +506,21 @@ def tile_moe_bdx_glu_sigmoid_kernel(
         factor_u(0, 2, 4)
         factor_y(0)
         factor_u(0, 1, 2)
-        load_w13(0, EARLY)
-        load_w2(3, UNITS[3])
         load_a1(4)
+        load_w2(3, UNITS[3])
         load_a3(3)
+        unstack_s2(2)
+        load_w13(0, EARLY)
+        spread_s13(0, EARLY)
         for j in range(3):
             apply_gate(1, j)
         sigmoid_plus(2)
         apply_gate(1, 3)
         square(2)
         sigmoid_minus(2)
-        derivative(2)
 
         for k in range(len(UNITS)):
-            split = 2 if SHARED[k] else 0
+            split = (SHARED[k + 1] or 2) if SHARED[k] else 0
             if k < last and SHARED[k + 1]:
                 factor_y(k + 1)
             elif split:
@@ -549,7 +538,9 @@ def tile_moe_bdx_glu_sigmoid_kernel(
                 load_w2(k + 4, UNITS[k + 4])
                 load_a3(k + 4)
             if k == 0:
+                load_s13(EARLY, E)
                 load_w13(EARLY, E)
+                spread_s13(EARLY, E)
             if k + AHEAD <= last:
                 for t in (2, 3, 0, 1):
                     gather(k + AHEAD, t)
@@ -561,10 +552,10 @@ def tile_moe_bdx_glu_sigmoid_kernel(
                 quantize_g(k + 1)
                 first_product(k + 1)
             da_mx[k] = lodge("da_mx", "pairs%d" % ((k + 1) % 2), 10 * WIDE + 4 * H)
+            quantize_da(k)
             if k + 2 <= last:
                 w2_sb[k + 2] = da_mx[k][:, 10 * WIDE : 10 * WIDE + UNITS[k + 2] * 2 * H]
                 reorder_w2(k + 2, w2_sb[k + 2])
-            quantize_da(k)
             if k < last:
                 second_product(k, 0, groups(k))
             if k == 3:

@@ -24,20 +24,19 @@ MULT = mybir.AluOpType.mult
 ADD = mybir.AluOpType.add
 SUB = mybir.AluOpType.subtract
 
-UNITS = [2, 2, 2, 2, 2, 2, 2, 1]
-SHARED = [1, 2, 2, 2, 0, 0, 0, 0]
-AHEAD = 3
-RING = 4
-HOMES = 5
+UNITS = [1, 1, 2, 2, 2, 2, 2, 2, 1]
 WIDE = 2 * C
 SPAN = PACK * WIDE
-BLOCK = PACK * GROUP
-OUT_CUTS = [0, 640, 1280]
-LAST_CUTS = [0, 640, 1088, 1280]
+OUT_CUTS = (256, 640, 1024)
+SHARED = (3, 4, 5, 6)
 RUN = 4
 LINE = 8
-EARLY = 6
 LIVE = 100
+HOMES = 5
+LATE = 3
+A3_HOMES = 6
+DIRECT = 4
+LEVELS = (E - DIRECT + 1) // 2
 
 
 def planes_by_runs(ap):
@@ -45,19 +44,7 @@ def planes_by_runs(ap):
 
 
 def words_by_runs(ap):
-    return ap.rearrange("p (c i) t -> p c t i", i=RUN)
-
-
-def as_planes(ap):
-    return ap.rearrange("p (t s) -> p t s", t=PACK)
-
-
-def by_groups(ap):
-    return ap.rearrange("p (j t c) -> p j t c", t=PACK, c=GROUP)
-
-
-def as_words(ap):
-    return ap.rearrange("p (s t) -> p s t", t=PACK)
+    return ap.rearrange("p (c i t) -> p c t i", i=RUN, t=PACK)
 
 
 def tile_moe_bdx_glu_sigmoid_kernel(
@@ -66,514 +53,382 @@ def tile_moe_bdx_glu_sigmoid_kernel(
     nc = tc.nc
     first = [sum(UNITS[:k]) for k in range(len(UNITS))]
     last = len(UNITS) - 1
-    skipped = UNITS[0] * C // GROUP
-    turned = S // GROUP - skipped
 
     with ExitStack() as ctx:
         keep = ctx.enter_context(tc.tile_pool(name="keep", bufs=1))
-        turns = ctx.enter_context(tc.tile_pool(name="turns", bufs=1))
-        ring3 = ctx.enter_context(tc.tile_pool(name="ring3", bufs=3))
-        psum_dh = ctx.enter_context(tc.psum_pool(name="psum_dh", bufs=4))
-        psum_turn = ctx.enter_context(tc.psum_pool(name="psum_turn", bufs=1))
-        psum_back = ctx.enter_context(tc.psum_pool(name="psum_back", bufs=1))
+        psum = ctx.enter_context(tc.psum_pool(name="psum", bufs=1))
+
+        def homes(name, count, columns, dtype):
+            return [keep.tile([P, columns], dtype, name="%s%d" % (name, r), align_bytes=64) for r in range(count)]
+
+        home = homes("home", HOMES, SPAN, F32)
+        w2_home = homes("w2_home", 2, 4 * H, U8)
+        exact_home = homes("exact_home", 4, PACK * C, F32)
+        y_home = homes("y_home", 1, SPAN, F32)
+        dh_bank = [psum.tile([P, 2, C], F32, name="dh_bank%d" % r) for r in range(4)]
+        gate_bank = [psum.tile([P, WIDE], F32, name="gate_bank%d" % r) for r in range(2)]
+        dx_bank = [psum.tile([P, WIDE], F32, name="dx_bank%d" % r) for r in range(2)]
 
         offs_sb = keep.tile([P, S // 16], U16, name="offs_sb")
         pos_sb = [keep.tile([P, T // 16], U16, name="pos_sb%d" % r) for r in range(3)]
         dy = [keep.tile([P, T], F32, name="dy%d" % t) for t in range(PACK)]
         dx = keep.tile([P, S], F32, name="dx")
         stacked = keep.tile([P, 2, H], U8, name="stacked", align_bytes=64)
-        s2_all = keep.tile([P, E * H], U8, name="s2_all", align_bytes=64)
-        s2_first = keep.tile([P, 2, H], U8, name="s2_first", align_bytes=64)
+        s2_all = keep.tile([P, (E - DIRECT - 2) * H], U8, name="s2_all", align_bytes=64)
+        s2_raw = keep.tile([P, DIRECT, H], U8, name="s2_raw", align_bytes=64)
+        s2_head = keep.tile([P, DIRECT, H], U8, name="s2_head", align_bytes=64)
         w13 = [keep.tile([P, E, 2 * K], U8, name="w13_%d" % m, align_bytes=64) for m in range(2)]
         s13 = keep.tile([P, E, 2, K], U8, name="s13", align_bytes=64)
-        sm_home = [keep.tile([P, SPAN // 2], F32, name="sm_home%d" % r, align_bytes=64) for r in range(RING)]
-        home = [keep.tile([P, SPAN], F32, name="home%d" % r, align_bytes=64) for r in range(HOMES)]
-        head = dx[:, :SPAN]
         ident = keep.tile([P, P], F32, name="ident")
         gate_rows = keep.tile([P, GROUP], F32, name="gate_rows")
-        gate_cols = keep.tile([P, turned], F32, name="gate_cols")
+        gate_cols = keep.tile([P, S // GROUP], F32, name="gate_cols")
 
+        nc.vector.memset(s2_raw[:].rearrange("p e n -> p (e n)").bitcast(I32), 0)
         nc.vector.memset(gate_rows[:], 0.0)
-        nc.vector.memset(stacked[:, 1, :].bitcast(I32), 0)
-        nc.vector.memset(s2_all[96:, 2 * H :].bitcast(I32), 0)
+        nc.vector.memset(stacked[:].rearrange("p b n -> p (b n)").bitcast(I32), 0)
+        nc.vector.memset(s2_all[96:, :].bitcast(I32), 0)
         nc.vector.memset(s13[:].bitcast(I32), 0)
         make_identity(nc, ident[:])
 
-        a1_sb, a3_sb, s_sb, w2_raw, dh, da_mx, g_pairs, turned_g = {}, {}, {}, {}, {}, {}, {}, {}
-        w2_sb, g_codes, g_scales, dx_ps, da3_exact = {}, {}, {}, {}, {}
+        a1_sb, a3_sb, w2_raw, w2_sb, gate_ps, g_words, g_mx = {}, {}, {}, {}, {}, {}, {}
+        dh, da3_exact, da_words, da_mx, dx_ps, sm = {}, {}, {}, {}, {}, {}
+
+        levels = []
 
         def width(k):
             return UNITS[k] * C
 
-        def groups(k):
-            return width(k) // GROUP
-
         def slots(k):
             return slice(first[k] * C, (first[k] + UNITS[k]) * C)
 
-        def cut(k):
-            return SHARED[k] * GROUP
-
-        def sm_flat(k):
-            return (sm_home[k % RING][:, WIDE - 2 * cut(k) : WIDE + 2 * cut(k)])
-
-        def y_flat(k):
-            return home[(k - 2) % HOMES][:, SPAN - PACK * cut(k) :]
-
-        def u_group(k, j0, j1):
-            if k == 0:
-                if j0 >= 2:
-                    return as_planes(home[-2 % HOMES][:, : SPAN // 2])[:, :, (j0 - 2) * GROUP : (j1 - 2) * GROUP]
-                return as_planes(home[-2 % HOMES][:, 2 * BLOCK : 3 * BLOCK])
-            if SHARED[k - 1] and not SHARED[k]:
-                start = SPAN // 2 if j0 < 2 else 0
-                part = as_planes(home[(k - 2) % HOMES][:, start : start + SPAN // 2])
-                return part[:, :, j0 % 2 * GROUP : (j0 % 2 + j1 - j0) * GROUP]
-            planes = as_planes(home[(k - 2) % HOMES][:, : PACK * (width(k) - cut(k))])
-            return planes[:, :, j0 * GROUP - cut(k) : j1 * GROUP - cut(k)]
-
-        def da_words(k):
-            return home[k % HOMES][:, : PACK * width(k)].bitcast(BF16).rearrange("p (j m b) -> p j m b", m=2, b=BLOCK)
-
-        def gathered(k, t):
-            if k == 0 or (k, t) == (2, 2):
-                return head[:, t * WIDE : (t + 1) * WIDE]
-            if k < AHEAD:
-                return home[k][:, t * WIDE : (t + 1) * WIDE]
-            if k == last:
-                return home[(k - AHEAD - 2) % HOMES][:, t * width(k) : (t + 1) * width(k)]
-            if t < 2:
-                return sm_home[(k - AHEAD) % RING][:, WIDE + (t - 1) * width(k) : WIDE + t * width(k)]
-            return home[(k - AHEAD - 2) % HOMES][:, (t - 2) * width(k) : (t - 1) * width(k)]
-
-        gate_first = home[-2 % HOMES][:, :WIDE]
+        def planes(ring, k):
+            return ring[k % len(ring)][:, : PACK * width(k)].rearrange("p (t s) -> p t s", t=PACK)
 
         def load_dy(t):
             nc.sync.dma_start(dy[t][:], dyT.rearrange("(p t) c -> p t c", t=PACK)[:, t, :])
 
-        def load_a1(k):
-            a1_sb[k] = turns.tile([P, PACK, width(k)], F32, tag="a1_%d" % (k % RING), name="a1_sb", align_bytes=64)
-            nc.sync.dma_start(a1_sb[k][:], a1.rearrange("(p t) s -> p t s", t=PACK)[:, :, slots(k)])
+        def load_a1(k, t0=0, t1=PACK):
+            pair = dx[:, :SPAN] if k < 2 else home[first[k] // 2 % HOMES][:]
+            start = first[k] % 2 * PACK * C
+            a1_sb[k] = pair[:, start : start + PACK * width(k)].rearrange("p (t s) -> p t s", t=PACK)
+            nc.sync.dma_start(a1_sb[k][:, t0:t1, :], a1.rearrange("(p t) s -> p t s", t=PACK)[:, t0:t1, slots(k)])
 
         def load_a3(k):
-            a3_sb[k] = turns.tile([P, PACK, width(k)], F32, tag="a3_%d" % (k % RING), name="a3_sb")
+            a3_sb[k] = keep.tile([P, PACK, width(k)], F32, tag="a3_%d" % (k % A3_HOMES), name="a3_sb", align_bytes=64)
             nc.sync.dma_start(a3_sb[k][:], a3.rearrange("(p t) s -> p t s", t=PACK)[:, :, slots(k)])
 
-        def load_w2(k, count):
-            if k == 0:
-                w2_raw[k] = turns.tile([P, count, 2 * H], U8, tag="pairs1", name="w2_raw", align_bytes=64)
-            else:
-                w2_raw[k] = ring3.tile([P, count, 2 * H], U8, name="w2_raw", align_bytes=64)
-            nc.sync.dma_start(
-                w2_raw[k][:].bitcast(I32),
-                w2_words[first[k] : first[k] + count, 0, :, :].rearrange("e p b -> p e b").bitcast(I32),
-            )
+        def load_w2(e0, e1):
+            raw = keep.tile([P, e1 - e0, 2 * H], U8, name="w2_raw%d" % e0, align_bytes=64)
+            nc.sync.dma_start(raw[:].bitcast(I32), w2_words[e0:e1, 0, :, :].rearrange("e p b -> p e b").bitcast(I32))
+            for k in range(len(UNITS)):
+                if e0 <= first[k] < e1:
+                    w2_raw[k] = raw[:, first[k] - e0 : first[k] - e0 + UNITS[k], :]
 
-        def load_w13(e0, e1):
+        def load_w13():
             for m, packed in enumerate((w1_words, w3_words)):
-                nc.sync.dma_start(
-                    w13[m][:, e0:e1, :].bitcast(I32), packed[e0:e1, 0, :, :].rearrange("e p b -> p e b").bitcast(I32)
-                )
+                nc.sync.dma_start(w13[m][:].bitcast(I32), packed[:, 0, :, :].rearrange("e p b -> p e b").bitcast(I32))
 
-        def load_s13(e0, e1):
+        def load_s13():
             for m, scales in enumerate((w1_scales, w3_scales)):
                 nc.sync.dma_start(
-                    s13[:16, e0:e1, m, :].bitcast(I32), scales[e0:e1, 0, :, :].rearrange("e f n -> f e n").bitcast(I32)
+                    s13[:16, :, m, :].bitcast(I32), scales[:, 0, :, :].rearrange("e f n -> f e n").bitcast(I32)
                 )
 
-        def spread_s13(e0, e1):
-            rows = s13[:, e0:e1, :, :].rearrange("p e m n -> p (e m n)").bitcast(I32)
+        def spread_s13():
+            rows = s13[:].rearrange("p e m n -> p (e m n)").bitcast(I32)
             for quad in range(1, 4):
                 nc.sync.dma_start(rows[32 * quad : 32 * quad + 4, :], rows[4 * quad : 4 * quad + 4, :])
 
-        def load_s2(parts):
-            for part in parts:
-                quad, b = divmod(part, 2)
-                count = (E - b + 1) // 2
+        def load_s2_head():
+            for row in range(4):
                 nc.sync.dma_start(
-                    stacked[32 * quad : 32 * quad + 4 * count, b, :].bitcast(I32),
-                    w2_scales[b::2, 0, 4 * quad : 4 * quad + 4, :].bitcast(I32),
+                    s2_raw[row:P:32, :, :].bitcast(I32),
+                    w2_scales[:DIRECT, 0, row::4, :].rearrange("e q n -> q e n").bitcast(I32),
                 )
 
-        def reorder_s2():
+        def load_s2(quad):
+            for b in range(2):
+                count = (E - DIRECT - b + 1) // 2
+                nc.gpsimd.dma_start(
+                    stacked[32 * quad : 32 * quad + 4 * count, b, :].bitcast(I32),
+                    w2_scales[DIRECT + b :: 2, 0, 4 * quad : 4 * quad + 4, :].bitcast(I32),
+                )
+
+        def reorder_s2(target, source):
             nc.vector.tensor_copy(
-                s2_first[:].rearrange("p b (t m) -> p b t m", t=PACK),
-                stacked[:].rearrange("p b (m t) -> p b t m", t=PACK),
+                target[:].rearrange("p b (t m) -> p b t m", t=PACK), source[:].rearrange("p b (m t) -> p b t m", t=PACK)
             )
 
-        def s2_plane(k):
-            if k == 0:
-                return s2_first[:]
-            return s2_all[:, first[k] * H : (first[k] + UNITS[k]) * H].rearrange("p (e n) -> p e n", n=H)
+        def s2_plane(e):
+            if e < DIRECT:
+                return s2_head[:, e, :]
+            if e < DIRECT + 2:
+                return levels[0][:, e - DIRECT, :]
+            return s2_all[:, (e - DIRECT - 2) * H : (e - DIRECT - 1) * H]
 
-        def unstack_s2(k):
+        def unstack_s2(level):
+            count = min(2, E - DIRECT - 2 * level)
             nc.sync.dma_start(
-                s2_plane(k)[:LIVE].bitcast(I32), s2_first[4 * k : 4 * k + LIVE, : UNITS[k], :].bitcast(I32)
+                s2_all[:LIVE, (2 * level - 2) * H : (2 * level - 2 + count) * H].bitcast(I32),
+                levels[0][4 * level : 4 * level + LIVE, :count, :].rearrange("p b n -> p (b n)").bitcast(I32),
             )
 
         def turn_gate():
-            bank = psum_back.tile([P, PACK, GROUP], F32, tag="dx", name="turn")
-            nc.tensor.transpose(bank[:, 0, :], gate_rows[:], ident[:])
-            signs = [-1.0 if j < SHARED[k] else 1.0 for k in range(1, len(UNITS)) for j in range(groups(k))]
-            edges = [c for c in range(turned) if c == 0 or signs[c] != signs[c - 1]] + [turned]
-            for c0, c1 in zip(edges[:-1], edges[1:]):
-                nc.scalar.activation(gate_cols[:, c0:c1], bank[:, 0, c0:c1], ACT.Copy, scale=signs[c0])
+            nc.tensor.transpose(dx_bank[1][:, :GROUP], gate_rows[:], ident[:])
+            nc.scalar.activation(gate_cols[:], dx_bank[1][:, : S // GROUP], ACT.Copy, scale=-1.0)
 
-        def gather(k, t):
-            picked = dy[t][:].indirect(offs_sb[:, first[k] * C // 16 : (first[k] * C + width(k)) // 16])
-            if k == 0:
-                nc.vector.tensor_tensor(gathered(k, t), picked, gate_first, MULT)
-            else:
-                nc.vector.tensor_copy(gathered(k, t), picked)
-
-        def round_first():
-            g_pairs[0] = home[-2 % HOMES][:, SPAN // 2 :]
-            planes = as_planes(head[:, :SPAN])
-            rounded = as_words(g_pairs[0][:].bitcast(BF16))
-            for c0, c1, sign in ((0, cut(0), -1.0), (cut(0), WIDE, 1.0)):
-                nc.scalar.activation(
-                    words_by_runs(rounded[:, c0:c1, :]), planes_by_runs(planes[:, :, c0:c1]), ACT.Copy, scale=sign
+        def spread_gate(k):
+            gate_ps[k] = gate_bank[k % 2][:, : width(k)]
+            for j in range(width(k) // GROUP):
+                col = first[k] * C // GROUP + j
+                nc.tensor.transpose(
+                    gate_ps[k][:, j * GROUP : (j + 1) * GROUP], gate_cols[:, col : col + 1].to_broadcast([P, P]), ident[:]
                 )
 
-        def apply_gate(k, j):
-            bank = psum_turn.tile([P, PACK, GROUP], F32, tag="turn%d" % (j % 3), name="turn")
-            for t in range(PACK):
-                nc.tensor.transpose(bank[:, t, :], gathered(k, t)[:, j * GROUP : (j + 1) * GROUP], ident[:])
-            turned_g[k, j] = turns.tile([P, N], BF16, tag="turned%d" % j, name="turned_g", align_bytes=64)
-            col = first[k] * C // GROUP - skipped + j
-            nc.scalar.activation(
-                turned_g[k, j][:].rearrange("s (u p e) -> s u p e", u=2, e=2),
-                bank[:].rearrange("s (u e) p -> s u p e", e=2),
-                ACT.Copy,
-                scale=gate_cols[:, col : col + 1],
+        def picked(e0, e1):
+            pair = home[(e0 // 2 - 2) % HOMES][:].rearrange("p (t s) -> p t s", t=PACK)
+            return pair[:, :, e0 % 2 * C : (e0 % 2 + e1 - e0) * C]
+
+        def gather(e0, e1, t, on_vector):
+            window = dy[t][:].indirect(offs_sb[:, e0 * C // 16 : e1 * C // 16])
+            if on_vector:
+                nc.vector.tensor_copy(picked(e0, e1)[:, t, :], window)
+            else:
+                nc.scalar.activation(picked(e0, e1)[:, t, :], window, ACT.Copy)
+
+        def apply_gate(k):
+            if k == 1:
+                g_words[k] = keep.tile([P, PACK * width(k)], BF16, tag="levels", name="g_words", align_bytes=64)
+            else:
+                g_words[k] = (exact_home[2 * (k % 2)] if k else y_home[0])[:].bitcast(BF16)[:, : PACK * width(k)]
+            runs = width(k) // RUN
+            nc.vector.tensor_tensor(
+                words_by_runs(g_words[k][:]),
+                planes_by_runs(picked(first[k], first[k] + UNITS[k])),
+                gate_ps[k][:].rearrange("p (c i) -> p c i", i=RUN).unsqueeze(2).to_broadcast([P, runs, PACK, RUN]),
+                MULT,
             )
 
-        def turn_back(k, half):
-            if half == 0:
-                g_pairs[k] = turns.tile(
-                    [P, 2 * width(k)], F32, tag="pairs%d" % (k % 2), name="g_pairs", align_bytes=64
-                )
-            bank = psum_turn.tile([P, 2, 2, GROUP], F32, tag="turn%d" % (half + 1), name="back")
-            for jj in range(2):
-                for u in range(2):
-                    nc.tensor.transpose(
-                        bank[:, jj, u, :], turned_g[k, 2 * half + jj][:].bitcast(F32)[:, u * P : (u + 1) * P], ident[:]
-                    )
+        def sigmoid_minus(k, t0=0, t1=PACK):
+            if t0 == 0:
+                sm[k] = keep.tile([P, PACK, width(k)], F32, tag="sm%d" % (k % 2), name="sm", align_bytes=64)
+            nc.scalar.activation(sm[k][:, t0:t1, :], a1_sb[k][:, t0:t1, :], ACT.Sigmoid, scale=-1.0)
+
+        def factor_y(k, engine):
+            cut = 0 if k == last else PACK if k + 2 in SHARED else PACK - 1
+            part = slice(0, cut) if engine is nc.gpsimd else slice(cut, PACK)
+            if part.start < part.stop:
+                engine.tensor_tensor(planes(y_home, k)[:, part, :], a3_sb[k][:, part, :], sm[k][:, part, :], MULT)
+
+        def reorder_w2(k):
+            w2_sb[k] = w2_home[k % 2][:, : UNITS[k] * 2 * H]
             nc.scalar.copy(
-                g_pairs[k][:, half * BLOCK : (half + 1) * BLOCK].rearrange("p (j s u) -> p j s u", j=2, u=2),
-                bank[:].rearrange("p j u s -> p j s u"),
-            )
-
-        def sigmoid_minus(k):
-            if cut(k):
-                nc.scalar.activation(
-                    by_groups(sm_flat(k)), a1_sb[k][:, :, : cut(k)].rearrange("p t (j c) -> p j t c", c=GROUP), ACT.Sigmoid, scale=-1.0
-                )
-
-        def sigmoid_plus(k):
-            s_sb[k] = turns.tile([P, PACK, width(k) - cut(k)], F32, tag="s%d" % (k % RING), name="s", align_bytes=64)
-            nc.scalar.activation(s_sb[k][:], a1_sb[k][:, :, cut(k) :], ACT.Sigmoid)
-
-        def square(k):
-            nc.scalar.activation(a1_sb[k][:, :, cut(k) :], s_sb[k][:], ACT.Square, bias=-0.5)
-
-        def derivative(k):
-            own = a1_sb[k][:, :, cut(k) :]
-            nc.scalar.activation(own, own, ACT.Copy, bias=0.25, scale=-1.0)
-
-        def copy_dx(k):
-            if k >= 0:
-                nc.scalar.copy(dx[:, slots(k)], dx_ps[k, 0][:])
-
-        def turn_backs(k):
-            for half in range(groups(k) // 2):
-                turn_back(k, half)
-
-        def scalar_step(k):
-            if k <= 2:
-                round_da3(k)
-                if k == 2:
-                    copy_dx(0)
-                apply_gate(k + 2, 0)
-                turn_backs(k + 1)
-                (sigmoid_minus if k > 0 else derivative)(k + 2)
-                if k == 2:
-                    copy_dx(1)
-                sigmoid_plus(k + 3)
-                apply_gate(k + 2, 1)
-                if k < 2:
-                    square(k + 3)
-                apply_gate(k + 2, 2)
-                if k < 2:
-                    derivative(k + 3)
-                apply_gate(k + 2, 3)
-                if k == 2:
-                    square(k + 3)
-            elif k == 3:
-                apply_gate(k + 2, 0)
-                turn_backs(k + 1)
-                round_da3(k)
-                derivative(k + 2)
-                copy_dx(k - 1)
-                apply_gate(k + 2, 1)
-                apply_gate(k + 2, 2)
-                sigmoid_plus(k + 3)
-                apply_gate(k + 2, 3)
-                square(k + 3)
-            elif k == 4:
-                apply_gate(k + 2, 0)
-                turn_backs(k + 1)
-                round_da3(k)
-                derivative(k + 2)
-                copy_dx(k - 1)
-                for j in range(1, groups(k + 2)):
-                    apply_gate(k + 2, j)
-            elif k == 5:
-                sigmoid_plus(k + 2)
-                turn_backs(k + 1)
-                square(k + 2)
-                copy_dx(k - 1)
-                derivative(k + 2)
-                apply_gate(k + 2, 0)
-                apply_gate(k + 2, 1)
-            else:
-                copy_dx(k - 1)
-                if k < last:
-                    turn_backs(k + 1)
-
-        def factor_y(k):
-            if cut(k):
-                nc.gpsimd.tensor_tensor(
-                    by_groups(y_flat(k)),
-                    a3_sb[k][:, :, : cut(k)].rearrange("p t (j c) -> p j t c", c=GROUP),
-                    by_groups(sm_flat(k)),
-                    MULT,
-                )
-
-        def factor_u(k, j0, j1):
-            cols = slice(j0 * GROUP, j1 * GROUP)
-            nc.gpsimd.tensor_tensor(u_group(k, j0, j1), a1_sb[k][:, :, cols], a3_sb[k][:, :, cols], MULT)
-
-        def reorder_w2(k, target):
-            nc.vector.tensor_copy(
-                target.bitcast(U16).rearrange("p (e t c i) -> p e c t i", t=PACK, i=LINE, c=P // LINE),
+                w2_sb[k][:].bitcast(U16).rearrange("p (e t c i) -> p e c t i", t=PACK, i=LINE, c=P // LINE),
                 w2_raw[k][:].bitcast(U16).rearrange("p e (c i t) -> p e c t i", t=PACK, i=LINE),
             )
 
         def quantize_g(k):
+            g_mx[k] = keep.tile([P, 5 * width(k)], U8, tag="sm%d" % ((k - 1) % 2), name="g_mx", align_bytes=64)
             nc.vector.quantize_mx(
-                out=g_codes[k].bitcast(U32).bitcast(FP8X4), scales=g_scales[k], in_=g_pairs[k][:].bitcast(BF16)
+                out=g_mx[k][:, : 4 * width(k)].bitcast(U32).bitcast(FP8X4),
+                scales=g_mx[k][:, 4 * width(k) :],
+                in_=g_words[k][:],
             )
 
         def first_product(k):
-            for j in range(groups(k)):
-                e = j * GROUP // C
-                dh[k, j] = psum_dh.tile([P, PACK, GROUP], F32, name="dh")
-                for t in range(PACK):
-                    start = e * 2 * H + 2 * P * t
-                    nc.tensor.matmul_mx(
-                        out=dh[k, j][:, t, :],
-                        lhsT=w2_sb[k][:, start : start + 2 * P].bitcast(FP4X4),
-                        lhsT_scale=s2_plane(k)[:, e, P * t : P * (t + 1)],
-                        rhs=g_codes[k][:, j * BLOCK : (j + 1) * BLOCK].bitcast(U32).bitcast(FP8X4),
-                        rhs_scale=g_scales[k][:, j * GROUP : (j + 1) * GROUP],
-                        start=True,
-                        stop=True,
+            for j in range(UNITS[k]):
+                for half in range(2):
+                    dh[k, j, half] = dh_bank[(2 * (first[k] + j) + half) % 4]
+                    for u in range(2):
+                        t = 2 * half + u
+                        start = j * 2 * H + 2 * P * t
+                        nc.tensor.matmul_mx(
+                            out=dh[k, j, half][:, u, :],
+                            lhsT=w2_sb[k][:, start : start + 2 * P].bitcast(FP4X4),
+                            lhsT_scale=s2_plane(first[k] + j)[:, P * t : P * (t + 1)],
+                            rhs=g_mx[k][:, 4 * j * C : 4 * (j + 1) * C].bitcast(U32).bitcast(FP8X4),
+                            rhs_scale=g_mx[k][:, 4 * width(k) + j * C : 4 * width(k) + (j + 1) * C],
+                            start=True,
+                            stop=True,
+                        )
+
+        def exact_da3(k):
+            for j in range(UNITS[k]):
+                da3_exact[k, j] = exact_home[2 * (k % 2) + j][:].rearrange("p (t s) -> p t s", t=PACK)
+                for half in range(2):
+                    pair = slice(2 * half, 2 * half + 2)
+                    nc.vector.scalar_tensor_tensor(
+                        da3_exact[k, j][:, pair, :],
+                        sm[k][:, pair, j * C : (j + 1) * C],
+                        1.0,
+                        dh[k, j, half][:],
+                        SUB,
+                        MULT,
                     )
 
-        def exact_da3(k, j):
-            nc.vector.scalar_tensor_tensor(
-                da3_exact[k][:, j * BLOCK : (j + 1) * BLOCK],
-                sm_flat(k)[:, j * BLOCK : (j + 1) * BLOCK],
-                1.0,
-                dh[k, j][:].rearrange("p t c -> p (t c)"),
-                SUB,
-                MULT,
-            )
-
-        def product(k, j, m):
-            c0 = j * GROUP - cut(k)
-            nc.vector.tensor_tensor(
-                words_by_runs(as_words(da_words(k)[:, j, m, :])),
-                planes_by_runs(dh[k, j][:]),
-                planes_by_runs(s_sb[k][:, :, c0 : c0 + GROUP] if m else u_group(k, j, j + 1)),
-                MULT,
-            )
-
-        def make_da(k):
-            if SHARED[k]:
-                da3_exact[k] = turns.tile([P, PACK * cut(k)], F32, tag="exact%d" % (k % 2), name="da3_exact", align_bytes=64)
-            for j in range(groups(k)):
-                if j < SHARED[k]:
-                    exact_da3(k, j)
-                else:
-                    product(k, j, 1)
-                    product(k, j, 0)
-
         def round_da3(k):
-            if SHARED[k]:
+            for j in range(UNITS[k]):
                 nc.scalar.copy(
-                    da_words(k)[:, : SHARED[k], 1, :].rearrange("p j (c i t) -> p j c t i", t=PACK, i=RUN),
-                    da3_exact[k][:, : PACK * cut(k)].rearrange("p (j t c i) -> p j c t i", t=PACK, c=GROUP // RUN, i=RUN),
+                    words_by_runs(da_words[k][:, 1, PACK * j * C : PACK * (j + 1) * C]), planes_by_runs(da3_exact[k, j][:])
                 )
 
-        def finish_da1(k):
-            if SHARED[k]:
-                nc.gpsimd.tensor_tensor(
-                    da_words(k)[:, : SHARED[k], 0, :].rearrange("p j (c t) -> p j t c", t=PACK),
-                    by_groups(da3_exact[k][:, : PACK * cut(k)]),
-                    by_groups(y_flat(k)),
+        def make_da1(k):
+            for j in reversed(range(UNITS[k])):
+                nc.vector.tensor_tensor(
+                    words_by_runs(da_words[k][:, 0, PACK * j * C : PACK * (j + 1) * C]),
+                    planes_by_runs(da3_exact[k, j][:]),
+                    planes_by_runs(planes(y_home, k)[:, :, j * C : (j + 1) * C]),
                     MULT,
                 )
 
-        def da_codes(k):
-            return da_mx[k][:, : 8 * width(k)].bitcast(U32).rearrange("p (j m c) -> p j m c", m=2, c=GROUP)
-
-        def da_scales(k):
-            return da_mx[k][:, 8 * WIDE : 8 * WIDE + 2 * width(k)].rearrange("p (j m c) -> p j m c", m=2, c=GROUP)
-
         def quantize_da(k):
-            for part in (slice(0, 1), slice(1, 2)) if k == last else (slice(0, groups(k)),):
-                nc.vector.quantize_mx(
-                    out=da_codes(k)[:, part, :, :].rearrange("p j m c -> p (j m c)").bitcast(FP8X4),
-                    scales=da_scales(k)[:, part, :, :].rearrange("p j m c -> p (j m c)"),
-                    in_=da_words(k)[:, part, :, :].rearrange("p j m b -> p (j m b)"),
-                )
+            da_mx[k] = keep.tile([P, 10 * width(k)], U8, tag="a3_%d" % ((k + 1) % A3_HOMES), name="da_mx", align_bytes=64)
+            nc.vector.quantize_mx(
+                out=da_mx[k][:, : 8 * width(k)].bitcast(U32).bitcast(FP8X4),
+                scales=da_mx[k][:, 8 * width(k) :],
+                in_=da_words[k][:].rearrange("p m b -> p (m b)"),
+            )
 
-        def lodge(name, tag, size):
-            return turns.tile([P, size], U8, tag=tag, name=name, align_bytes=64)
-
-        def second_product(k, j0, j1):
-            pool, tag = (psum_turn, "turn%d" % (2 * j0)) if k == last else (psum_back, "dx")
-            dx_ps[k, j0] = pool.tile([P, (j1 - j0) * GROUP], F32, tag=tag, name="dx_ps")
-            for j in range(j0, j1):
-                e = first[k] + j * GROUP // C
+        def second_product(k):
+            dx_ps[k] = dx_bank[k % 2][:, : width(k)]
+            for j in range(UNITS[k]):
+                e = first[k] + j
                 for m in range(2):
+                    col = m * width(k) + j * C
                     nc.tensor.matmul_mx(
-                        out=dx_ps[k, j0][:, (j - j0) * GROUP : (j - j0 + 1) * GROUP],
+                        out=dx_ps[k][:, j * C : (j + 1) * C],
                         lhsT=w13[m][:, e, :].bitcast(FP4X4),
                         lhsT_scale=s13[:, e, m, :],
-                        rhs=da_codes(k)[:, j, m, :].bitcast(FP8X4),
-                        rhs_scale=da_scales(k)[:, j, m, :],
+                        rhs=da_mx[k][:, 4 * col : 4 * (col + C)].bitcast(U32).bitcast(FP8X4),
+                        rhs_scale=da_mx[k][:, 8 * width(k) + col : 8 * width(k) + col + C],
                         start=(m == 0),
                         stop=(m == 1),
                     )
 
+        def copy_dx(k):
+            if k == last:
+                nc.vector.tensor_copy(dx[:, slots(k)], dx_ps[k][:])
+            else:
+                nc.scalar.copy(dx[:, slots(k)], dx_ps[k][:])
+
+        load_a1(0, 0, 1)
         load_dy(0)
         nc.sync.dma_start(offs_sb[:], offs)
-        nc.sync.dma_start(gate_rows[:turned, :], gate[0, WIDE:].rearrange("(b s) -> b s", s=GROUP))
-        load_a1(0)
-        nc.sync.dma_start(gate_first, gate[:P, :WIDE])
+        load_s2_head()
         load_dy(1)
-        load_s2(range(4))
-        load_w2(0, UNITS[0] + UNITS[1])
-        load_a1(1)
-        load_s2(range(4, 8))
         load_dy(2)
+        nc.sync.dma_start(gate_rows[: S // GROUP, :], gate[0, :].rearrange("(b s) -> b s", s=GROUP))
+        load_w2(0, 1)
         load_dy(3)
+        load_a1(0, 1, PACK)
         load_a3(0)
-        load_a1(2)
+        load_w2(1, 4)
+        load_a1(1)
         load_a3(1)
-
-        turn_gate()
-        sigmoid_plus(0)
-        sigmoid_minus(0)
-        square(0)
-        derivative(0)
-        sigmoid_plus(1)
-        sigmoid_minus(1)
-        square(1)
-        derivative(1)
-        for k, t in ((1, 0), (2, 0), (0, 0), (0, 1), (1, 1), (2, 1)):
-            gather(k, t)
-        w2_head = lodge("w2_head", "pairs0", 8 * H)
-        w2_sb[0], w2_sb[1] = w2_head[:, : 4 * H], w2_head[:, 4 * H :]
-        reorder_w2(0, w2_head[:])
-        reorder_s2()
-        unstack_s2(1)
-        load_w2(2, UNITS[2])
-        load_a1(3)
+        load_a1(2)
         load_a3(2)
-        load_s13(0, EARLY)
-        for k, t in ((0, 2), (0, 3), (1, 2), (1, 3), (2, 3)):
-            gather(k, t)
-        round_first()
-        g_head = lodge("g_head", "s3", 5 * WIDE)
-        g_codes[0], g_scales[0] = g_head[:, : 4 * WIDE], g_head[:, 4 * WIDE :]
+        load_a1(3)
+        for quad in range(4):
+            load_s2(quad)
+
+        sigmoid_minus(0, 0, 1)
+        reorder_s2(s2_head, s2_raw)
+        gather(0, 2, 0, True)
+        gather(2, 4, 0, False)
+        gather(4, 6, 0, True)
+        gather(0, 2, 1, True)
+        gather(2, 4, 1, False)
+        turn_gate()
+        spread_gate(0)
+        spread_gate(1)
+        gather(4, 6, 1, False)
+        reorder_w2(0)
+        gather(0, 2, 2, True)
+        gather(2, 4, 2, False)
+        gather(4, 6, 2, False)
+        gather(0, 1, 3, True)
+        gather(1, 2, 3, True)
+        apply_gate(0)
         quantize_g(0)
         first_product(0)
-        gather(2, 2)
-        factor_u(0, 2, 4)
-        factor_y(0)
-        factor_u(0, 1, 2)
-        load_a1(4)
-        load_w2(3, UNITS[3])
-        load_a3(3)
-        unstack_s2(2)
-        load_w13(0, EARLY)
-        spread_s13(0, EARLY)
-        for j in range(3):
-            apply_gate(1, j)
-        sigmoid_plus(2)
-        apply_gate(1, 3)
-        square(2)
-        sigmoid_minus(2)
+        sigmoid_minus(0, 1, PACK)
+        factor_y(0, nc.gpsimd)
+        gather(2, 4, 3, False)
+        reorder_w2(1)
 
-        for k in range(len(UNITS)):
-            split = (SHARED[k + 1] or 2) if SHARED[k] else 0
-            if k < last and SHARED[k + 1]:
-                factor_y(k + 1)
-            elif split:
-                factor_u(k + 1, 0, split)
-            make_da(k)
-            finish_da1(k)
-            if k < last:
-                factor_u(k + 1, split, groups(k + 1))
-            scalar_step(k)
-            if k + 5 <= last:
-                load_a1(k + 5)
-            if k + 3 <= last:
-                unstack_s2(k + 3)
-            if k + 4 <= last:
-                load_w2(k + 4, UNITS[k + 4])
-                load_a3(k + 4)
-            if k == 0:
-                load_s13(EARLY, E)
-                load_w13(EARLY, E)
-                spread_s13(EARLY, E)
-            if k + AHEAD <= last:
-                for t in (2, 3, 0, 1):
-                    gather(k + AHEAD, t)
-            if k < last:
-                after_s = lodge("after_s", "s%d" % (k % RING), 5 * WIDE)
-                codes = lodge("codes", "exact%d" % (k % 2), 4 * WIDE) if SHARED[k] else after_s
-                g_codes[k + 1] = codes[:, : 4 * width(k + 1)]
-                g_scales[k + 1] = after_s[:, 4 * WIDE : 4 * WIDE + width(k + 1)]
+        for k in range(len(UNITS) + 1):
+            if k + 1 <= last:
+                sigmoid_minus(k + 1)
+                apply_gate(k + 1)
+            if 4 <= k + 3 <= last:
+                for t in range(PACK - (k + 3 in SHARED)):
+                    gather(first[k + 3], first[k + 3] + UNITS[k + 3], t, False)
+            if k + 2 <= last:
+                spread_gate(k + 2)
+            if k + 2 in SHARED:
+                gather(first[k + 2], first[k + 2] + UNITS[k + 2], PACK - 1, True)
+            if k <= last:
+                exact_da3(k)
+                da_words[k] = home[(k - 2) % HOMES][:].bitcast(BF16)[:, : 2 * PACK * width(k)].rearrange("p (m b) -> p m b", m=2)
+                round_da3(k)
+                factor_y(k, nc.vector)
+            if k + 1 <= last:
                 quantize_g(k + 1)
                 first_product(k + 1)
-            da_mx[k] = lodge("da_mx", "pairs%d" % ((k + 1) % 2), 10 * WIDE + 4 * H)
-            quantize_da(k)
-            if k + 2 <= last:
-                w2_sb[k + 2] = da_mx[k][:, 10 * WIDE : 10 * WIDE + UNITS[k + 2] * 2 * H]
-                reorder_w2(k + 2, w2_sb[k + 2])
-            if k < last:
-                second_product(k, 0, groups(k))
-            if k == 3:
+            if k == 0:
+                levels.append(keep.tile([P, 2, H], U8, tag="levels", name="s2_levels", align_bytes=64))
+                reorder_s2(levels[0], stacked)
+            if k >= 1:
+                quantize_da(k - 1)
+            if k > LATE:
+                second_product(k - 1)
+            if 1 <= k <= last - 3:
+                load_a1(k + 3)
+            if 1 <= k < LEVELS:
+                unstack_s2(k)
+            if k + 3 <= last:
+                if k % 2 == 0:
+                    load_w2(first[k + 3], min(first[k + 3] + 4, E))
+                load_a3(k + 3)
+            if k == LATE - 2:
+                load_s13()
+            if k == LATE - 1:
+                spread_s13()
+            if k == LATE:
+                load_w13()
+                for early in range(LATE):
+                    second_product(early)
+                    copy_dx(early)
+            if k == last - 3:
                 for r, pos in enumerate((pos1, pos2, pos3)):
                     nc.sync.dma_start(pos_sb[r][:], pos)
+            if k <= last:
+                make_da1(k)
+            if k + 2 <= last:
+                reorder_w2(k + 2)
+            if k + 1 <= last:
+                factor_y(k + 1, nc.gpsimd)
+            if k > LATE:
+                copy_dx(k - 1)
 
-        second_product(last, 0, 1)
-        nc.scalar.copy(dx[:, S - 2 * GROUP : S - GROUP], dx_ps[last, 0][:])
-        second_product(last, 1, 2)
-        nc.vector.tensor_copy(dx[:, S - GROUP :], dx_ps[last, 1][:])
+        def fetch(r, c0, c1):
+            return dx[:].indirect(pos_sb[r][:, c0 // 16 : c1 // 16])
 
-        for r in range(3):
-            cuts = LAST_CUTS if r == 2 else OUT_CUTS
-            for c0, c1 in zip(cuts[:-1], cuts[1:]):
-                picked = dx[:].indirect(pos_sb[r][:, c0 // 16 : c1 // 16])
-                if r == 0:
-                    nc.vector.tensor_copy(home[0][:, c0:c1], picked)
-                else:
-                    nc.vector.tensor_tensor(home[r][:, c0:c1], picked, home[r - 1][:, c0:c1], ADD)
-                if r == 2:
-                    nc.sync.dma_start(out[:, c0:c1], home[r][:, c0:c1])
+        one, two, three = home[2:]
+        total = y_home[0]
+        c1, c2, c3 = OUT_CUTS
+        nc.vector.tensor_copy(two[:, :c1], fetch(1, 0, c1))
+        for c0, c4 in ((0, c1), (c1, c2), (c2, T)):
+            nc.scalar.activation(one[:, c0:c4], fetch(0, c0, c4), ACT.Copy)
+        for c0, c4 in ((c2, c3), (c3, T)):
+            nc.scalar.activation(two[:, c0:c4], fetch(1, c0, c4), ACT.Copy)
+        nc.vector.tensor_tensor(three[:, :c1], fetch(2, 0, c1), two[:, :c1], ADD)
+        nc.vector.tensor_tensor(two[:, c1:c2], fetch(1, c1, c2), one[:, c1:c2], ADD)
+        nc.vector.tensor_tensor(total[:, :c1], three[:, :c1], one[:, :c1], ADD)
+        nc.sync.dma_start(out[:, :c1], total[:, :c1])
+        nc.vector.tensor_tensor(total[:, c1:c2], fetch(2, c1, c2), two[:, c1:c2], ADD)
+        nc.sync.dma_start(out[:, c1:c2], total[:, c1:c2])
+        nc.vector.tensor_tensor(three[:, c2:T], fetch(2, c2, T), one[:, c2:T], ADD)
+        for c0, c4 in ((c2, c3), (c3, T)):
+            nc.vector.tensor_tensor(total[:, c0:c4], three[:, c0:c4], two[:, c0:c4], ADD)
+            nc.sync.dma_start(out[:, c0:c4], total[:, c0:c4])

@@ -27,16 +27,17 @@ SUB = mybir.AluOpType.subtract
 UNITS = [1, 1, 2, 2, 2, 2, 2, 2, 1]
 WIDE = 2 * C
 SPAN = PACK * WIDE
-OUT_CUTS = (256, 640, 1024)
-SHARED = (3, 4, 5, 6)
+OUT_CUTS = (256, 576, 1024)
+SHARED = (3, 4, 5)
 RUN = 4
 LINE = 8
 LIVE = 100
 HOMES = 5
 LATE = 3
+LEAD = 7
+TURN = 8
 A3_HOMES = 6
-DIRECT = 4
-LEVELS = (E - DIRECT + 1) // 2
+LEVELS = (E + 1) // 2
 
 
 def planes_by_runs(ap):
@@ -63,8 +64,8 @@ def tile_moe_bdx_glu_sigmoid_kernel(
 
         home = homes("home", HOMES, SPAN, F32)
         w2_home = homes("w2_home", 2, 4 * H, U8)
-        exact_home = homes("exact_home", 4, PACK * C, F32)
-        y_home = homes("y_home", 1, SPAN, F32)
+        exact_home = homes("exact_home", 2, SPAN, F32)
+        y_home = homes("y_home", 2, SPAN, F32)
         dh_bank = [psum.tile([P, 2, C], F32, name="dh_bank%d" % r) for r in range(4)]
         gate_bank = [psum.tile([P, WIDE], F32, name="gate_bank%d" % r) for r in range(2)]
         dx_bank = [psum.tile([P, WIDE], F32, name="dx_bank%d" % r) for r in range(2)]
@@ -74,26 +75,22 @@ def tile_moe_bdx_glu_sigmoid_kernel(
         dy = [keep.tile([P, T], F32, name="dy%d" % t) for t in range(PACK)]
         dx = keep.tile([P, S], F32, name="dx")
         stacked = keep.tile([P, 2, H], U8, name="stacked", align_bytes=64)
-        s2_all = keep.tile([P, (E - DIRECT - 2) * H], U8, name="s2_all", align_bytes=64)
-        s2_raw = keep.tile([P, DIRECT, H], U8, name="s2_raw", align_bytes=64)
-        s2_head = keep.tile([P, DIRECT, H], U8, name="s2_head", align_bytes=64)
+        s2_levels = keep.tile([P, 2, H], U8, name="s2_levels", align_bytes=64)
+        s2_all = keep.tile([P, (E - 2) * H], U8, name="s2_all", align_bytes=64)
         w13 = [keep.tile([P, E, 2 * K], U8, name="w13_%d" % m, align_bytes=64) for m in range(2)]
         s13 = keep.tile([P, E, 2, K], U8, name="s13", align_bytes=64)
         ident = keep.tile([P, P], F32, name="ident")
         gate_rows = keep.tile([P, GROUP], F32, name="gate_rows")
         gate_cols = keep.tile([P, S // GROUP], F32, name="gate_cols")
 
-        nc.vector.memset(s2_raw[:].rearrange("p e n -> p (e n)").bitcast(I32), 0)
         nc.vector.memset(gate_rows[:], 0.0)
-        nc.vector.memset(stacked[:].rearrange("p b n -> p (b n)").bitcast(I32), 0)
+        nc.vector.memset(stacked[:, 1, :].bitcast(I32), 0)
         nc.vector.memset(s2_all[96:, :].bitcast(I32), 0)
         nc.vector.memset(s13[:].bitcast(I32), 0)
         make_identity(nc, ident[:])
 
         a1_sb, a3_sb, w2_raw, w2_sb, gate_ps, g_words, g_mx = {}, {}, {}, {}, {}, {}, {}
-        dh, da3_exact, da_words, da_mx, dx_ps, sm = {}, {}, {}, {}, {}, {}
-
-        levels = []
+        dh, da_words, da_mx, dx_ps, sm = {}, {}, {}, {}, {}
 
         def width(k):
             return UNITS[k] * C
@@ -124,9 +121,9 @@ def tile_moe_bdx_glu_sigmoid_kernel(
                 if e0 <= first[k] < e1:
                     w2_raw[k] = raw[:, first[k] - e0 : first[k] - e0 + UNITS[k], :]
 
-        def load_w13():
-            for m, packed in enumerate((w1_words, w3_words)):
-                nc.sync.dma_start(w13[m][:].bitcast(I32), packed[:, 0, :, :].rearrange("e p b -> p e b").bitcast(I32))
+        def load_w13(m):
+            packed = (w1_words, w3_words)[m]
+            nc.sync.dma_start(w13[m][:].bitcast(I32), packed[:, 0, :, :].rearrange("e p b -> p e b").bitcast(I32))
 
         def load_s13():
             for m, scales in enumerate((w1_scales, w3_scales)):
@@ -139,38 +136,30 @@ def tile_moe_bdx_glu_sigmoid_kernel(
             for quad in range(1, 4):
                 nc.sync.dma_start(rows[32 * quad : 32 * quad + 4, :], rows[4 * quad : 4 * quad + 4, :])
 
-        def load_s2_head():
-            for row in range(4):
+        def load_s2(b, quads):
+            count = (E - b + 1) // 2
+            for quad in quads:
                 nc.sync.dma_start(
-                    s2_raw[row:P:32, :, :].bitcast(I32),
-                    w2_scales[:DIRECT, 0, row::4, :].rearrange("e q n -> q e n").bitcast(I32),
-                )
-
-        def load_s2(quad):
-            for b in range(2):
-                count = (E - DIRECT - b + 1) // 2
-                nc.gpsimd.dma_start(
                     stacked[32 * quad : 32 * quad + 4 * count, b, :].bitcast(I32),
-                    w2_scales[DIRECT + b :: 2, 0, 4 * quad : 4 * quad + 4, :].bitcast(I32),
+                    w2_scales[b::2, 0, 4 * quad : 4 * quad + 4, :].bitcast(I32),
                 )
 
-        def reorder_s2(target, source):
+        def reorder_s2(b):
             nc.vector.tensor_copy(
-                target[:].rearrange("p b (t m) -> p b t m", t=PACK), source[:].rearrange("p b (m t) -> p b t m", t=PACK)
+                s2_levels[:, b, :].rearrange("p (t m) -> p t m", t=PACK),
+                stacked[:, b, :].rearrange("p (m t) -> p t m", t=PACK),
             )
 
         def s2_plane(e):
-            if e < DIRECT:
-                return s2_head[:, e, :]
-            if e < DIRECT + 2:
-                return levels[0][:, e - DIRECT, :]
-            return s2_all[:, (e - DIRECT - 2) * H : (e - DIRECT - 1) * H]
+            if e < 2:
+                return s2_levels[:, e, :]
+            return s2_all[:, (e - 2) * H : (e - 1) * H]
 
         def unstack_s2(level):
-            count = min(2, E - DIRECT - 2 * level)
+            count = min(2, E - 2 * level)
             nc.sync.dma_start(
                 s2_all[:LIVE, (2 * level - 2) * H : (2 * level - 2 + count) * H].bitcast(I32),
-                levels[0][4 * level : 4 * level + LIVE, :count, :].rearrange("p b n -> p (b n)").bitcast(I32),
+                s2_levels[4 * level : 4 * level + LIVE, :count, :].rearrange("p b n -> p (b n)").bitcast(I32),
             )
 
         def turn_gate():
@@ -186,7 +175,7 @@ def tile_moe_bdx_glu_sigmoid_kernel(
                 )
 
         def picked(e0, e1):
-            pair = home[(e0 // 2 - 2) % HOMES][:].rearrange("p (t s) -> p t s", t=PACK)
+            pair = (home[(e0 // 2 - 2) % HOMES] if e0 < first[LEAD] else exact_home[e0 // 2 % 2])[:].rearrange("p (t s) -> p t s", t=PACK)
             return pair[:, :, e0 % 2 * C : (e0 % 2 + e1 - e0) * C]
 
         def gather(e0, e1, t, on_vector):
@@ -197,10 +186,7 @@ def tile_moe_bdx_glu_sigmoid_kernel(
                 nc.scalar.activation(picked(e0, e1)[:, t, :], window, ACT.Copy)
 
         def apply_gate(k):
-            if k == 1:
-                g_words[k] = keep.tile([P, PACK * width(k)], BF16, tag="levels", name="g_words", align_bytes=64)
-            else:
-                g_words[k] = (exact_home[2 * (k % 2)] if k else y_home[0])[:].bitcast(BF16)[:, : PACK * width(k)]
+            g_words[k] = y_home[k % 2][:].bitcast(BF16)[:, : PACK * width(k)]
             runs = width(k) // RUN
             nc.vector.tensor_tensor(
                 words_by_runs(g_words[k][:]),
@@ -214,11 +200,11 @@ def tile_moe_bdx_glu_sigmoid_kernel(
                 sm[k] = keep.tile([P, PACK, width(k)], F32, tag="sm%d" % (k % 2), name="sm", align_bytes=64)
             nc.scalar.activation(sm[k][:, t0:t1, :], a1_sb[k][:, t0:t1, :], ACT.Sigmoid, scale=-1.0)
 
-        def factor_y(k, engine):
-            cut = 0 if k == last else PACK if k + 2 in SHARED else PACK - 1
-            part = slice(0, cut) if engine is nc.gpsimd else slice(cut, PACK)
-            if part.start < part.stop:
-                engine.tensor_tensor(planes(y_home, k)[:, part, :], a3_sb[k][:, part, :], sm[k][:, part, :], MULT)
+        def y_planes(k):
+            return planes(y_home, k) if k < last else planes(y_home[1:], k)
+
+        def factor_y(k, engine, t0, t1):
+            engine.tensor_tensor(y_planes(k)[:, t0:t1, :], a3_sb[k][:, t0:t1, :], sm[k][:, t0:t1, :], MULT)
 
         def reorder_w2(k):
             w2_sb[k] = w2_home[k % 2][:, : UNITS[k] * 2 * H]
@@ -254,32 +240,22 @@ def tile_moe_bdx_glu_sigmoid_kernel(
 
         def exact_da3(k):
             for j in range(UNITS[k]):
-                da3_exact[k, j] = exact_home[2 * (k % 2) + j][:].rearrange("p (t s) -> p t s", t=PACK)
                 for half in range(2):
-                    pair = slice(2 * half, 2 * half + 2)
+                    part = (slice(None), slice(2 * half, 2 * half + 2), slice(j * C, (j + 1) * C))
                     nc.vector.scalar_tensor_tensor(
-                        da3_exact[k, j][:, pair, :],
-                        sm[k][:, pair, j * C : (j + 1) * C],
-                        1.0,
-                        dh[k, j, half][:],
-                        SUB,
-                        MULT,
+                        planes(exact_home, k)[part], sm[k][part], 1.0, dh[k, j, half][:], SUB, MULT
                     )
 
         def round_da3(k):
-            for j in range(UNITS[k]):
-                nc.scalar.copy(
-                    words_by_runs(da_words[k][:, 1, PACK * j * C : PACK * (j + 1) * C]), planes_by_runs(da3_exact[k, j][:])
-                )
+            nc.scalar.copy(words_by_runs(da_words[k][:, 1, :]), planes_by_runs(planes(exact_home, k)))
 
         def make_da1(k):
-            for j in reversed(range(UNITS[k])):
-                nc.vector.tensor_tensor(
-                    words_by_runs(da_words[k][:, 0, PACK * j * C : PACK * (j + 1) * C]),
-                    planes_by_runs(da3_exact[k, j][:]),
-                    planes_by_runs(planes(y_home, k)[:, :, j * C : (j + 1) * C]),
-                    MULT,
-                )
+            nc.vector.tensor_tensor(
+                words_by_runs(da_words[k][:, 0, :]),
+                planes_by_runs(planes(exact_home, k)),
+                planes_by_runs(y_planes(k)),
+                MULT,
+            )
 
         def quantize_da(k):
             da_mx[k] = keep.tile([P, 10 * width(k)], U8, tag="a3_%d" % ((k + 1) % A3_HOMES), name="da_mx", align_bytes=64)
@@ -305,8 +281,8 @@ def tile_moe_bdx_glu_sigmoid_kernel(
                         stop=(m == 1),
                     )
 
-        def copy_dx(k):
-            if k == last:
+        def copy_dx(k, engine):
+            if engine is nc.vector:
                 nc.vector.tensor_copy(dx[:, slots(k)], dx_ps[k][:])
             else:
                 nc.scalar.copy(dx[:, slots(k)], dx_ps[k][:])
@@ -314,25 +290,23 @@ def tile_moe_bdx_glu_sigmoid_kernel(
         load_a1(0, 0, 1)
         load_dy(0)
         nc.sync.dma_start(offs_sb[:], offs)
-        load_s2_head()
+        load_s2(0, range(4))
         load_dy(1)
-        load_dy(2)
         nc.sync.dma_start(gate_rows[: S // GROUP, :], gate[0, :].rearrange("(b s) -> b s", s=GROUP))
+        load_dy(2)
         load_w2(0, 1)
         load_dy(3)
         load_a1(0, 1, PACK)
+        load_s2(1, range(2))
         load_a3(0)
+        load_s2(1, range(2, 4))
         load_w2(1, 4)
         load_a1(1)
         load_a3(1)
         load_a1(2)
         load_a3(2)
-        load_a1(3)
-        for quad in range(4):
-            load_s2(quad)
 
         sigmoid_minus(0, 0, 1)
-        reorder_s2(s2_head, s2_raw)
         gather(0, 2, 0, True)
         gather(2, 4, 0, False)
         gather(4, 6, 0, True)
@@ -346,13 +320,19 @@ def tile_moe_bdx_glu_sigmoid_kernel(
         gather(0, 2, 2, True)
         gather(2, 4, 2, False)
         gather(4, 6, 2, False)
+        reorder_s2(0)
         gather(0, 1, 3, True)
         gather(1, 2, 3, True)
         apply_gate(0)
+        gather(4, 5, 3, True)
+        gather(5, 6, 3, True)
         quantize_g(0)
         first_product(0)
+        reorder_s2(1)
+        unstack_s2(1)
+        load_a1(3)
         sigmoid_minus(0, 1, PACK)
-        factor_y(0, nc.gpsimd)
+        factor_y(0, nc.gpsimd, 0, PACK)
         gather(2, 4, 3, False)
         reorder_w2(1)
 
@@ -360,56 +340,62 @@ def tile_moe_bdx_glu_sigmoid_kernel(
             if k + 1 <= last:
                 sigmoid_minus(k + 1)
                 apply_gate(k + 1)
-            if 4 <= k + 3 <= last:
+            if 4 <= k + 3 < LEAD:
                 for t in range(PACK - (k + 3 in SHARED)):
                     gather(first[k + 3], first[k + 3] + UNITS[k + 3], t, False)
             if k + 2 <= last:
                 spread_gate(k + 2)
-            if k + 2 in SHARED:
+            if k + 2 in SHARED[1:]:
                 gather(first[k + 2], first[k + 2] + UNITS[k + 2], PACK - 1, True)
+            if TURN <= k <= last:
+                copy_dx(k - 2, nc.vector if k < last else nc.scalar)
             if k <= last:
                 exact_da3(k)
                 da_words[k] = home[(k - 2) % HOMES][:].bitcast(BF16)[:, : 2 * PACK * width(k)].rearrange("p (m b) -> p m b", m=2)
                 round_da3(k)
-                factor_y(k, nc.vector)
-            if k + 1 <= last:
-                quantize_g(k + 1)
-                first_product(k + 1)
-            if k == 0:
-                levels.append(keep.tile([P, 2, H], U8, tag="levels", name="s2_levels", align_bytes=64))
-                reorder_s2(levels[0], stacked)
             if k >= 1:
                 quantize_da(k - 1)
             if k > LATE:
                 second_product(k - 1)
             if 1 <= k <= last - 3:
                 load_a1(k + 3)
-            if 1 <= k < LEVELS:
-                unstack_s2(k)
+            if k + 2 < LEVELS:
+                unstack_s2(k + 2)
             if k + 3 <= last:
                 if k % 2 == 0:
                     load_w2(first[k + 3], min(first[k + 3] + 4, E))
                 load_a3(k + 3)
             if k == LATE - 2:
                 load_s13()
+                load_w13(0)
             if k == LATE - 1:
                 spread_s13()
             if k == LATE:
-                load_w13()
+                load_w13(1)
                 for early in range(LATE):
                     second_product(early)
-                    copy_dx(early)
+                    copy_dx(early, nc.scalar)
             if k == last - 3:
                 for r, pos in enumerate((pos1, pos2, pos3)):
                     nc.sync.dma_start(pos_sb[r][:], pos)
+            if k + 2 == last:
+                factor_y(k + 1, nc.vector, PACK - 1, PACK)
             if k <= last:
                 make_da1(k)
+            if k + 1 <= last:
+                quantize_g(k + 1)
+                first_product(k + 1)
+            if LEAD <= k + 3 <= last:
+                for t in range(PACK - (k + 3 in SHARED)):
+                    gather(first[k + 3], first[k + 3] + UNITS[k + 3], t, False)
             if k + 2 <= last:
                 reorder_w2(k + 2)
             if k + 1 <= last:
-                factor_y(k + 1, nc.gpsimd)
-            if k > LATE:
-                copy_dx(k - 1)
+                factor_y(k + 1, nc.gpsimd if k + 1 < last else nc.vector, 0, PACK - (k + 2 == last))
+            if LATE < k < TURN - 1 or k == last:
+                copy_dx(k - 1, nc.scalar)
+            if k > last:
+                copy_dx(k - 1, nc.vector)
 
         def fetch(r, c0, c1):
             return dx[:].indirect(pos_sb[r][:, c0 // 16 : c1 // 16])
@@ -418,17 +404,17 @@ def tile_moe_bdx_glu_sigmoid_kernel(
         total = y_home[0]
         c1, c2, c3 = OUT_CUTS
         nc.vector.tensor_copy(two[:, :c1], fetch(1, 0, c1))
-        for c0, c4 in ((0, c1), (c1, c2), (c2, T)):
+        for c0, c4 in ((c1, c2), (0, c1), (c2, c3), (c3, T)):
             nc.scalar.activation(one[:, c0:c4], fetch(0, c0, c4), ACT.Copy)
         for c0, c4 in ((c2, c3), (c3, T)):
             nc.scalar.activation(two[:, c0:c4], fetch(1, c0, c4), ACT.Copy)
         nc.vector.tensor_tensor(three[:, :c1], fetch(2, 0, c1), two[:, :c1], ADD)
         nc.vector.tensor_tensor(two[:, c1:c2], fetch(1, c1, c2), one[:, c1:c2], ADD)
         nc.vector.tensor_tensor(total[:, :c1], three[:, :c1], one[:, :c1], ADD)
-        nc.sync.dma_start(out[:, :c1], total[:, :c1])
         nc.vector.tensor_tensor(total[:, c1:c2], fetch(2, c1, c2), two[:, c1:c2], ADD)
-        nc.sync.dma_start(out[:, c1:c2], total[:, c1:c2])
-        nc.vector.tensor_tensor(three[:, c2:T], fetch(2, c2, T), one[:, c2:T], ADD)
+        nc.sync.dma_start(out[:, :c2], total[:, :c2])
+        for c0, c4 in ((c2, c3), (c3, T)):
+            nc.vector.tensor_tensor(three[:, c0:c4], fetch(2, c0, c4), one[:, c0:c4], ADD)
         for c0, c4 in ((c2, c3), (c3, T)):
             nc.vector.tensor_tensor(total[:, c0:c4], three[:, c0:c4], two[:, c0:c4], ADD)
             nc.sync.dma_start(out[:, c0:c4], total[:, c0:c4])

@@ -28,15 +28,14 @@ UNITS = [1, 1, 2, 2, 2, 2, 2, 2, 1]
 WIDE = 2 * C
 SPAN = PACK * WIDE
 OUT_CUTS = (256, 576, 1024)
-SHARED = (3, 4, 5)
+SHARED = {4: 1, 5: 1, 8: 2}
 RUN = 4
 LINE = 8
 LIVE = 100
 HOMES = 5
 LATE = 3
 LEAD = 7
-TURN = 8
-A3_HOMES = 6
+A3_HOMES = 7
 LEVELS = (E + 1) // 2
 
 
@@ -64,7 +63,7 @@ def tile_moe_bdx_glu_sigmoid_kernel(
 
         home = homes("home", HOMES, SPAN, F32)
         w2_home = homes("w2_home", 2, 4 * H, U8)
-        exact_home = homes("exact_home", 2, SPAN, F32)
+        exact_home = homes("exact_home", 3, SPAN, F32)
         y_home = homes("y_home", 2, SPAN, F32)
         dh_bank = [psum.tile([P, 2, C], F32, name="dh_bank%d" % r) for r in range(4)]
         gate_bank = [psum.tile([P, WIDE], F32, name="gate_bank%d" % r) for r in range(2)]
@@ -127,14 +126,14 @@ def tile_moe_bdx_glu_sigmoid_kernel(
 
         def load_s13():
             for m, scales in enumerate((w1_scales, w3_scales)):
-                nc.sync.dma_start(
+                nc.gpsimd.dma_start(
                     s13[:16, :, m, :].bitcast(I32), scales[:, 0, :, :].rearrange("e f n -> f e n").bitcast(I32)
                 )
 
         def spread_s13():
             rows = s13[:].rearrange("p e m n -> p (e m n)").bitcast(I32)
             for quad in range(1, 4):
-                nc.sync.dma_start(rows[32 * quad : 32 * quad + 4, :], rows[4 * quad : 4 * quad + 4, :])
+                nc.gpsimd.dma_start(rows[32 * quad : 32 * quad + 4, :], rows[4 * quad : 4 * quad + 4, :])
 
         def load_s2(b, quads):
             count = (E - b + 1) // 2
@@ -175,7 +174,7 @@ def tile_moe_bdx_glu_sigmoid_kernel(
                 )
 
         def picked(e0, e1):
-            pair = (home[(e0 // 2 - 2) % HOMES] if e0 < first[LEAD] else exact_home[e0 // 2 % 2])[:].rearrange("p (t s) -> p t s", t=PACK)
+            pair = (home[(e0 // 2 - 2) % HOMES] if e0 < first[LEAD] else exact_home[(e0 // 2 - 2) % 3])[:].rearrange("p (t s) -> p t s", t=PACK)
             return pair[:, :, e0 % 2 * C : (e0 % 2 + e1 - e0) * C]
 
         def gather(e0, e1, t, on_vector):
@@ -203,8 +202,8 @@ def tile_moe_bdx_glu_sigmoid_kernel(
         def y_planes(k):
             return planes(y_home, k) if k < last else planes(y_home[1:], k)
 
-        def factor_y(k, engine, t0, t1):
-            engine.tensor_tensor(y_planes(k)[:, t0:t1, :], a3_sb[k][:, t0:t1, :], sm[k][:, t0:t1, :], MULT)
+        def factor_y(k, engine):
+            engine.tensor_tensor(y_planes(k), a3_sb[k][:], sm[k][:], MULT)
 
         def reorder_w2(k):
             w2_sb[k] = w2_home[k % 2][:, : UNITS[k] * 2 * H]
@@ -306,6 +305,8 @@ def tile_moe_bdx_glu_sigmoid_kernel(
         load_a1(2)
         load_a3(2)
 
+        load_s13()
+        spread_s13()
         sigmoid_minus(0, 0, 1)
         gather(0, 2, 0, True)
         gather(2, 4, 0, False)
@@ -332,27 +333,33 @@ def tile_moe_bdx_glu_sigmoid_kernel(
         unstack_s2(1)
         load_a1(3)
         sigmoid_minus(0, 1, PACK)
-        factor_y(0, nc.gpsimd, 0, PACK)
+        factor_y(0, nc.gpsimd)
         gather(2, 4, 3, False)
         reorder_w2(1)
+
+        def gather_planes(k, on_vector):
+            cut = PACK - SHARED.get(k, 0)
+            for t in range(cut, PACK) if on_vector else range(cut):
+                gather(first[k], first[k] + UNITS[k], t, on_vector)
 
         for k in range(len(UNITS) + 1):
             if k + 1 <= last:
                 sigmoid_minus(k + 1)
-                apply_gate(k + 1)
             if 4 <= k + 3 < LEAD:
-                for t in range(PACK - (k + 3 in SHARED)):
-                    gather(first[k + 3], first[k + 3] + UNITS[k + 3], t, False)
-            if k + 2 <= last:
-                spread_gate(k + 2)
-            if k + 2 in SHARED[1:]:
-                gather(first[k + 2], first[k + 2] + UNITS[k + 2], PACK - 1, True)
-            if TURN <= k <= last:
-                copy_dx(k - 2, nc.vector if k < last else nc.scalar)
+                gather_planes(k + 3, False)
+            if 4 <= k + 1 <= last:
+                gather_planes(k + 1, True)
             if k <= last:
                 exact_da3(k)
                 da_words[k] = home[(k - 2) % HOMES][:].bitcast(BF16)[:, : 2 * PACK * width(k)].rearrange("p (m b) -> p m b", m=2)
+            if k + 1 <= last:
+                apply_gate(k + 1)
+            if k + 2 <= last:
+                spread_gate(k + 2)
+            if k <= last:
                 round_da3(k)
+            if k == last:
+                factor_y(k, nc.vector)
             if k >= 1:
                 quantize_da(k - 1)
             if k > LATE:
@@ -365,11 +372,8 @@ def tile_moe_bdx_glu_sigmoid_kernel(
                 if k % 2 == 0:
                     load_w2(first[k + 3], min(first[k + 3] + 4, E))
                 load_a3(k + 3)
-            if k == LATE - 2:
-                load_s13()
-                load_w13(0)
             if k == LATE - 1:
-                spread_s13()
+                load_w13(0)
             if k == LATE:
                 load_w13(1)
                 for early in range(LATE):
@@ -378,24 +382,19 @@ def tile_moe_bdx_glu_sigmoid_kernel(
             if k == last - 3:
                 for r, pos in enumerate((pos1, pos2, pos3)):
                     nc.sync.dma_start(pos_sb[r][:], pos)
-            if k + 2 == last:
-                factor_y(k + 1, nc.vector, PACK - 1, PACK)
-            if k <= last:
-                make_da1(k)
             if k + 1 <= last:
                 quantize_g(k + 1)
                 first_product(k + 1)
+            if k + 1 < last:
+                factor_y(k + 1, nc.gpsimd)
+            if k <= last:
+                make_da1(k)
             if LEAD <= k + 3 <= last:
-                for t in range(PACK - (k + 3 in SHARED)):
-                    gather(first[k + 3], first[k + 3] + UNITS[k + 3], t, False)
+                gather_planes(k + 3, False)
             if k + 2 <= last:
                 reorder_w2(k + 2)
-            if k + 1 <= last:
-                factor_y(k + 1, nc.gpsimd if k + 1 < last else nc.vector, 0, PACK - (k + 2 == last))
-            if LATE < k < TURN - 1 or k == last:
-                copy_dx(k - 1, nc.scalar)
-            if k > last:
-                copy_dx(k - 1, nc.vector)
+            if k > LATE:
+                copy_dx(k - 1, nc.scalar if k <= last else nc.vector)
 
         def fetch(r, c0, c1):
             return dx[:].indirect(pos_sb[r][:, c0 // 16 : c1 // 16])

@@ -28,12 +28,15 @@ UNITS = [1, 1, 2, 2, 2, 2, 2, 2, 1]
 WIDE = 2 * C
 SPAN = PACK * WIDE
 OUT_CUTS = (256, 576, 1024)
-SHARED = {4: 1, 5: 1, 8: 2}
+SHARED = {4: 1, 5: 1, 8: 1}
+SPLIT = (3, 5, 6, 7)
+G_START = 1536
 RUN = 4
 LINE = 8
 LIVE = 100
 HOMES = 5
-LATE = 3
+LATE = 2
+EARLY = 8
 LEAD = 7
 A3_HOMES = 7
 LEVELS = (E + 1) // 2
@@ -64,10 +67,10 @@ def tile_moe_bdx_glu_sigmoid_kernel(
         home = homes("home", HOMES, SPAN, F32)
         w2_home = homes("w2_home", 2, 4 * H, U8)
         exact_home = homes("exact_home", 3, SPAN, F32)
-        y_home = homes("y_home", 2, SPAN, F32)
+        y_home = keep.tile([P, 2 * SPAN], F32, name="y_home", align_bytes=64)
         dh_bank = [psum.tile([P, 2, C], F32, name="dh_bank%d" % r) for r in range(4)]
-        gate_bank = [psum.tile([P, WIDE], F32, name="gate_bank%d" % r) for r in range(2)]
-        dx_bank = [psum.tile([P, WIDE], F32, name="dx_bank%d" % r) for r in range(2)]
+        gate_bank = psum.tile([P, WIDE], F32, name="gate_bank")
+        dx_bank = [psum.tile([P, WIDE], F32, name="dx_bank%d" % r) for r in range(3)]
 
         offs_sb = keep.tile([P, S // 16], U16, name="offs_sb")
         pos_sb = [keep.tile([P, T // 16], U16, name="pos_sb%d" % r) for r in range(3)]
@@ -89,7 +92,7 @@ def tile_moe_bdx_glu_sigmoid_kernel(
         make_identity(nc, ident[:])
 
         a1_sb, a3_sb, w2_raw, w2_sb, gate_ps, g_words, g_mx = {}, {}, {}, {}, {}, {}, {}
-        dh, da_words, da_mx, dx_ps, sm = {}, {}, {}, {}, {}
+        dh, da_words, da_mx, dx_ps, sm, a3_rest = {}, {}, {}, {}, {}, {}
 
         def width(k):
             return UNITS[k] * C
@@ -109,9 +112,16 @@ def tile_moe_bdx_glu_sigmoid_kernel(
             a1_sb[k] = pair[:, start : start + PACK * width(k)].rearrange("p (t s) -> p t s", t=PACK)
             nc.sync.dma_start(a1_sb[k][:, t0:t1, :], a1.rearrange("(p t) s -> p t s", t=PACK)[:, t0:t1, slots(k)])
 
+        def y_cut(k):
+            return PACK - 1 if k in SPLIT else PACK
+
         def load_a3(k):
-            a3_sb[k] = keep.tile([P, PACK, width(k)], F32, tag="a3_%d" % (k % A3_HOMES), name="a3_sb", align_bytes=64)
-            nc.sync.dma_start(a3_sb[k][:], a3.rearrange("(p t) s -> p t s", t=PACK)[:, :, slots(k)])
+            rows = a3.rearrange("(p t) s -> p t s", t=PACK)[:, :, slots(k)]
+            a3_sb[k] = keep.tile([P, y_cut(k), width(k)], F32, tag="a3_%d" % (k % A3_HOMES), name="a3_sb", align_bytes=64)
+            nc.sync.dma_start(a3_sb[k][:], rows[:, : y_cut(k), :])
+            if k in SPLIT:
+                a3_rest[k] = keep.tile([P, 1, width(k)], F32, name="a3_rest%d" % k, align_bytes=64)
+                nc.sync.dma_start(a3_rest[k][:], rows[:, y_cut(k) :, :])
 
         def load_w2(e0, e1):
             raw = keep.tile([P, e1 - e0, 2 * H], U8, name="w2_raw%d" % e0, align_bytes=64)
@@ -120,9 +130,11 @@ def tile_moe_bdx_glu_sigmoid_kernel(
                 if e0 <= first[k] < e1:
                     w2_raw[k] = raw[:, first[k] - e0 : first[k] - e0 + UNITS[k], :]
 
-        def load_w13(m):
-            packed = (w1_words, w3_words)[m]
-            nc.sync.dma_start(w13[m][:].bitcast(I32), packed[:, 0, :, :].rearrange("e p b -> p e b").bitcast(I32))
+        def load_w13(e0, e1):
+            for m, packed in enumerate((w1_words, w3_words)):
+                nc.sync.dma_start(
+                    w13[m][:, e0:e1, :].bitcast(I32), packed[e0:e1, 0, :, :].rearrange("e p b -> p e b").bitcast(I32)
+                )
 
         def load_s13():
             for m, scales in enumerate((w1_scales, w3_scales)):
@@ -166,7 +178,7 @@ def tile_moe_bdx_glu_sigmoid_kernel(
             nc.scalar.activation(gate_cols[:], dx_bank[1][:, : S // GROUP], ACT.Copy, scale=-1.0)
 
         def spread_gate(k):
-            gate_ps[k] = gate_bank[k % 2][:, : width(k)]
+            gate_ps[k] = gate_bank[:, first[k] % 2 * C : first[k] % 2 * C + width(k)]
             for j in range(width(k) // GROUP):
                 col = first[k] * C // GROUP + j
                 nc.tensor.transpose(
@@ -185,7 +197,8 @@ def tile_moe_bdx_glu_sigmoid_kernel(
                 nc.scalar.activation(picked(e0, e1)[:, t, :], window, ACT.Copy)
 
         def apply_gate(k):
-            g_words[k] = y_home[k % 2][:].bitcast(BF16)[:, : PACK * width(k)]
+            start = 2 * SPAN - WIDE * (1 - k) if k < 2 else k % 2 * 2 * SPAN + G_START
+            g_words[k] = y_home[:].bitcast(BF16)[:, start : start + PACK * width(k)]
             runs = width(k) // RUN
             nc.vector.tensor_tensor(
                 words_by_runs(g_words[k][:]),
@@ -200,10 +213,14 @@ def tile_moe_bdx_glu_sigmoid_kernel(
             nc.scalar.activation(sm[k][:, t0:t1, :], a1_sb[k][:, t0:t1, :], ACT.Sigmoid, scale=-1.0)
 
         def y_planes(k):
-            return planes(y_home, k) if k < last else planes(y_home[1:], k)
+            start = {0: SPAN // 2, last: SPAN}.get(k, k % 2 * SPAN)
+            return y_home[:, start : start + PACK * width(k)].rearrange("p (t s) -> p t s", t=PACK)
 
         def factor_y(k, engine):
-            engine.tensor_tensor(y_planes(k), a3_sb[k][:], sm[k][:], MULT)
+            engine.tensor_tensor(y_planes(k)[:, : y_cut(k), :], a3_sb[k][:], sm[k][:, : y_cut(k), :], MULT)
+
+        def finish_y(k):
+            nc.vector.tensor_tensor(y_planes(k)[:, y_cut(k) :, :], a3_rest[k][:], sm[k][:, y_cut(k) :, :], MULT)
 
         def reorder_w2(k):
             w2_sb[k] = w2_home[k % 2][:, : UNITS[k] * 2 * H]
@@ -257,18 +274,19 @@ def tile_moe_bdx_glu_sigmoid_kernel(
             )
 
         def quantize_da(k):
-            da_mx[k] = keep.tile([P, 10 * width(k)], U8, tag="a3_%d" % ((k + 1) % A3_HOMES), name="da_mx", align_bytes=64)
-            nc.vector.quantize_mx(
-                out=da_mx[k][:, : 8 * width(k)].bitcast(U32).bitcast(FP8X4),
-                scales=da_mx[k][:, 8 * width(k) :],
-                in_=da_words[k][:].rearrange("p m b -> p (m b)"),
-            )
+            da_mx[k] = keep.tile([P, 10 * width(k)], U8, tag="a3_%d" % ((k + 1 + (k + 1 >= last)) % A3_HOMES), name="da_mx", align_bytes=64)
+            for m0, m1 in ((1, 2), (0, 1)) if k == last else ((0, 2),):
+                nc.vector.quantize_mx(
+                    out=da_mx[k][:, 4 * m0 * width(k) : 4 * m1 * width(k)].bitcast(U32).bitcast(FP8X4),
+                    scales=da_mx[k][:, (8 + m0) * width(k) : (8 + m1) * width(k)],
+                    in_=da_words[k][:, m0:m1, :].rearrange("p m b -> p (m b)"),
+                )
 
         def second_product(k):
-            dx_ps[k] = dx_bank[k % 2][:, : width(k)]
+            dx_ps[k] = dx_bank[first[k] // 2 % 3][:, first[k] % 2 * C : first[k] % 2 * C + width(k)]
             for j in range(UNITS[k]):
                 e = first[k] + j
-                for m in range(2):
+                for m in (1, 0):
                     col = m * width(k) + j * C
                     nc.tensor.matmul_mx(
                         out=dx_ps[k][:, j * C : (j + 1) * C],
@@ -276,8 +294,8 @@ def tile_moe_bdx_glu_sigmoid_kernel(
                         lhsT_scale=s13[:, e, m, :],
                         rhs=da_mx[k][:, 4 * col : 4 * (col + C)].bitcast(U32).bitcast(FP8X4),
                         rhs_scale=da_mx[k][:, 8 * width(k) + col : 8 * width(k) + col + C],
-                        start=(m == 0),
-                        stop=(m == 1),
+                        start=(m == 1),
+                        stop=(m == 0),
                     )
 
         def copy_dx(k, engine):
@@ -287,10 +305,10 @@ def tile_moe_bdx_glu_sigmoid_kernel(
                 nc.scalar.copy(dx[:, slots(k)], dx_ps[k][:])
 
         load_a1(0, 0, 1)
-        load_dy(0)
         nc.sync.dma_start(offs_sb[:], offs)
-        load_s2(0, range(4))
+        load_dy(0)
         load_dy(1)
+        load_s2(0, range(4))
         nc.sync.dma_start(gate_rows[: S // GROUP, :], gate[0, :].rearrange("(b s) -> b s", s=GROUP))
         load_dy(2)
         load_w2(0, 1)
@@ -298,9 +316,9 @@ def tile_moe_bdx_glu_sigmoid_kernel(
         load_a1(0, 1, PACK)
         load_s2(1, range(2))
         load_a3(0)
+        load_a1(1)
         load_s2(1, range(2, 4))
         load_w2(1, 4)
-        load_a1(1)
         load_a3(1)
         load_a1(2)
         load_a3(2)
@@ -325,17 +343,15 @@ def tile_moe_bdx_glu_sigmoid_kernel(
         gather(0, 1, 3, True)
         gather(1, 2, 3, True)
         apply_gate(0)
-        gather(4, 5, 3, True)
-        gather(5, 6, 3, True)
         quantize_g(0)
         first_product(0)
         reorder_s2(1)
         unstack_s2(1)
         load_a1(3)
         sigmoid_minus(0, 1, PACK)
-        factor_y(0, nc.gpsimd)
         gather(2, 4, 3, False)
         reorder_w2(1)
+        gather(4, 6, 3, False)
 
         def gather_planes(k, on_vector):
             cut = PACK - SHARED.get(k, 0)
@@ -358,8 +374,10 @@ def tile_moe_bdx_glu_sigmoid_kernel(
                 spread_gate(k + 2)
             if k <= last:
                 round_da3(k)
-            if k == last:
+            if k in (0, last):
                 factor_y(k, nc.vector)
+            if k in SPLIT:
+                finish_y(k)
             if k >= 1:
                 quantize_da(k - 1)
             if k > LATE:
@@ -372,13 +390,13 @@ def tile_moe_bdx_glu_sigmoid_kernel(
                 if k % 2 == 0:
                     load_w2(first[k + 3], min(first[k + 3] + 4, E))
                 load_a3(k + 3)
-            if k == LATE - 1:
-                load_w13(0)
+            if k == LATE + 1:
+                load_w13(EARLY, E)
             if k == LATE:
-                load_w13(1)
+                load_w13(0, EARLY)
                 for early in range(LATE):
                     second_product(early)
-                    copy_dx(early, nc.scalar)
+                nc.scalar.copy(dx[:, :WIDE], dx_bank[0][:])
             if k == last - 3:
                 for r, pos in enumerate((pos1, pos2, pos3)):
                     nc.sync.dma_start(pos_sb[r][:], pos)
@@ -400,7 +418,7 @@ def tile_moe_bdx_glu_sigmoid_kernel(
             return dx[:].indirect(pos_sb[r][:, c0 // 16 : c1 // 16])
 
         one, two, three = home[2:]
-        total = y_home[0]
+        total = y_home
         c1, c2, c3 = OUT_CUTS
         nc.vector.tensor_copy(two[:, :c1], fetch(1, 0, c1))
         for c0, c4 in ((c1, c2), (0, c1), (c2, c3), (c3, T)):

@@ -28,15 +28,15 @@ UNITS = [1, 1, 2, 2, 2, 2, 2, 2, 1]
 WIDE = 2 * C
 SPAN = PACK * WIDE
 OUT_CUTS = (256, 576, 1024)
-SHARED = {4: 1, 5: 1, 8: 1}
-SPLIT = (3, 5, 6, 7)
+SHARED = {4: 1, 5: 1, 6: 1, 7: 1}
+SPLIT = (7,)
 G_START = 1536
 RUN = 4
 LINE = 8
 LIVE = 100
 HOMES = 5
-LATE = 2
-EARLY = 8
+LATE = 1
+EARLY = 6
 LEAD = 7
 A3_HOMES = 7
 LEVELS = (E + 1) // 2
@@ -69,8 +69,7 @@ def tile_moe_bdx_glu_sigmoid_kernel(
         exact_home = homes("exact_home", 3, SPAN, F32)
         y_home = keep.tile([P, 2 * SPAN], F32, name="y_home", align_bytes=64)
         dh_bank = [psum.tile([P, 2, C], F32, name="dh_bank%d" % r) for r in range(4)]
-        gate_bank = psum.tile([P, WIDE], F32, name="gate_bank")
-        dx_bank = [psum.tile([P, WIDE], F32, name="dx_bank%d" % r) for r in range(3)]
+        bank = [psum.tile([P, WIDE], F32, name="bank%d" % r) for r in range(4)]
 
         offs_sb = keep.tile([P, S // 16], U16, name="offs_sb")
         pos_sb = [keep.tile([P, T // 16], U16, name="pos_sb%d" % r) for r in range(3)]
@@ -174,11 +173,11 @@ def tile_moe_bdx_glu_sigmoid_kernel(
             )
 
         def turn_gate():
-            nc.tensor.transpose(dx_bank[1][:, :GROUP], gate_rows[:], ident[:])
-            nc.scalar.activation(gate_cols[:], dx_bank[1][:, : S // GROUP], ACT.Copy, scale=-1.0)
+            nc.tensor.transpose(bank[3][:, :GROUP], gate_rows[:], ident[:])
+            nc.scalar.activation(gate_cols[:], bank[3][:, : S // GROUP], ACT.Copy, scale=-1.0)
 
         def spread_gate(k):
-            gate_ps[k] = gate_bank[:, first[k] % 2 * C : first[k] % 2 * C + width(k)]
+            gate_ps[k] = bank[k % 4][:, : width(k)]
             for j in range(width(k) // GROUP):
                 col = first[k] * C // GROUP + j
                 nc.tensor.transpose(
@@ -213,8 +212,8 @@ def tile_moe_bdx_glu_sigmoid_kernel(
             nc.scalar.activation(sm[k][:, t0:t1, :], a1_sb[k][:, t0:t1, :], ACT.Sigmoid, scale=-1.0)
 
         def y_planes(k):
-            start = {0: SPAN // 2, last: SPAN}.get(k, k % 2 * SPAN)
-            return y_home[:, start : start + PACK * width(k)].rearrange("p (t s) -> p t s", t=PACK)
+            start = {0: SPAN // 2, last: 0}.get(k, k % 2 * SPAN)
+            return (y_home if k < last else exact_home[0])[:, start : start + PACK * width(k)].rearrange("p (t s) -> p t s", t=PACK)
 
         def factor_y(k, engine):
             engine.tensor_tensor(y_planes(k)[:, : y_cut(k), :], a3_sb[k][:], sm[k][:, : y_cut(k), :], MULT)
@@ -283,7 +282,7 @@ def tile_moe_bdx_glu_sigmoid_kernel(
                 )
 
         def second_product(k):
-            dx_ps[k] = dx_bank[first[k] // 2 % 3][:, first[k] % 2 * C : first[k] % 2 * C + width(k)]
+            dx_ps[k] = bank[(k + 3) % 4][:, : width(k)]
             for j in range(UNITS[k]):
                 e = first[k] + j
                 for m in (1, 0):
@@ -363,24 +362,29 @@ def tile_moe_bdx_glu_sigmoid_kernel(
                 sigmoid_minus(k + 1)
             if 4 <= k + 3 < LEAD:
                 gather_planes(k + 3, False)
-            if 4 <= k + 1 <= last:
-                gather_planes(k + 1, True)
+            if k + 1 <= last:
+                apply_gate(k + 1)
+            if 2 <= k < last:
+                second_product(k - 2)
+                copy_dx(k - 2, nc.scalar)
+            if k + 2 <= last:
+                spread_gate(k + 2)
+            if 4 <= k + 2 <= last:
+                gather_planes(k + 2, True)
+            if k == last:
+                factor_y(k, nc.vector)
             if k <= last:
                 exact_da3(k)
                 da_words[k] = home[(k - 2) % HOMES][:].bitcast(BF16)[:, : 2 * PACK * width(k)].rearrange("p (m b) -> p m b", m=2)
-            if k + 1 <= last:
-                apply_gate(k + 1)
-            if k + 2 <= last:
-                spread_gate(k + 2)
             if k <= last:
                 round_da3(k)
-            if k in (0, last):
+            if k == 0:
                 factor_y(k, nc.vector)
             if k in SPLIT:
                 finish_y(k)
             if k >= 1:
                 quantize_da(k - 1)
-            if k > LATE:
+            if k >= last - 1:
                 second_product(k - 1)
             if 1 <= k <= last - 3:
                 load_a1(k + 3)
@@ -390,13 +394,10 @@ def tile_moe_bdx_glu_sigmoid_kernel(
                 if k % 2 == 0:
                     load_w2(first[k + 3], min(first[k + 3] + 4, E))
                 load_a3(k + 3)
-            if k == LATE + 1:
+            if k == LATE + 2:
                 load_w13(EARLY, E)
             if k == LATE:
                 load_w13(0, EARLY)
-                for early in range(LATE):
-                    second_product(early)
-                nc.scalar.copy(dx[:, :WIDE], dx_bank[0][:])
             if k == last - 3:
                 for r, pos in enumerate((pos1, pos2, pos3)):
                     nc.sync.dma_start(pos_sb[r][:], pos)
@@ -411,7 +412,7 @@ def tile_moe_bdx_glu_sigmoid_kernel(
                 gather_planes(k + 3, False)
             if k + 2 <= last:
                 reorder_w2(k + 2)
-            if k > LATE:
+            if k >= last - 1:
                 copy_dx(k - 1, nc.scalar if k <= last else nc.vector)
 
         def fetch(r, c0, c1):

@@ -28,7 +28,6 @@ UNITS = [1, 1, 2, 2, 2, 2, 2, 2, 1]
 WIDE = 2 * C
 SPAN = PACK * WIDE
 OUT_CUTS = (256, 576, 1024)
-SHARED = {4: 1, 5: 1, 6: 1, 7: 1}
 SPLIT = (7,)
 G_START = 1536
 RUN = 4
@@ -223,7 +222,7 @@ def tile_moe_bdx_glu_sigmoid_kernel(
 
         def reorder_w2(k):
             w2_sb[k] = w2_home[k % 2][:, : UNITS[k] * 2 * H]
-            nc.scalar.copy(
+            nc.vector.tensor_copy(
                 w2_sb[k][:].bitcast(U16).rearrange("p (e t c i) -> p e c t i", t=PACK, i=LINE, c=P // LINE),
                 w2_raw[k][:].bitcast(U16).rearrange("p e (c i t) -> p e c t i", t=PACK, i=LINE),
             )
@@ -320,6 +319,7 @@ def tile_moe_bdx_glu_sigmoid_kernel(
         load_w2(1, 4)
         load_a3(1)
         load_a1(2)
+        load_w2(first[3], first[5])
         load_a3(2)
 
         load_s13()
@@ -344,24 +344,23 @@ def tile_moe_bdx_glu_sigmoid_kernel(
         apply_gate(0)
         quantize_g(0)
         first_product(0)
+        reorder_w2(1)
         reorder_s2(1)
         unstack_s2(1)
         load_a1(3)
         sigmoid_minus(0, 1, PACK)
         gather(2, 4, 3, False)
-        reorder_w2(1)
         gather(4, 6, 3, False)
 
-        def gather_planes(k, on_vector):
-            cut = PACK - SHARED.get(k, 0)
-            for t in range(cut, PACK) if on_vector else range(cut):
-                gather(first[k], first[k] + UNITS[k], t, on_vector)
+        def gather_planes(k):
+            for t in range(PACK):
+                gather(first[k], first[k] + UNITS[k], t, False)
 
         for k in range(len(UNITS) + 1):
             if k + 1 <= last:
                 sigmoid_minus(k + 1)
             if 4 <= k + 3 < LEAD:
-                gather_planes(k + 3, False)
+                gather_planes(k + 3)
             if k + 1 <= last:
                 apply_gate(k + 1)
             if 2 <= k < last:
@@ -369,8 +368,6 @@ def tile_moe_bdx_glu_sigmoid_kernel(
                 copy_dx(k - 2, nc.scalar)
             if k + 2 <= last:
                 spread_gate(k + 2)
-            if 4 <= k + 2 <= last:
-                gather_planes(k + 2, True)
             if k == last:
                 factor_y(k, nc.vector)
             if k <= last:
@@ -391,9 +388,9 @@ def tile_moe_bdx_glu_sigmoid_kernel(
             if k + 2 < LEVELS:
                 unstack_s2(k + 2)
             if k + 3 <= last:
-                if k % 2 == 0:
-                    load_w2(first[k + 3], min(first[k + 3] + 4, E))
                 load_a3(k + 3)
+                if k in (1, 3):
+                    load_w2(first[k + 4], min(first[k + 4] + 4, E))
             if k == LATE + 2:
                 load_w13(EARLY, E)
             if k == LATE:
@@ -401,6 +398,8 @@ def tile_moe_bdx_glu_sigmoid_kernel(
             if k == last - 3:
                 for r, pos in enumerate((pos1, pos2, pos3)):
                     nc.sync.dma_start(pos_sb[r][:], pos)
+            if k + 2 <= last:
+                reorder_w2(k + 2)
             if k + 1 <= last:
                 quantize_g(k + 1)
                 first_product(k + 1)
@@ -409,9 +408,7 @@ def tile_moe_bdx_glu_sigmoid_kernel(
             if k <= last:
                 make_da1(k)
             if LEAD <= k + 3 <= last:
-                gather_planes(k + 3, False)
-            if k + 2 <= last:
-                reorder_w2(k + 2)
+                gather_planes(k + 3)
             if k >= last - 1:
                 copy_dx(k - 1, nc.scalar if k <= last else nc.vector)
 

@@ -37,6 +37,7 @@ HOMES = 5
 LATE = 1
 EARLY = 6
 LEAD = 7
+W2_TURN = LEAD - 1
 A3_HOMES = 7
 LEVELS = (E + 1) // 2
 
@@ -222,7 +223,8 @@ def tile_moe_bdx_glu_sigmoid_kernel(
 
         def reorder_w2(k):
             w2_sb[k] = w2_home[k % 2][:, : UNITS[k] * 2 * H]
-            nc.vector.tensor_copy(
+            copy = nc.vector.tensor_copy if k < W2_TURN else nc.scalar.copy
+            copy(
                 w2_sb[k][:].bitcast(U16).rearrange("p (e t c i) -> p e c t i", t=PACK, i=LINE, c=P // LINE),
                 w2_raw[k][:].bitcast(U16).rearrange("p e (c i t) -> p e c t i", t=PACK, i=LINE),
             )
@@ -398,7 +400,7 @@ def tile_moe_bdx_glu_sigmoid_kernel(
             if k == last - 3:
                 for r, pos in enumerate((pos1, pos2, pos3)):
                     nc.sync.dma_start(pos_sb[r][:], pos)
-            if k + 2 <= last:
+            if k + 2 < W2_TURN:
                 reorder_w2(k + 2)
             if k + 1 <= last:
                 quantize_g(k + 1)
@@ -409,6 +411,8 @@ def tile_moe_bdx_glu_sigmoid_kernel(
                 make_da1(k)
             if LEAD <= k + 3 <= last:
                 gather_planes(k + 3)
+            if W2_TURN <= k + 2 <= last:
+                reorder_w2(k + 2)
             if k >= last - 1:
                 copy_dx(k - 1, nc.scalar if k <= last else nc.vector)
 

@@ -8,6 +8,7 @@ S = E * C
 P = 128
 PACK = 4
 GROUP = 128
+BANK = 512
 FLOPS = 2 * S * (N * H + 2 * H * K)
 BYTES = 4 * (N * T + 2 * H * S + S + K * T) + E * (N * H + 2 * H * K) * 17 // 32 + 2 * P * (S + 3 * T) // 16
 
@@ -24,21 +25,22 @@ MULT = mybir.AluOpType.mult
 ADD = mybir.AluOpType.add
 SUB = mybir.AluOpType.subtract
 
-UNITS = [1, 1, 2, 2, 2, 2, 2, 2, 1]
+UNITS = [1, 2, 2, 2, 2, 2, 2, 1, 1]
 WIDE = 2 * C
 SPAN = PACK * WIDE
-OUT_CUTS = (256, 576, 1024)
-SPLIT = (7,)
-G_START = 1536
+OUT_CUTS = (256, 448, 960)
 RUN = 4
 LINE = 8
 LIVE = 100
-HOMES = 5
-LATE = 1
-EARLY = 6
-LEAD = 7
-W2_TURN = LEAD - 1
-A3_HOMES = 7
+LAG = 3
+AHEAD = 3
+HEAD = 3
+HOMES = 4
+WORDS_AT = 4 * SPAN
+W2_AT = WORDS_AT + 2 * SPAN
+ROOM = W2_AT + 4 * H
+A1_AT = ROOM - 4 * SPAN
+PACKED = 5 * WIDE
 LEVELS = (E + 1) // 2
 
 
@@ -56,20 +58,22 @@ def tile_moe_bdx_glu_sigmoid_kernel(
     nc = tc.nc
     first = [sum(UNITS[:k]) for k in range(len(UNITS))]
     last = len(UNITS) - 1
+    late = last - 1
 
     with ExitStack() as ctx:
         keep = ctx.enter_context(tc.tile_pool(name="keep", bufs=1))
+        rooms = ctx.enter_context(tc.tile_pool(name="rooms", bufs=1))
         psum = ctx.enter_context(tc.psum_pool(name="psum", bufs=1))
 
-        def homes(name, count, columns, dtype):
+        def ring(name, count, columns, dtype):
             return [keep.tile([P, columns], dtype, name="%s%d" % (name, r), align_bytes=64) for r in range(count)]
 
-        home = homes("home", HOMES, SPAN, F32)
-        w2_home = homes("w2_home", 2, 4 * H, U8)
-        exact_home = homes("exact_home", 3, SPAN, F32)
-        y_home = keep.tile([P, 2 * SPAN], F32, name="y_home", align_bytes=64)
-        dh_bank = [psum.tile([P, 2, C], F32, name="dh_bank%d" % r) for r in range(4)]
-        bank = [psum.tile([P, WIDE], F32, name="bank%d" % r) for r in range(4)]
+        y_ring = ring("y", 2, SPAN, F32)
+        exact_ring = ring("exact", LAG + 1, SPAN, F32)
+        word_ring = ring("words", LAG, SPAN, BF16)
+        dh_bank = [psum.tile([P, BANK], F32, name="dh_bank%d" % r) for r in range(4)]
+        gate_bank = [psum.tile([P, BANK], F32, name="gate_bank%d" % r) for r in range(2)]
+        dx_bank = [psum.tile([P, BANK], F32, name="dx_bank%d" % r) for r in range(2)]
 
         offs_sb = keep.tile([P, S // 16], U16, name="offs_sb")
         pos_sb = [keep.tile([P, T // 16], U16, name="pos_sb%d" % r) for r in range(3)]
@@ -86,69 +90,93 @@ def tile_moe_bdx_glu_sigmoid_kernel(
 
         nc.vector.memset(gate_rows[:], 0.0)
         nc.vector.memset(stacked[:, 1, :].bitcast(I32), 0)
-        nc.vector.memset(s2_all[96:, :].bitcast(I32), 0)
-        nc.vector.memset(s13[:].bitcast(I32), 0)
         make_identity(nc, ident[:])
+        nc.gpsimd.memset(s2_all[96:, :].bitcast(I32), 0)
+        nc.gpsimd.memset(s13[:].bitcast(I32), 0)
 
-        a1_sb, a3_sb, w2_raw, w2_sb, gate_ps, g_words, g_mx = {}, {}, {}, {}, {}, {}, {}
-        dh, da_words, da_mx, dx_ps, sm, a3_rest = {}, {}, {}, {}, {}, {}
+        w2_raw, da_mx, tenants = {}, {}, {}
 
         def width(k):
             return UNITS[k] * C
 
+        def span(k):
+            return PACK * width(k)
+
         def slots(k):
             return slice(first[k] * C, (first[k] + UNITS[k]) * C)
 
-        def planes(ring, k):
-            return ring[k % len(ring)][:, : PACK * width(k)].rearrange("p (t s) -> p t s", t=PACK)
+        def home(tiles, k):
+            return tiles[k % len(tiles)][:, : span(k)]
+
+        def tenant(name, room, k, columns, dtype):
+            if (name, room, k) not in tenants:
+                tenants[name, room, k] = keep.tile(
+                    [P, columns], dtype, tag="%s%d" % (room, k % AHEAD), name=name, align_bytes=64
+                )
+            return tenants[name, room, k][:]
+
+        def lodger(name, k, room, start, columns, dtype):
+            if (name, k) not in tenants:
+                tenants[name, k] = rooms.tile(
+                    [P, columns], dtype, name="%s%d" % (name, k), offset=room % HOMES * ROOM + start, align_bytes=64
+                )
+            return tenants[name, k][:]
+
+        def w2_sb(k):
+            return lodger("w2_sb", k, k + 1, W2_AT, UNITS[k] * 2 * H, U8)
+
+        def sm(k):
+            return tenant("sm", "sm_room", k, span(k), F32)
+
+        def a3_sb(k):
+            return tenant("a3_sb", "a3_room", k, span(k), F32)
+
+        def codes_of_step(k, room):
+            return tenant("codes", room, k, 3 * PACKED, U8)
+
+        def by_plane(ap):
+            return ap.rearrange("p (t s) -> p t s", t=PACK)
 
         def load_dy(t):
             nc.sync.dma_start(dy[t][:], dyT.rearrange("(p t) c -> p t c", t=PACK)[:, t, :])
 
-        def load_a1(k, t0=0, t1=PACK):
-            pair = dx[:, :SPAN] if k < 2 else home[first[k] // 2 % HOMES][:]
-            start = first[k] % 2 * PACK * C
-            a1_sb[k] = pair[:, start : start + PACK * width(k)].rearrange("p (t s) -> p t s", t=PACK)
-            nc.sync.dma_start(a1_sb[k][:, t0:t1, :], a1.rearrange("(p t) s -> p t s", t=PACK)[:, t0:t1, slots(k)])
+        def a1_home(k):
+            if k == 0:
+                return by_plane(sm(0))
+            return by_plane(lodger("a1_sb", k, k + 2, A1_AT, SPAN, F32)[:, : span(k)])
 
-        def y_cut(k):
-            return PACK - 1 if k in SPLIT else PACK
+        def load_rows(place, rows, k, t0=0, t1=PACK):
+            nc.sync.dma_start(place[:, t0:t1, :], rows.rearrange("(p t) s -> p t s", t=PACK)[:, t0:t1, slots(k)])
+
+        def load_a1(k, t0=0, t1=PACK):
+            load_rows(a1_home(k), a1, k, t0, t1)
 
         def load_a3(k):
-            rows = a3.rearrange("(p t) s -> p t s", t=PACK)[:, :, slots(k)]
-            a3_sb[k] = keep.tile([P, y_cut(k), width(k)], F32, tag="a3_%d" % (k % A3_HOMES), name="a3_sb", align_bytes=64)
-            nc.sync.dma_start(a3_sb[k][:], rows[:, : y_cut(k), :])
-            if k in SPLIT:
-                a3_rest[k] = keep.tile([P, 1, width(k)], F32, name="a3_rest%d" % k, align_bytes=64)
-                nc.sync.dma_start(a3_rest[k][:], rows[:, y_cut(k) :, :])
+            load_rows(by_plane(a3_sb(k)), a3, k)
 
-        def load_w2(e0, e1):
+        def load_w2(k0, k1):
+            e0, e1 = first[k0], first[k1 - 1] + UNITS[k1 - 1]
             raw = keep.tile([P, e1 - e0, 2 * H], U8, name="w2_raw%d" % e0, align_bytes=64)
             nc.sync.dma_start(raw[:].bitcast(I32), w2_words[e0:e1, 0, :, :].rearrange("e p b -> p e b").bitcast(I32))
-            for k in range(len(UNITS)):
-                if e0 <= first[k] < e1:
-                    w2_raw[k] = raw[:, first[k] - e0 : first[k] - e0 + UNITS[k], :]
+            for k in range(k0, k1):
+                w2_raw[k] = raw[:, first[k] - e0 : first[k] - e0 + UNITS[k], :]
 
-        def load_w13(e0, e1):
+        def load_w13():
             for m, packed in enumerate((w1_words, w3_words)):
-                nc.sync.dma_start(
-                    w13[m][:, e0:e1, :].bitcast(I32), packed[e0:e1, 0, :, :].rearrange("e p b -> p e b").bitcast(I32)
-                )
+                nc.sync.dma_start(w13[m][:].bitcast(I32), packed[:, 0, :, :].rearrange("e p b -> p e b").bitcast(I32))
 
         def load_s13():
             for m, scales in enumerate((w1_scales, w3_scales)):
                 nc.gpsimd.dma_start(
                     s13[:16, :, m, :].bitcast(I32), scales[:, 0, :, :].rearrange("e f n -> f e n").bitcast(I32)
                 )
-
-        def spread_s13():
             rows = s13[:].rearrange("p e m n -> p (e m n)").bitcast(I32)
             for quad in range(1, 4):
                 nc.gpsimd.dma_start(rows[32 * quad : 32 * quad + 4, :], rows[4 * quad : 4 * quad + 4, :])
 
-        def load_s2(b, quads):
+        def load_s2(b):
             count = (E - b + 1) // 2
-            for quad in quads:
+            for quad in range(4):
                 nc.sync.dma_start(
                     stacked[32 * quad : 32 * quad + 4 * count, b, :].bitcast(I32),
                     w2_scales[b::2, 0, 4 * quad : 4 * quad + 4, :].bitcast(I32),
@@ -173,254 +201,247 @@ def tile_moe_bdx_glu_sigmoid_kernel(
             )
 
         def turn_gate():
-            nc.tensor.transpose(bank[3][:, :GROUP], gate_rows[:], ident[:])
-            nc.scalar.activation(gate_cols[:], bank[3][:, : S // GROUP], ACT.Copy, scale=-1.0)
+            nc.tensor.transpose(dx_bank[1][:, :GROUP], gate_rows[:], ident[:])
+            nc.scalar.activation(gate_cols[:], dx_bank[1][:, : S // GROUP], ACT.Copy, scale=-1.0)
 
         def spread_gate(k):
-            gate_ps[k] = bank[k % 4][:, : width(k)]
             for j in range(width(k) // GROUP):
                 col = first[k] * C // GROUP + j
                 nc.tensor.transpose(
-                    gate_ps[k][:, j * GROUP : (j + 1) * GROUP], gate_cols[:, col : col + 1].to_broadcast([P, P]), ident[:]
+                    gate_bank[k % 2][:, j * GROUP : (j + 1) * GROUP],
+                    gate_cols[:, col : col + 1].to_broadcast([P, P]),
+                    ident[:],
                 )
 
-        def picked(e0, e1):
-            pair = (home[(e0 // 2 - 2) % HOMES] if e0 < first[LEAD] else exact_home[(e0 // 2 - 2) % 3])[:].rearrange("p (t s) -> p t s", t=PACK)
-            return pair[:, :, e0 % 2 * C : (e0 % 2 + e1 - e0) * C]
+        def picked(k):
+            if k == 0:
+                return by_plane(dx[:, S - span(0) :])
+            if k == HEAD:
+                return by_plane(exact_ring[LAG][:])
+            return by_plane(lodger("picked", k, k, 0, SPAN, F32)[:, : span(k)])
 
-        def gather(e0, e1, t, on_vector):
-            window = dy[t][:].indirect(offs_sb[:, e0 * C // 16 : e1 * C // 16])
-            if on_vector:
-                nc.vector.tensor_copy(picked(e0, e1)[:, t, :], window)
+        def gather(k, t, engine):
+            window = dy[t][:].indirect(offs_sb[:, first[k] * C // 16 : (first[k] + UNITS[k]) * C // 16])
+            plane = picked(k)[:, t, :]
+            if engine is nc.vector:
+                nc.vector.tensor_copy(plane, window)
             else:
-                nc.scalar.activation(picked(e0, e1)[:, t, :], window, ACT.Copy)
+                nc.scalar.activation(plane, window, ACT.Copy)
+
+        def g_words(k):
+            return y_ring[k % len(y_ring)][:].bitcast(BF16)[:, : span(k)]
 
         def apply_gate(k):
-            start = 2 * SPAN - WIDE * (1 - k) if k < 2 else k % 2 * 2 * SPAN + G_START
-            g_words[k] = y_home[:].bitcast(BF16)[:, start : start + PACK * width(k)]
             runs = width(k) // RUN
+            row = gate_bank[k % 2][:, : width(k)].rearrange("p (c i) -> p c i", i=RUN)
             nc.vector.tensor_tensor(
-                words_by_runs(g_words[k][:]),
-                planes_by_runs(picked(first[k], first[k] + UNITS[k])),
-                gate_ps[k][:].rearrange("p (c i) -> p c i", i=RUN).unsqueeze(2).to_broadcast([P, runs, PACK, RUN]),
+                words_by_runs(g_words(k)),
+                planes_by_runs(picked(k)),
+                row.unsqueeze(2).to_broadcast([P, runs, PACK, RUN]),
                 MULT,
             )
 
         def sigmoid_minus(k, t0=0, t1=PACK):
-            if t0 == 0:
-                sm[k] = keep.tile([P, PACK, width(k)], F32, tag="sm%d" % (k % 2), name="sm", align_bytes=64)
-            nc.scalar.activation(sm[k][:, t0:t1, :], a1_sb[k][:, t0:t1, :], ACT.Sigmoid, scale=-1.0)
+            nc.scalar.activation(by_plane(sm(k))[:, t0:t1, :], a1_home(k)[:, t0:t1, :], ACT.Sigmoid, scale=-1.0)
 
-        def y_planes(k):
-            start = {0: SPAN // 2, last: 0}.get(k, k % 2 * SPAN)
-            return (y_home if k < last else exact_home[0])[:, start : start + PACK * width(k)].rearrange("p (t s) -> p t s", t=PACK)
+        def factor_y(k):
+            nc.gpsimd.tensor_tensor(home(y_ring, k), a3_sb(k), sm(k), MULT)
 
-        def factor_y(k, engine):
-            engine.tensor_tensor(y_planes(k)[:, : y_cut(k), :], a3_sb[k][:], sm[k][:, : y_cut(k), :], MULT)
-
-        def finish_y(k):
-            nc.vector.tensor_tensor(y_planes(k)[:, y_cut(k) :, :], a3_rest[k][:], sm[k][:, y_cut(k) :, :], MULT)
-
-        def reorder_w2(k):
-            w2_sb[k] = w2_home[k % 2][:, : UNITS[k] * 2 * H]
-            copy = nc.vector.tensor_copy if k < W2_TURN else nc.scalar.copy
+        def reorder_w2(k, engine):
+            copy = nc.vector.tensor_copy if engine is nc.vector else nc.scalar.copy
             copy(
-                w2_sb[k][:].bitcast(U16).rearrange("p (e t c i) -> p e c t i", t=PACK, i=LINE, c=P // LINE),
-                w2_raw[k][:].bitcast(U16).rearrange("p e (c i t) -> p e c t i", t=PACK, i=LINE),
+                w2_sb(k).bitcast(U16).rearrange("p (e t c i) -> p e c t i", t=PACK, i=LINE, c=P // LINE),
+                w2_raw[k].bitcast(U16).rearrange("p e (c i t) -> p e c t i", t=PACK, i=LINE),
             )
 
-        def quantize_g(k):
-            g_mx[k] = keep.tile([P, 5 * width(k)], U8, tag="sm%d" % ((k - 1) % 2), name="g_mx", align_bytes=64)
+        def quantize(packed, words, count):
             nc.vector.quantize_mx(
-                out=g_mx[k][:, : 4 * width(k)].bitcast(U32).bitcast(FP8X4),
-                scales=g_mx[k][:, 4 * width(k) :],
-                in_=g_words[k][:],
+                out=packed[:, : 4 * count].bitcast(U32).bitcast(FP8X4), scales=packed[:, 4 * count : 5 * count], in_=words
             )
+
+        def columns(packed, count, start):
+            return (
+                packed[:, 4 * start : 4 * (start + C)].bitcast(U32).bitcast(FP8X4),
+                packed[:, 4 * count + start : 4 * count + start + C],
+            )
+
+        def g_mx(k):
+            return codes_of_step(k - 1, "a3_room")[:, :PACKED]
+
+        def dh_part(k, b):
+            return dh_bank[(2 * (k == last) + b) % 4]
 
         def first_product(k):
-            for j in range(UNITS[k]):
-                for half in range(2):
-                    dh[k, j, half] = dh_bank[(2 * (first[k] + j) + half) % 4]
-                    for u in range(2):
-                        t = 2 * half + u
-                        start = j * 2 * H + 2 * P * t
-                        nc.tensor.matmul_mx(
-                            out=dh[k, j, half][:, u, :],
-                            lhsT=w2_sb[k][:, start : start + 2 * P].bitcast(FP4X4),
-                            lhsT_scale=s2_plane(first[k] + j)[:, P * t : P * (t + 1)],
-                            rhs=g_mx[k][:, 4 * j * C : 4 * (j + 1) * C].bitcast(U32).bitcast(FP8X4),
-                            rhs_scale=g_mx[k][:, 4 * width(k) + j * C : 4 * width(k) + (j + 1) * C],
-                            start=True,
-                            stop=True,
-                        )
-
-        def exact_da3(k):
-            for j in range(UNITS[k]):
-                for half in range(2):
-                    part = (slice(None), slice(2 * half, 2 * half + 2), slice(j * C, (j + 1) * C))
-                    nc.vector.scalar_tensor_tensor(
-                        planes(exact_home, k)[part], sm[k][part], 1.0, dh[k, j, half][:], SUB, MULT
+            for t in range(PACK):
+                for j in range(UNITS[k]):
+                    place = t * width(k) + j * C
+                    start = j * 2 * H + 2 * P * t
+                    codes, scales = columns(g_mx(k), width(k), j * C)
+                    nc.tensor.matmul_mx(
+                        out=dh_part(k, place // BANK)[:, place % BANK : place % BANK + C],
+                        lhsT=w2_sb(k)[:, start : start + 2 * P].bitcast(FP4X4),
+                        lhsT_scale=s2_plane(first[k] + j)[:, P * t : P * (t + 1)],
+                        rhs=codes,
+                        rhs_scale=scales,
+                        start=True,
+                        stop=True,
                     )
 
-        def round_da3(k):
-            nc.scalar.copy(words_by_runs(da_words[k][:, 1, :]), planes_by_runs(planes(exact_home, k)))
+        def exact_da3(k):
+            for b in range(span(k) // BANK):
+                part = slice(b * BANK, (b + 1) * BANK)
+                nc.vector.scalar_tensor_tensor(
+                    home(exact_ring, k)[:, part], sm(k)[:, part], 1.0, dh_part(k, b)[:], SUB, MULT
+                )
+
+        def da_words(k, m):
+            if m == 1 and k < late:
+                return lodger("da3_words", k, k + LAG + 2, WORDS_AT, span(k), BF16)
+            return word_ring[k % LAG][:, m * span(k) : (m + 1) * span(k)]
 
         def make_da1(k):
             nc.vector.tensor_tensor(
-                words_by_runs(da_words[k][:, 0, :]),
-                planes_by_runs(planes(exact_home, k)),
-                planes_by_runs(y_planes(k)),
-                MULT,
+                words_by_runs(da_words(k, 0)), planes_by_runs(by_plane(home(exact_ring, k))), planes_by_runs(by_plane(home(y_ring, k))), MULT
             )
 
-        def quantize_da(k):
-            da_mx[k] = keep.tile([P, 10 * width(k)], U8, tag="a3_%d" % ((k + 1 + (k + 1 >= last)) % A3_HOMES), name="da_mx", align_bytes=64)
-            for m0, m1 in ((1, 2), (0, 1)) if k == last else ((0, 2),):
-                nc.vector.quantize_mx(
-                    out=da_mx[k][:, 4 * m0 * width(k) : 4 * m1 * width(k)].bitcast(U32).bitcast(FP8X4),
-                    scales=da_mx[k][:, (8 + m0) * width(k) : (8 + m1) * width(k)],
-                    in_=da_words[k][:, m0:m1, :].rearrange("p m b -> p (m b)"),
-                )
+        def round_da3(k):
+            nc.scalar.copy(words_by_runs(da_words(k, 1)), planes_by_runs(by_plane(home(exact_ring, k))))
+
+        def da_operand(k, m, j):
+            if k >= late:
+                return columns(da_mx[k], 2 * width(k), m * width(k) + j * C)
+            return columns(da_mx[k][:, m * PACKED :], width(k), j * C)
 
         def second_product(k):
-            dx_ps[k] = bank[(k + 3) % 4][:, : width(k)]
             for j in range(UNITS[k]):
                 e = first[k] + j
-                for m in (1, 0):
-                    col = m * width(k) + j * C
+                for m in range(2):
+                    codes, scales = da_operand(k, m, j)
                     nc.tensor.matmul_mx(
-                        out=dx_ps[k][:, j * C : (j + 1) * C],
+                        out=dx_bank[k % 2][:, j * C : (j + 1) * C],
                         lhsT=w13[m][:, e, :].bitcast(FP4X4),
                         lhsT_scale=s13[:, e, m, :],
-                        rhs=da_mx[k][:, 4 * col : 4 * (col + C)].bitcast(U32).bitcast(FP8X4),
-                        rhs_scale=da_mx[k][:, 8 * width(k) + col : 8 * width(k) + col + C],
-                        start=(m == 1),
-                        stop=(m == 0),
+                        rhs=codes,
+                        rhs_scale=scales,
+                        start=(m == 0),
+                        stop=(m == 1),
                     )
 
-        def copy_dx(k, engine):
-            if engine is nc.vector:
-                nc.vector.tensor_copy(dx[:, slots(k)], dx_ps[k][:])
+        def finish_da(k, place):
+            da_mx[k] = place[:, PACKED:]
+            if k >= late:
+                quantize(da_mx[k], word_ring[k % LAG][:, : 2 * span(k)], 2 * width(k))
             else:
-                nc.scalar.copy(dx[:, slots(k)], dx_ps[k][:])
+                for m in range(2):
+                    quantize(da_mx[k][:, m * PACKED :], da_words(k, m), width(k))
+            second_product(k)
+
+        def copy_dx(k, engine):
+            copy = nc.vector.tensor_copy if engine is nc.vector else nc.scalar.copy
+            copy(dx[:, slots(k)], dx_bank[k % 2][:, : width(k)])
 
         load_a1(0, 0, 1)
         nc.sync.dma_start(offs_sb[:], offs)
         load_dy(0)
         load_dy(1)
-        load_s2(0, range(4))
+        load_s2(0)
         nc.sync.dma_start(gate_rows[: S // GROUP, :], gate[0, :].rearrange("(b s) -> b s", s=GROUP))
         load_dy(2)
         load_w2(0, 1)
         load_dy(3)
         load_a1(0, 1, PACK)
-        load_s2(1, range(2))
+        load_s2(1)
         load_a3(0)
+        load_w2(1, 2)
         load_a1(1)
-        load_s2(1, range(2, 4))
-        load_w2(1, 4)
         load_a3(1)
         load_a1(2)
-        load_w2(first[3], first[5])
-        load_a3(2)
-
+        load_w2(2, 4)
         load_s13()
-        spread_s13()
+
         sigmoid_minus(0, 0, 1)
-        gather(0, 2, 0, True)
-        gather(2, 4, 0, False)
-        gather(4, 6, 0, True)
-        gather(0, 2, 1, True)
-        gather(2, 4, 1, False)
-        turn_gate()
-        spread_gate(0)
-        spread_gate(1)
-        gather(4, 6, 1, False)
-        reorder_w2(0)
-        gather(0, 2, 2, True)
-        gather(2, 4, 2, False)
-        gather(4, 6, 2, False)
+        for t in range(PACK - 1):
+            gather(0, t, nc.scalar if t % 2 else nc.vector)
+            gather(1, t, nc.vector)
+            gather(2, t, nc.scalar)
+            gather(HEAD, t, nc.scalar)
+            if t == 1:
+                turn_gate()
+                spread_gate(0)
+                spread_gate(1)
+        reorder_w2(0, nc.vector)
         reorder_s2(0)
-        gather(0, 1, 3, True)
-        gather(1, 2, 3, True)
+        gather(0, PACK - 1, nc.vector)
         apply_gate(0)
-        quantize_g(0)
+        gather(1, PACK - 1, nc.vector)
+        quantize(g_mx(0), g_words(0), width(0))
         first_product(0)
-        reorder_w2(1)
+        gather(2, PACK - 1, nc.scalar)
+        sigmoid_minus(0, 1, PACK)
+        factor_y(0)
         reorder_s2(1)
         unstack_s2(1)
-        load_a1(3)
-        sigmoid_minus(0, 1, PACK)
-        gather(2, 4, 3, False)
-        gather(4, 6, 3, False)
+        reorder_w2(1, nc.scalar)
+        sigmoid_minus(1)
+        gather(HEAD, PACK - 1, nc.scalar)
+        reorder_w2(2, nc.scalar)
 
-        def gather_planes(k):
-            for t in range(PACK):
-                gather(first[k], first[k] + UNITS[k], t, False)
+        finished = {k: [k - LAG] for k in range(LAG, late)}
+        finished[late] = [late - LAG, late - LAG + 1]
+        finished[last] = [late - 1, late]
 
-        for k in range(len(UNITS) + 1):
-            if k + 1 <= last:
-                sigmoid_minus(k + 1)
-            if 4 <= k + 3 < LEAD:
-                gather_planes(k + 3)
-            if k + 1 <= last:
+        for k in range(len(UNITS)):
+            coming = k + AHEAD
+            for j in finished.get(k - 1, [])[:1]:
+                copy_dx(j, nc.vector)
+            if k < last:
                 apply_gate(k + 1)
-            if 2 <= k < last:
-                second_product(k - 2)
-                copy_dx(k - 2, nc.scalar)
+            if k + 2 <= last:
+                load_a3(k + 2)
+            if k + HOMES - 1 <= last:
+                load_a1(k + HOMES - 1)
             if k + 2 <= last:
                 spread_gate(k + 2)
-            if k == last:
-                factor_y(k, nc.vector)
-            if k <= last:
-                exact_da3(k)
-                da_words[k] = home[(k - 2) % HOMES][:].bitcast(BF16)[:, : 2 * PACK * width(k)].rearrange("p (m b) -> p m b", m=2)
-            if k <= last:
-                round_da3(k)
-            if k == 0:
-                factor_y(k, nc.vector)
-            if k in SPLIT:
-                finish_y(k)
-            if k >= 1:
-                quantize_da(k - 1)
-            if k >= last - 1:
-                second_product(k - 1)
-            if 1 <= k <= last - 3:
-                load_a1(k + 3)
+            exact_da3(k)
+            for j in finished.get(k - 1, [])[1:]:
+                copy_dx(j, nc.vector)
+            if k + 2 <= last:
+                sigmoid_minus(k + 2)
+            if 0 <= k - 1 < late:
+                round_da3(k - 1)
             if k + 2 < LEVELS:
                 unstack_s2(k + 2)
-            if k + 3 <= last:
-                load_a3(k + 3)
-                if k in (1, 3):
-                    load_w2(first[k + 4], min(first[k + 4] + 4, E))
-            if k == LATE + 2:
-                load_w13(EARLY, E)
-            if k == LATE:
-                load_w13(0, EARLY)
+            if k in (1, 3):
+                load_w2(k + 3, min(k + 5 + (k == 3), last + 1))
+            if k == 1:
+                load_w13()
             if k == last - 3:
                 for r, pos in enumerate((pos1, pos2, pos3)):
                     nc.sync.dma_start(pos_sb[r][:], pos)
-            if k + 2 < W2_TURN:
-                reorder_w2(k + 2)
-            if k + 1 <= last:
-                quantize_g(k + 1)
+            for j, room in zip(finished.get(k, []), ("a3_room", "sm_room")):
+                finish_da(j, codes_of_step(k, room))
+            if k >= late:
+                round_da3(k)
+            if k < last:
+                quantize(g_mx(k + 1), g_words(k + 1), width(k + 1))
                 first_product(k + 1)
-            if k + 1 < last:
-                factor_y(k + 1, nc.gpsimd)
-            if k <= last:
-                make_da1(k)
-            if LEAD <= k + 3 <= last:
-                gather_planes(k + 3)
-            if W2_TURN <= k + 2 <= last:
-                reorder_w2(k + 2)
-            if k >= last - 1:
-                copy_dx(k - 1, nc.scalar if k <= last else nc.vector)
+                factor_y(k + 1)
+            make_da1(k)
+            if coming <= last:
+                reorder_w2(coming, nc.scalar)
+            if coming < last:
+                for t in range(PACK):
+                    gather(coming + 1, t, nc.scalar)
+        copy_dx(late - 1, nc.scalar)
+        finish_da(last, codes_of_step(last + 1, "sm_room"))
+        copy_dx(late, nc.vector)
+        copy_dx(last, nc.vector)
 
         def fetch(r, c0, c1):
             return dx[:].indirect(pos_sb[r][:, c0 // 16 : c1 // 16])
 
-        one, two, three = home[2:]
-        total = y_home
+        one, two, three = (lodger("part", r, r, 0, T, F32) for r in range(3))
+        total = y_ring[0]
         c1, c2, c3 = OUT_CUTS
         nc.vector.tensor_copy(two[:, :c1], fetch(1, 0, c1))
         for c0, c4 in ((c1, c2), (0, c1), (c2, c3), (c3, T)):

@@ -25,7 +25,7 @@ MULT = mybir.AluOpType.mult
 ADD = mybir.AluOpType.add
 SUB = mybir.AluOpType.subtract
 
-UNITS = [1, 2, 2, 2, 2, 2, 2, 1, 1]
+UNITS = [1, 1, 2, 2, 2, 2, 2, 2, 1]
 WIDE = 2 * C
 SPAN = PACK * WIDE
 OUT_CUTS = (256, 448, 960)
@@ -41,6 +41,10 @@ W2_AT = WORDS_AT + 2 * SPAN
 ROOM = W2_AT + 4 * H
 A1_AT = ROOM - 4 * SPAN
 PACKED = 5 * WIDE
+WORD_BYTES = 2 * SPAN
+Y_AT = (WORD_BYTES, 4 * WORD_BYTES)
+WORDS_IN_ROW = (3 * WORD_BYTES, 0, 6 * WORD_BYTES)
+G_ASTRIDE = {1: Y_AT[1] - WORD_BYTES // 4, 2: Y_AT[0] - WORD_BYTES // 2, 3: WORDS_IN_ROW[2] - WORD_BYTES // 2}
 LEVELS = (E + 1) // 2
 
 
@@ -63,14 +67,13 @@ def tile_moe_bdx_glu_sigmoid_kernel(
     with ExitStack() as ctx:
         keep = ctx.enter_context(tc.tile_pool(name="keep", bufs=1))
         rooms = ctx.enter_context(tc.tile_pool(name="rooms", bufs=1))
+        row = ctx.enter_context(tc.tile_pool(name="row", bufs=1))
         psum = ctx.enter_context(tc.psum_pool(name="psum", bufs=1))
 
         def ring(name, count, columns, dtype):
             return [keep.tile([P, columns], dtype, name="%s%d" % (name, r), align_bytes=64) for r in range(count)]
 
-        y_ring = ring("y", 2, SPAN, F32)
         exact_ring = ring("exact", LAG + 1, SPAN, F32)
-        word_ring = ring("words", LAG, SPAN, BF16)
         dh_bank = [psum.tile([P, BANK], F32, name="dh_bank%d" % r) for r in range(4)]
         gate_bank = [psum.tile([P, BANK], F32, name="gate_bank%d" % r) for r in range(2)]
         dx_bank = [psum.tile([P, BANK], F32, name="dx_bank%d" % r) for r in range(2)]
@@ -122,7 +125,20 @@ def tile_moe_bdx_glu_sigmoid_kernel(
                 )
             return tenants[name, k][:]
 
+        def in_row(name, k, start, columns, dtype):
+            if (name, k) not in tenants:
+                tenants[name, k] = row.tile([P, columns], dtype, name="%s%d" % (name, k), offset=start, align_bytes=64)
+            return tenants[name, k][:]
+
+        def y_sb(k):
+            return in_row("y", k, Y_AT[k % 2], span(k), F32)
+
+        def word_pair(k):
+            return in_row("words", k, WORDS_IN_ROW[k % LAG], SPAN, BF16)
+
         def w2_sb(k):
+            if 1 <= k <= LAG:
+                return codes_of_step(k - 1, "sm_room")[:, PACKED : PACKED + UNITS[k] * 2 * H]
             return lodger("w2_sb", k, k + 1, W2_AT, UNITS[k] * 2 * H, U8)
 
         def sm(k):
@@ -229,7 +245,7 @@ def tile_moe_bdx_glu_sigmoid_kernel(
                 nc.scalar.activation(plane, window, ACT.Copy)
 
         def g_words(k):
-            return y_ring[k % len(y_ring)][:].bitcast(BF16)[:, : span(k)]
+            return in_row("g_words", k, G_ASTRIDE.get(k, Y_AT[k % 2]), span(k), BF16)
 
         def apply_gate(k):
             runs = width(k) // RUN
@@ -245,7 +261,7 @@ def tile_moe_bdx_glu_sigmoid_kernel(
             nc.scalar.activation(by_plane(sm(k))[:, t0:t1, :], a1_home(k)[:, t0:t1, :], ACT.Sigmoid, scale=-1.0)
 
         def factor_y(k):
-            nc.gpsimd.tensor_tensor(home(y_ring, k), a3_sb(k), sm(k), MULT)
+            nc.gpsimd.tensor_tensor(y_sb(k), a3_sb(k), sm(k), MULT)
 
         def reorder_w2(k, engine):
             copy = nc.vector.tensor_copy if engine is nc.vector else nc.scalar.copy
@@ -266,7 +282,7 @@ def tile_moe_bdx_glu_sigmoid_kernel(
             )
 
         def g_mx(k):
-            return codes_of_step(k - 1, "a3_room")[:, :PACKED]
+            return codes_of_step(k - 1, "a3_room" if k > LAG else "sm_room")[:, :PACKED]
 
         def dh_part(k, b):
             return dh_bank[(2 * (k == last) + b) % 4]
@@ -295,20 +311,20 @@ def tile_moe_bdx_glu_sigmoid_kernel(
                 )
 
         def da_words(k, m):
-            if m == 1 and k < late:
+            if m == 1 and k < last:
                 return lodger("da3_words", k, k + LAG + 2, WORDS_AT, span(k), BF16)
-            return word_ring[k % LAG][:, m * span(k) : (m + 1) * span(k)]
+            return word_pair(k)[:, m * span(k) : (m + 1) * span(k)]
 
         def make_da1(k):
             nc.vector.tensor_tensor(
-                words_by_runs(da_words(k, 0)), planes_by_runs(by_plane(home(exact_ring, k))), planes_by_runs(by_plane(home(y_ring, k))), MULT
+                words_by_runs(da_words(k, 0)), planes_by_runs(by_plane(home(exact_ring, k))), planes_by_runs(by_plane(y_sb(k))), MULT
             )
 
         def round_da3(k):
             nc.scalar.copy(words_by_runs(da_words(k, 1)), planes_by_runs(by_plane(home(exact_ring, k))))
 
         def da_operand(k, m, j):
-            if k >= late:
+            if k == last:
                 return columns(da_mx[k], 2 * width(k), m * width(k) + j * C)
             return columns(da_mx[k][:, m * PACKED :], width(k), j * C)
 
@@ -329,8 +345,8 @@ def tile_moe_bdx_glu_sigmoid_kernel(
 
         def finish_da(k, place):
             da_mx[k] = place[:, PACKED:]
-            if k >= late:
-                quantize(da_mx[k], word_ring[k % LAG][:, : 2 * span(k)], 2 * width(k))
+            if k == last:
+                quantize(da_mx[k], word_pair(k)[:, : 2 * span(k)], 2 * width(k))
             else:
                 for m in range(2):
                     quantize(da_mx[k][:, m * PACKED :], da_words(k, m), width(k))
@@ -340,6 +356,7 @@ def tile_moe_bdx_glu_sigmoid_kernel(
             copy = nc.vector.tensor_copy if engine is nc.vector else nc.scalar.copy
             copy(dx[:, slots(k)], dx_bank[k % 2][:, : width(k)])
 
+        a1_rest = exact_ring[LAG][:, 2 * WIDE : 2 * WIDE + (PACK - 1) * C].rearrange("p (t s) -> p t s", s=C)
         load_a1(0, 0, 1)
         nc.sync.dma_start(offs_sb[:], offs)
         load_dy(0)
@@ -349,22 +366,22 @@ def tile_moe_bdx_glu_sigmoid_kernel(
         load_dy(2)
         load_w2(0, 1)
         load_dy(3)
-        load_a1(0, 1, PACK)
+        nc.sync.dma_start(a1_rest, a1.rearrange("(p t) s -> p t s", t=PACK)[:, 1:, slots(0)])
         load_s2(1)
         load_a3(0)
         load_w2(1, 2)
         load_a1(1)
         load_a3(1)
         load_a1(2)
-        load_w2(2, 4)
         load_s13()
 
         sigmoid_minus(0, 0, 1)
         for t in range(PACK - 1):
-            gather(0, t, nc.scalar if t % 2 else nc.vector)
+            gather(0, t, nc.vector)
             gather(1, t, nc.vector)
             gather(2, t, nc.scalar)
-            gather(HEAD, t, nc.scalar)
+            if t < 2:
+                gather(HEAD, t, nc.scalar)
             if t == 1:
                 turn_gate()
                 spread_gate(0)
@@ -377,14 +394,14 @@ def tile_moe_bdx_glu_sigmoid_kernel(
         quantize(g_mx(0), g_words(0), width(0))
         first_product(0)
         gather(2, PACK - 1, nc.scalar)
-        sigmoid_minus(0, 1, PACK)
+        nc.scalar.activation(by_plane(sm(0))[:, 1:, :], a1_rest, ACT.Sigmoid, scale=-1.0)
         factor_y(0)
         reorder_s2(1)
         unstack_s2(1)
-        reorder_w2(1, nc.scalar)
+        load_w2(2, 4)
         sigmoid_minus(1)
+        gather(HEAD, PACK - 2, nc.scalar)
         gather(HEAD, PACK - 1, nc.scalar)
-        reorder_w2(2, nc.scalar)
 
         finished = {k: [k - LAG] for k in range(LAG, late)}
         finished[late] = [late - LAG, late - LAG + 1]
@@ -407,7 +424,7 @@ def tile_moe_bdx_glu_sigmoid_kernel(
                 copy_dx(j, nc.vector)
             if k + 2 <= last:
                 sigmoid_minus(k + 2)
-            if 0 <= k - 1 < late:
+            if k >= 1:
                 round_da3(k - 1)
             if k + 2 < LEVELS:
                 unstack_s2(k + 2)
@@ -420,14 +437,16 @@ def tile_moe_bdx_glu_sigmoid_kernel(
                     nc.sync.dma_start(pos_sb[r][:], pos)
             for j, room in zip(finished.get(k, []), ("a3_room", "sm_room")):
                 finish_da(j, codes_of_step(k, room))
-            if k >= late:
+            if k == last:
                 round_da3(k)
+            if k < LAG:
+                reorder_w2(k + 1, nc.vector)
             if k < last:
                 quantize(g_mx(k + 1), g_words(k + 1), width(k + 1))
                 first_product(k + 1)
                 factor_y(k + 1)
             make_da1(k)
-            if coming <= last:
+            if LAG < coming <= last:
                 reorder_w2(coming, nc.scalar)
             if coming < last:
                 for t in range(PACK):
@@ -441,7 +460,7 @@ def tile_moe_bdx_glu_sigmoid_kernel(
             return dx[:].indirect(pos_sb[r][:, c0 // 16 : c1 // 16])
 
         one, two, three = (lodger("part", r, r, 0, T, F32) for r in range(3))
-        total = y_ring[0]
+        total = in_row("total", 0, Y_AT[1], T, F32)
         c1, c2, c3 = OUT_CUTS
         nc.vector.tensor_copy(two[:, :c1], fetch(1, 0, c1))
         for c0, c4 in ((c1, c2), (0, c1), (c2, c3), (c3, T)):

@@ -35,6 +35,7 @@ LIVE = 100
 LAG = 3
 AHEAD = 3
 HEAD = 3
+W2_TURN = 6
 HOMES = 4
 WORDS_AT = 4 * SPAN
 W2_AT = WORDS_AT + 2 * SPAN
@@ -139,6 +140,8 @@ def tile_moe_bdx_glu_sigmoid_kernel(
         def w2_sb(k):
             if 1 <= k <= LAG:
                 return codes_of_step(k - 1, "sm_room")[:, PACKED : PACKED + UNITS[k] * 2 * H]
+            if LAG < k < W2_TURN:
+                return tenant("w2_sb", "sm_room", k - 1, UNITS[k] * 2 * H, U8)
             return lodger("w2_sb", k, k + 1, W2_AT, UNITS[k] * 2 * H, U8)
 
         def sm(k):
@@ -439,14 +442,14 @@ def tile_moe_bdx_glu_sigmoid_kernel(
                 finish_da(j, codes_of_step(k, room))
             if k == last:
                 round_da3(k)
-            if k < LAG:
+            if k + 1 < W2_TURN:
                 reorder_w2(k + 1, nc.vector)
             if k < last:
                 quantize(g_mx(k + 1), g_words(k + 1), width(k + 1))
                 first_product(k + 1)
                 factor_y(k + 1)
             make_da1(k)
-            if LAG < coming <= last:
+            if W2_TURN <= coming <= last:
                 reorder_w2(coming, nc.scalar)
             if coming < last:
                 for t in range(PACK):

@@ -45,7 +45,6 @@ PACKED = 5 * WIDE
 WORD_BYTES = 2 * SPAN
 Y_AT = (WORD_BYTES, 4 * WORD_BYTES)
 WORDS_IN_ROW = (3 * WORD_BYTES, 0, 6 * WORD_BYTES)
-G_ASTRIDE = {1: Y_AT[1] - WORD_BYTES // 4, 2: Y_AT[0] - WORD_BYTES // 2, 3: WORDS_IN_ROW[2] - WORD_BYTES // 2}
 LEVELS = (E + 1) // 2
 
 
@@ -76,8 +75,8 @@ def tile_moe_bdx_glu_sigmoid_kernel(
 
         exact_ring = ring("exact", LAG + 1, SPAN, F32)
         dh_bank = [psum.tile([P, BANK], F32, name="dh_bank%d" % r) for r in range(4)]
-        gate_bank = [psum.tile([P, BANK], F32, name="gate_bank%d" % r) for r in range(2)]
-        dx_bank = [psum.tile([P, BANK], F32, name="dx_bank%d" % r) for r in range(2)]
+        gate_bank = psum.tile([P, BANK], F32, name="gate_bank")
+        dx_bank = [psum.tile([P, BANK], F32, name="dx_bank%d" % r) for r in range(3)]
 
         offs_sb = keep.tile([P, S // 16], U16, name="offs_sb")
         pos_sb = [keep.tile([P, T // 16], U16, name="pos_sb%d" % r) for r in range(3)]
@@ -137,9 +136,12 @@ def tile_moe_bdx_glu_sigmoid_kernel(
         def word_pair(k):
             return in_row("words", k, WORDS_IN_ROW[k % LAG], SPAN, BF16)
 
+        def exact(k):
+            return dx[:, :SPAN] if k == LAG else home(exact_ring, k)
+
         def w2_sb(k):
             if 1 <= k <= LAG:
-                return codes_of_step(k - 1, "sm_room")[:, PACKED : PACKED + UNITS[k] * 2 * H]
+                return codes_of_step(k - 1, "a3_room")[:, PACKED : PACKED + UNITS[k] * 2 * H]
             if LAG < k < W2_TURN:
                 return tenant("w2_sb", "sm_room", k - 1, UNITS[k] * 2 * H, U8)
             return lodger("w2_sb", k, k + 1, W2_AT, UNITS[k] * 2 * H, U8)
@@ -175,8 +177,12 @@ def tile_moe_bdx_glu_sigmoid_kernel(
 
         def load_w2(k0, k1):
             e0, e1 = first[k0], first[k1 - 1] + UNITS[k1 - 1]
-            raw = keep.tile([P, e1 - e0, 2 * H], U8, name="w2_raw%d" % e0, align_bytes=64)
-            nc.sync.dma_start(raw[:].bitcast(I32), w2_words[e0:e1, 0, :, :].rearrange("e p b -> p e b").bitcast(I32))
+            if 1 <= k0 <= LAG:
+                flat = in_row("w2_raw", k0, WORDS_IN_ROW[k0 - 1], (e1 - e0) * 2 * H, U8)
+            else:
+                flat = keep.tile([P, (e1 - e0) * 2 * H], U8, name="w2_raw%d" % e0, align_bytes=64)[:]
+            raw = flat.rearrange("p (e b) -> p e b", b=2 * H)
+            nc.sync.dma_start(raw.bitcast(I32), w2_words[e0:e1, 0, :, :].rearrange("e p b -> p e b").bitcast(I32))
             for k in range(k0, k1):
                 w2_raw[k] = raw[:, first[k] - e0 : first[k] - e0 + UNITS[k], :]
 
@@ -189,9 +195,11 @@ def tile_moe_bdx_glu_sigmoid_kernel(
                 nc.gpsimd.dma_start(
                     s13[:16, :, m, :].bitcast(I32), scales[:, 0, :, :].rearrange("e f n -> f e n").bitcast(I32)
                 )
+
+        def spread_s13():
             rows = s13[:].rearrange("p e m n -> p (e m n)").bitcast(I32)
             for quad in range(1, 4):
-                nc.gpsimd.dma_start(rows[32 * quad : 32 * quad + 4, :], rows[4 * quad : 4 * quad + 4, :])
+                nc.sync.dma_start(rows[32 * quad : 32 * quad + 4, :], rows[4 * quad : 4 * quad + 4, :])
 
         def load_s2(b):
             count = (E - b + 1) // 2
@@ -220,14 +228,14 @@ def tile_moe_bdx_glu_sigmoid_kernel(
             )
 
         def turn_gate():
-            nc.tensor.transpose(dx_bank[1][:, :GROUP], gate_rows[:], ident[:])
-            nc.scalar.activation(gate_cols[:], dx_bank[1][:, : S // GROUP], ACT.Copy, scale=-1.0)
+            nc.tensor.transpose(dx_bank[2][:, :GROUP], gate_rows[:], ident[:])
+            nc.scalar.activation(gate_cols[:], dx_bank[2][:, : S // GROUP], ACT.Copy, scale=-1.0)
 
         def spread_gate(k):
             for j in range(width(k) // GROUP):
                 col = first[k] * C // GROUP + j
                 nc.tensor.transpose(
-                    gate_bank[k % 2][:, j * GROUP : (j + 1) * GROUP],
+                    gate_bank[:, j * GROUP : (j + 1) * GROUP],
                     gate_cols[:, col : col + 1].to_broadcast([P, P]),
                     ident[:],
                 )
@@ -248,11 +256,11 @@ def tile_moe_bdx_glu_sigmoid_kernel(
                 nc.scalar.activation(plane, window, ACT.Copy)
 
         def g_words(k):
-            return in_row("g_words", k, G_ASTRIDE.get(k, Y_AT[k % 2]), span(k), BF16)
+            return in_row("g_words", k, Y_AT[k % 2], span(k), BF16)
 
         def apply_gate(k):
             runs = width(k) // RUN
-            row = gate_bank[k % 2][:, : width(k)].rearrange("p (c i) -> p c i", i=RUN)
+            row = gate_bank[:, : width(k)].rearrange("p (c i) -> p c i", i=RUN)
             nc.vector.tensor_tensor(
                 words_by_runs(g_words(k)),
                 planes_by_runs(picked(k)),
@@ -285,7 +293,7 @@ def tile_moe_bdx_glu_sigmoid_kernel(
             )
 
         def g_mx(k):
-            return codes_of_step(k - 1, "a3_room" if k > LAG else "sm_room")[:, :PACKED]
+            return codes_of_step(k - 1, "a3_room")[:, :PACKED]
 
         def dh_part(k, b):
             return dh_bank[(2 * (k == last) + b) % 4]
@@ -306,11 +314,11 @@ def tile_moe_bdx_glu_sigmoid_kernel(
                         stop=True,
                     )
 
-        def exact_da3(k):
-            for b in range(span(k) // BANK):
+        def exact_da3(k, b0, b1):
+            for b in range(b0, b1):
                 part = slice(b * BANK, (b + 1) * BANK)
                 nc.vector.scalar_tensor_tensor(
-                    home(exact_ring, k)[:, part], sm(k)[:, part], 1.0, dh_part(k, b)[:], SUB, MULT
+                    exact(k)[:, part], sm(k)[:, part], 1.0, dh_part(k, b)[:], SUB, MULT
                 )
 
         def da_words(k, m):
@@ -320,16 +328,21 @@ def tile_moe_bdx_glu_sigmoid_kernel(
 
         def make_da1(k):
             nc.vector.tensor_tensor(
-                words_by_runs(da_words(k, 0)), planes_by_runs(by_plane(home(exact_ring, k))), planes_by_runs(by_plane(y_sb(k))), MULT
+                words_by_runs(da_words(k, 0)), planes_by_runs(by_plane(exact(k))), planes_by_runs(by_plane(y_sb(k))), MULT
             )
 
         def round_da3(k):
-            nc.scalar.copy(words_by_runs(da_words(k, 1)), planes_by_runs(by_plane(home(exact_ring, k))))
+            nc.scalar.copy(words_by_runs(da_words(k, 1)), planes_by_runs(by_plane(exact(k))))
 
         def da_operand(k, m, j):
             if k == last:
                 return columns(da_mx[k], 2 * width(k), m * width(k) + j * C)
             return columns(da_mx[k][:, m * PACKED :], width(k), j * C)
+
+        def dx_ps(k):
+            if k < 2:
+                return dx_bank[0][:, slots(k)]
+            return dx_bank[(k - 1) % 3][:, : width(k)]
 
         def second_product(k):
             for j in range(UNITS[k]):
@@ -337,7 +350,7 @@ def tile_moe_bdx_glu_sigmoid_kernel(
                 for m in range(2):
                     codes, scales = da_operand(k, m, j)
                     nc.tensor.matmul_mx(
-                        out=dx_bank[k % 2][:, j * C : (j + 1) * C],
+                        out=dx_ps(k)[:, j * C : (j + 1) * C],
                         lhsT=w13[m][:, e, :].bitcast(FP4X4),
                         lhsT_scale=s13[:, e, m, :],
                         rhs=codes,
@@ -357,7 +370,10 @@ def tile_moe_bdx_glu_sigmoid_kernel(
 
         def copy_dx(k, engine):
             copy = nc.vector.tensor_copy if engine is nc.vector else nc.scalar.copy
-            copy(dx[:, slots(k)], dx_bank[k % 2][:, : width(k)])
+            if k == 1:
+                copy(dx[:, :BANK], dx_bank[0][:])
+            else:
+                copy(dx[:, slots(k)], dx_ps(k))
 
         a1_rest = exact_ring[LAG][:, 2 * WIDE : 2 * WIDE + (PACK - 1) * C].rearrange("p (t s) -> p t s", s=C)
         load_a1(0, 0, 1)
@@ -388,11 +404,11 @@ def tile_moe_bdx_glu_sigmoid_kernel(
             if t == 1:
                 turn_gate()
                 spread_gate(0)
-                spread_gate(1)
         reorder_w2(0, nc.vector)
         reorder_s2(0)
         gather(0, PACK - 1, nc.vector)
         apply_gate(0)
+        spread_gate(1)
         gather(1, PACK - 1, nc.vector)
         quantize(g_mx(0), g_words(0), width(0))
         first_product(0)
@@ -401,7 +417,7 @@ def tile_moe_bdx_glu_sigmoid_kernel(
         factor_y(0)
         reorder_s2(1)
         unstack_s2(1)
-        load_w2(2, 4)
+        load_w2(2, 3)
         sigmoid_minus(1)
         gather(HEAD, PACK - 2, nc.scalar)
         gather(HEAD, PACK - 1, nc.scalar)
@@ -410,10 +426,12 @@ def tile_moe_bdx_glu_sigmoid_kernel(
         finished[late] = [late - LAG, late - LAG + 1]
         finished[last] = [late - 1, late]
 
+        copied = {late: [1, 2, LAG], last: finished[late]}
+
         for k in range(len(UNITS)):
             coming = k + AHEAD
-            for j in finished.get(k - 1, [])[:1]:
-                copy_dx(j, nc.vector)
+            opening = int(1 <= k < last)
+            exact_da3(k, 0, opening)
             if k < last:
                 apply_gate(k + 1)
             if k + 2 <= last:
@@ -422,19 +440,22 @@ def tile_moe_bdx_glu_sigmoid_kernel(
                 load_a1(k + HOMES - 1)
             if k + 2 <= last:
                 spread_gate(k + 2)
-            exact_da3(k)
-            for j in finished.get(k - 1, [])[1:]:
-                copy_dx(j, nc.vector)
+            exact_da3(k, opening, span(k) // BANK)
+            for j in copied.get(k, []):
+                copy_dx(j, nc.scalar if j == LAG else nc.vector)
             if k + 2 <= last:
                 sigmoid_minus(k + 2)
             if k >= 1:
                 round_da3(k - 1)
             if k + 2 < LEVELS:
                 unstack_s2(k + 2)
+            if k == 0:
+                load_w2(3, 4)
             if k in (1, 3):
                 load_w2(k + 3, min(k + 5 + (k == 3), last + 1))
             if k == 1:
                 load_w13()
+                spread_s13()
             if k == last - 3:
                 for r, pos in enumerate((pos1, pos2, pos3)):
                     nc.sync.dma_start(pos_sb[r][:], pos)

@@ -390,6 +390,7 @@ def tile_moe_bdx_glu_sigmoid_kernel(
         load_a3(0)
         load_w2(1, 2)
         load_a1(1)
+        load_w2(2, 3)
         load_a3(1)
         load_a1(2)
         load_s13()
@@ -417,7 +418,7 @@ def tile_moe_bdx_glu_sigmoid_kernel(
         factor_y(0)
         reorder_s2(1)
         unstack_s2(1)
-        load_w2(2, 3)
+        load_w2(3, 4)
         sigmoid_minus(1)
         gather(HEAD, PACK - 2, nc.scalar)
         gather(HEAD, PACK - 1, nc.scalar)
@@ -450,9 +451,9 @@ def tile_moe_bdx_glu_sigmoid_kernel(
             if k + 2 < LEVELS:
                 unstack_s2(k + 2)
             if k == 0:
-                load_w2(3, 4)
-            if k in (1, 3):
-                load_w2(k + 3, min(k + 5 + (k == 3), last + 1))
+                load_w2(LAG + 1, W2_TURN)
+            if k == 2:
+                load_w2(W2_TURN, last + 1)
             if k == 1:
                 load_w13()
                 spread_s13()

@@ -68,6 +68,7 @@ def tile_moe_bdx_glu_sigmoid_kernel(
         keep = ctx.enter_context(tc.tile_pool(name="keep", bufs=1))
         rooms = ctx.enter_context(tc.tile_pool(name="rooms", bufs=1))
         row = ctx.enter_context(tc.tile_pool(name="row", bufs=1))
+        shelf = ctx.enter_context(tc.tile_pool(name="shelf", bufs=1))
         psum = ctx.enter_context(tc.psum_pool(name="psum", bufs=1))
 
         def ring(name, count, columns, dtype):
@@ -81,8 +82,7 @@ def tile_moe_bdx_glu_sigmoid_kernel(
         offs_sb = keep.tile([P, S // 16], U16, name="offs_sb")
         pos_sb = [keep.tile([P, T // 16], U16, name="pos_sb%d" % r) for r in range(3)]
         dy = [keep.tile([P, T], F32, name="dy%d" % t) for t in range(PACK)]
-        dx = keep.tile([P, S], F32, name="dx")
-        stacked = keep.tile([P, 2, H], U8, name="stacked", align_bytes=64)
+        stacked = shelf.tile([P, 2, H], U8, name="stacked", offset=2 * WORD_BYTES, align_bytes=64)
         s2_levels = keep.tile([P, 2, H], U8, name="s2_levels", align_bytes=64)
         s2_all = keep.tile([P, (E - 2) * H], U8, name="s2_all", align_bytes=64)
         w13 = [keep.tile([P, E, 2 * K], U8, name="w13_%d" % m, align_bytes=64) for m in range(2)]
@@ -130,14 +130,26 @@ def tile_moe_bdx_glu_sigmoid_kernel(
                 tenants[name, k] = row.tile([P, columns], dtype, name="%s%d" % (name, k), offset=start, align_bytes=64)
             return tenants[name, k][:]
 
+        def on_shelf(name, start, columns, dtype):
+            if name not in tenants:
+                tenants[name] = shelf.tile([P, columns], dtype, name=name, offset=start, align_bytes=64)
+            return tenants[name][:]
+
+        def dx():
+            return on_shelf("dx", 0, S, F32)
+
         def y_sb(k):
             return in_row("y", k, Y_AT[k % 2], span(k), F32)
 
         def word_pair(k):
+            if k == LAG:
+                return on_shelf("words_held", 0, SPAN, BF16)
+            if k == 2 * LAG:
+                return lodger("words", k, 2 * LAG + 2, WORDS_AT, SPAN, BF16)
             return in_row("words", k, WORDS_IN_ROW[k % LAG], SPAN, BF16)
 
         def exact(k):
-            return dx[:, :SPAN] if k == LAG else home(exact_ring, k)
+            return on_shelf("exact_held", WORD_BYTES, SPAN, F32) if k == LAG else home(exact_ring, k)
 
         def w2_sb(k):
             if 1 <= k <= LAG:
@@ -150,9 +162,13 @@ def tile_moe_bdx_glu_sigmoid_kernel(
             return tenant("sm", "sm_room", k, span(k), F32)
 
         def a3_sb(k):
+            if k == 0:
+                return on_shelf("a3_first", WORD_BYTES, span(0), F32)
             return tenant("a3_sb", "a3_room", k, span(k), F32)
 
         def codes_of_step(k, room):
+            if k == 0:
+                return on_shelf("codes_first", WORD_BYTES + WORD_BYTES // 2, 2 * PACKED, U8)
             return tenant("codes", room, k, 3 * PACKED, U8)
 
         def by_plane(ap):
@@ -179,6 +195,8 @@ def tile_moe_bdx_glu_sigmoid_kernel(
             e0, e1 = first[k0], first[k1 - 1] + UNITS[k1 - 1]
             if 1 <= k0 <= LAG:
                 flat = in_row("w2_raw", k0, WORDS_IN_ROW[k0 - 1], (e1 - e0) * 2 * H, U8)
+            elif k0 == LAG + 1:
+                flat = on_shelf("w2_raw_held", 0, (e1 - e0) * 2 * H, U8)
             else:
                 flat = keep.tile([P, (e1 - e0) * 2 * H], U8, name="w2_raw%d" % e0, align_bytes=64)[:]
             raw = flat.rearrange("p (e b) -> p e b", b=2 * H)
@@ -242,9 +260,9 @@ def tile_moe_bdx_glu_sigmoid_kernel(
 
         def picked(k):
             if k == 0:
-                return by_plane(dx[:, S - span(0) :])
-            if k == HEAD:
-                return by_plane(exact_ring[LAG][:])
+                return by_plane(on_shelf("picked_first", 0, span(0), F32))
+            if k in (HEAD - 1, HEAD):
+                return by_plane(exact_ring[k][:])
             return by_plane(lodger("picked", k, k, 0, SPAN, F32)[:, : span(k)])
 
         def gather(k, t, engine):
@@ -322,6 +340,8 @@ def tile_moe_bdx_glu_sigmoid_kernel(
                 )
 
         def da_words(k, m):
+            if m == 1 and k == late:
+                return in_row("da3_words", k, WORDS_IN_ROW[0], SPAN, BF16)
             if m == 1 and k < last:
                 return lodger("da3_words", k, k + LAG + 2, WORDS_AT, span(k), BF16)
             return word_pair(k)[:, m * span(k) : (m + 1) * span(k)]
@@ -371,11 +391,13 @@ def tile_moe_bdx_glu_sigmoid_kernel(
         def copy_dx(k, engine):
             copy = nc.vector.tensor_copy if engine is nc.vector else nc.scalar.copy
             if k == 1:
-                copy(dx[:, :BANK], dx_bank[0][:])
+                copy(dx()[:, :BANK], dx_bank[0][:])
             else:
-                copy(dx[:, slots(k)], dx_ps(k))
+                copy(dx()[:, slots(k)], dx_ps(k))
 
-        a1_rest = exact_ring[LAG][:, 2 * WIDE : 2 * WIDE + (PACK - 1) * C].rearrange("p (t s) -> p t s", s=C)
+        a1_middle = exact_ring[HEAD][:, 3 * WIDE - C : 3 * WIDE + C].rearrange("p (t s) -> p t s", s=C)
+        a1_end = exact_ring[HEAD - 1][:, SPAN - C :]
+        a1_rows = a1.rearrange("(p t) s -> p t s", t=PACK)[:, :, slots(0)]
         load_a1(0, 0, 1)
         nc.sync.dma_start(offs_sb[:], offs)
         load_dy(0)
@@ -385,10 +407,11 @@ def tile_moe_bdx_glu_sigmoid_kernel(
         load_dy(2)
         load_w2(0, 1)
         load_dy(3)
-        nc.sync.dma_start(a1_rest, a1.rearrange("(p t) s -> p t s", t=PACK)[:, 1:, slots(0)])
-        load_s2(1)
+        nc.sync.dma_start(a1_middle, a1_rows[:, 1:3, :])
+        nc.sync.dma_start(a1_end, a1_rows[:, 3, :])
         load_a3(0)
         load_w2(1, 2)
+        load_s2(1)
         load_a1(1)
         load_w2(2, 3)
         load_a3(1)
@@ -406,15 +429,16 @@ def tile_moe_bdx_glu_sigmoid_kernel(
                 turn_gate()
                 spread_gate(0)
         reorder_w2(0, nc.vector)
-        reorder_s2(0)
         gather(0, PACK - 1, nc.vector)
+        gather(1, PACK - 1, nc.scalar)
         apply_gate(0)
         spread_gate(1)
-        gather(1, PACK - 1, nc.vector)
+        reorder_s2(0)
         quantize(g_mx(0), g_words(0), width(0))
         first_product(0)
+        nc.scalar.activation(by_plane(sm(0))[:, 1:3, :], a1_middle, ACT.Sigmoid, scale=-1.0)
+        nc.scalar.activation(by_plane(sm(0))[:, 3, :], a1_end, ACT.Sigmoid, scale=-1.0)
         gather(2, PACK - 1, nc.scalar)
-        nc.scalar.activation(by_plane(sm(0))[:, 1:, :], a1_rest, ACT.Sigmoid, scale=-1.0)
         factor_y(0)
         reorder_s2(1)
         unstack_s2(1)
@@ -451,7 +475,9 @@ def tile_moe_bdx_glu_sigmoid_kernel(
             if k + 2 < LEVELS:
                 unstack_s2(k + 2)
             if k == 0:
-                load_w2(LAG + 1, W2_TURN)
+                load_w2(LAG + 1, LAG + 2)
+            if k == 1:
+                load_w2(LAG + 2, W2_TURN)
             if k == 2:
                 load_w2(W2_TURN, last + 1)
             if k == 1:
@@ -482,7 +508,7 @@ def tile_moe_bdx_glu_sigmoid_kernel(
         copy_dx(last, nc.vector)
 
         def fetch(r, c0, c1):
-            return dx[:].indirect(pos_sb[r][:, c0 // 16 : c1 // 16])
+            return dx().indirect(pos_sb[r][:, c0 // 16 : c1 // 16])
 
         one, two, three = (lodger("part", r, r, 0, T, F32) for r in range(3))
         total = in_row("total", 0, Y_AT[1], T, F32)

@@ -35,7 +35,7 @@ LIVE = 100
 LAG = 3
 AHEAD = 3
 HEAD = 3
-W2_TURN = 6
+W2_TURN = LAG + 2
 HOMES = 4
 WORDS_AT = 4 * SPAN
 W2_AT = WORDS_AT + 2 * SPAN
@@ -45,6 +45,8 @@ PACKED = 5 * WIDE
 WORD_BYTES = 2 * SPAN
 Y_AT = (WORD_BYTES, 4 * WORD_BYTES)
 WORDS_IN_ROW = (3 * WORD_BYTES, 0, 6 * WORD_BYTES)
+DA3_PLACE = [(5, WORDS_AT), (6, WORDS_AT), (8, WORDS_AT), (9, WORDS_AT), (10, WORDS_AT), (10, WORD_BYTES), (7, WORDS_AT), (7, 0)]
+EXACT_PLACE = [0, 1, 2, None, 0, 1, 3, 2, 0]
 LEVELS = (E + 1) // 2
 
 
@@ -146,10 +148,10 @@ def tile_moe_bdx_glu_sigmoid_kernel(
                 return on_shelf("words_held", 0, SPAN, BF16)
             if k == 2 * LAG:
                 return lodger("words", k, 2 * LAG + 2, WORDS_AT, SPAN, BF16)
-            return in_row("words", k, WORDS_IN_ROW[k % LAG], SPAN, BF16)
+            return in_row("words", k, WORDS_IN_ROW[0 if k == last else k % LAG], SPAN, BF16)
 
         def exact(k):
-            return on_shelf("exact_held", WORD_BYTES, SPAN, F32) if k == LAG else home(exact_ring, k)
+            return on_shelf("exact_held", WORD_BYTES, SPAN, F32) if k == LAG else exact_ring[EXACT_PLACE[k]][:, : span(k)]
 
         def w2_sb(k):
             if 1 <= k <= LAG:
@@ -265,9 +267,10 @@ def tile_moe_bdx_glu_sigmoid_kernel(
                 return by_plane(exact_ring[k][:])
             return by_plane(lodger("picked", k, k, 0, SPAN, F32)[:, : span(k)])
 
-        def gather(k, t, engine):
-            window = dy[t][:].indirect(offs_sb[:, first[k] * C // 16 : (first[k] + UNITS[k]) * C // 16])
-            plane = picked(k)[:, t, :]
+        def gather(k, t, engine, j0=0, j1=None):
+            j1 = UNITS[k] if j1 is None else j1
+            window = dy[t][:].indirect(offs_sb[:, (first[k] + j0) * C // 16 : (first[k] + j1) * C // 16])
+            plane = picked(k)[:, t, j0 * C : j1 * C]
             if engine is nc.vector:
                 nc.vector.tensor_copy(plane, window)
             else:
@@ -340,10 +343,9 @@ def tile_moe_bdx_glu_sigmoid_kernel(
                 )
 
         def da_words(k, m):
-            if m == 1 and k == late:
-                return in_row("da3_words", k, WORDS_IN_ROW[0], SPAN, BF16)
             if m == 1 and k < last:
-                return lodger("da3_words", k, k + LAG + 2, WORDS_AT, span(k), BF16)
+                room, start = DA3_PLACE[k]
+                return lodger("da3_words", k, room, start, span(k), BF16)
             return word_pair(k)[:, m * span(k) : (m + 1) * span(k)]
 
         def make_da1(k):
@@ -355,19 +357,19 @@ def tile_moe_bdx_glu_sigmoid_kernel(
             nc.scalar.copy(words_by_runs(da_words(k, 1)), planes_by_runs(by_plane(exact(k))))
 
         def da_operand(k, m, j):
-            if k == last:
-                return columns(da_mx[k], 2 * width(k), m * width(k) + j * C)
-            return columns(da_mx[k][:, m * PACKED :], width(k), j * C)
+            return columns(da_mx[k, m], width(k), j * C)
 
         def dx_ps(k):
             if k < 2:
                 return dx_bank[0][:, slots(k)]
+            if k == last:
+                return gate_bank[:, : width(k)]
             return dx_bank[(k - 1) % 3][:, : width(k)]
 
         def second_product(k):
             for j in range(UNITS[k]):
                 e = first[k] + j
-                for m in range(2):
+                for m in (1, 0):
                     codes, scales = da_operand(k, m, j)
                     nc.tensor.matmul_mx(
                         out=dx_ps(k)[:, j * C : (j + 1) * C],
@@ -375,18 +377,15 @@ def tile_moe_bdx_glu_sigmoid_kernel(
                         lhsT_scale=s13[:, e, m, :],
                         rhs=codes,
                         rhs_scale=scales,
-                        start=(m == 0),
-                        stop=(m == 1),
+                        start=(m == 1),
+                        stop=(m == 0),
                     )
 
-        def finish_da(k, place):
-            da_mx[k] = place[:, PACKED:]
-            if k == last:
-                quantize(da_mx[k], word_pair(k)[:, : 2 * span(k)], 2 * width(k))
-            else:
-                for m in range(2):
-                    quantize(da_mx[k][:, m * PACKED :], da_words(k, m), width(k))
-            second_product(k)
+        def quantize_da(k, m, place):
+            da_mx[k, m] = place
+            quantize(place, da_words(k, m), width(k))
+            if (k, 1 - m) in da_mx:
+                second_product(k)
 
         def copy_dx(k, engine):
             copy = nc.vector.tensor_copy if engine is nc.vector else nc.scalar.copy
@@ -422,9 +421,12 @@ def tile_moe_bdx_glu_sigmoid_kernel(
         for t in range(PACK - 1):
             gather(0, t, nc.vector)
             gather(1, t, nc.vector)
-            gather(2, t, nc.scalar)
             if t < 2:
+                gather(2, t, nc.scalar)
                 gather(HEAD, t, nc.scalar)
+            else:
+                gather(2, t, nc.scalar, 0, 1)
+                gather(2, t, nc.vector, 1, 2)
             if t == 1:
                 turn_gate()
                 spread_gate(0)
@@ -447,11 +449,20 @@ def tile_moe_bdx_glu_sigmoid_kernel(
         gather(HEAD, PACK - 2, nc.scalar)
         gather(HEAD, PACK - 1, nc.scalar)
 
-        finished = {k: [k - LAG] for k in range(LAG, late)}
-        finished[late] = [late - LAG, late - LAG + 1]
-        finished[last] = [late - 1, late]
+        rounded = {1: [0], 2: [1], 4: [2], 5: [3], 6: [4, 5], 7: [6], 8: [7]}
+        quantized = {
+            3: [(0, 1), (0, 0)],
+            4: [(1, 1), (1, 0)],
+            5: [(2, 0)],
+            6: [(2, 1), (3, 0)],
+            7: [(3, 1), (4, 1), (4, 0)],
+            8: [(5, 1), (5, 0), (6, 1), (6, 0), (7, 1), (7, 0)],
+        }
+        copied = {late: [1, 2], last: [3, 4]}
 
-        copied = {late: [1, 2, LAG], last: finished[late]}
+        def code_place(k, n):
+            part = n + (k < last)
+            return codes_of_step(k, "a3_room" if part < 3 else "sm_room")[:, part % 3 * PACKED :]
 
         for k in range(len(UNITS)):
             coming = k + AHEAD
@@ -467,29 +478,30 @@ def tile_moe_bdx_glu_sigmoid_kernel(
                 spread_gate(k + 2)
             exact_da3(k, opening, span(k) // BANK)
             for j in copied.get(k, []):
-                copy_dx(j, nc.scalar if j == LAG else nc.vector)
+                copy_dx(j, nc.vector)
             if k + 2 <= last:
                 sigmoid_minus(k + 2)
-            if k >= 1:
-                round_da3(k - 1)
+            for j in rounded.get(k, []):
+                round_da3(j)
             if k + 2 < LEVELS:
                 unstack_s2(k + 2)
             if k == 0:
                 load_w2(LAG + 1, LAG + 2)
             if k == 1:
-                load_w2(LAG + 2, W2_TURN)
+                load_w2(W2_TURN, W2_TURN + 1)
             if k == 2:
-                load_w2(W2_TURN, last + 1)
+                load_w2(W2_TURN + 1, last + 1)
             if k == 1:
                 load_w13()
                 spread_s13()
             if k == last - 3:
                 for r, pos in enumerate((pos1, pos2, pos3)):
                     nc.sync.dma_start(pos_sb[r][:], pos)
-            for j, room in zip(finished.get(k, []), ("a3_room", "sm_room")):
-                finish_da(j, codes_of_step(k, room))
+            for n, (j, m) in enumerate(quantized.get(k, [])):
+                quantize_da(j, m, code_place(k, n))
             if k == last:
                 round_da3(k)
+                quantize_da(k, 1, codes_of_step(last + 1, "sm_room")[:, PACKED:])
             if k + 1 < W2_TURN:
                 reorder_w2(k + 1, nc.vector)
             if k < last:
@@ -502,8 +514,9 @@ def tile_moe_bdx_glu_sigmoid_kernel(
             if coming < last:
                 for t in range(PACK):
                     gather(coming + 1, t, nc.scalar)
+        copy_dx(late - 2, nc.scalar)
         copy_dx(late - 1, nc.scalar)
-        finish_da(last, codes_of_step(last + 1, "sm_room"))
+        quantize_da(last, 0, codes_of_step(last + 1, "sm_room")[:, 2 * PACKED :])
         copy_dx(late, nc.vector)
         copy_dx(last, nc.vector)
 

@@ -29,7 +29,7 @@ UNITS = [1, 1, 2, 2, 2, 2, 2, 2, 1]
 WIDE = 2 * C
 SPAN = PACK * WIDE
 OUT_CUTS = (256, 448, 960)
-RUN = 4
+RUN = 2
 LINE = 8
 LIVE = 100
 LAG = 3

@@ -28,7 +28,7 @@ SUB = mybir.AluOpType.subtract
 UNITS = [1, 1, 2, 2, 2, 2, 2, 2, 1]
 WIDE = 2 * C
 SPAN = PACK * WIDE
-OUT_CUTS = (256, 448, 960)
+OUT_CUTS = (256, 576, 1024)
 RUN = 2
 LINE = 8
 LIVE = 100
@@ -45,7 +45,7 @@ PACKED = 5 * WIDE
 WORD_BYTES = 2 * SPAN
 Y_AT = (WORD_BYTES, 4 * WORD_BYTES)
 WORDS_IN_ROW = (3 * WORD_BYTES, 0, 6 * WORD_BYTES)
-DA3_PLACE = [(5, WORDS_AT), (6, WORDS_AT), (8, WORDS_AT), (9, WORDS_AT), (10, WORDS_AT), (10, WORD_BYTES), (7, WORDS_AT), (7, 0)]
+DA3_PLACE = [(3, WORDS_AT), (6, WORDS_AT), (8, WORDS_AT), (9, WORDS_AT), (9, WORD_BYTES), (10, WORDS_AT), (7, WORDS_AT), (7, 0)]
 EXACT_PLACE = [0, 1, 2, None, 0, 1, 3, 2, 0]
 LEVELS = (E + 1) // 2
 
@@ -221,9 +221,9 @@ def tile_moe_bdx_glu_sigmoid_kernel(
             for quad in range(1, 4):
                 nc.sync.dma_start(rows[32 * quad : 32 * quad + 4, :], rows[4 * quad : 4 * quad + 4, :])
 
-        def load_s2(b):
+        def load_s2(b, quads):
             count = (E - b + 1) // 2
-            for quad in range(4):
+            for quad in quads:
                 nc.sync.dma_start(
                     stacked[32 * quad : 32 * quad + 4 * count, b, :].bitcast(I32),
                     w2_scales[b::2, 0, 4 * quad : 4 * quad + 4, :].bitcast(I32),
@@ -401,7 +401,7 @@ def tile_moe_bdx_glu_sigmoid_kernel(
         nc.sync.dma_start(offs_sb[:], offs)
         load_dy(0)
         load_dy(1)
-        load_s2(0)
+        load_s2(0, range(4))
         nc.sync.dma_start(gate_rows[: S // GROUP, :], gate[0, :].rearrange("(b s) -> b s", s=GROUP))
         load_dy(2)
         load_w2(0, 1)
@@ -410,8 +410,9 @@ def tile_moe_bdx_glu_sigmoid_kernel(
         nc.sync.dma_start(a1_end, a1_rows[:, 3, :])
         load_a3(0)
         load_w2(1, 2)
-        load_s2(1)
+        load_s2(1, range(2))
         load_a1(1)
+        load_s2(1, range(2, 4))
         load_w2(2, 3)
         load_a3(1)
         load_a1(2)
@@ -449,7 +450,7 @@ def tile_moe_bdx_glu_sigmoid_kernel(
         gather(HEAD, PACK - 2, nc.scalar)
         gather(HEAD, PACK - 1, nc.scalar)
 
-        rounded = {1: [0], 2: [1], 4: [2], 5: [3], 6: [4, 5], 7: [6], 8: [7]}
+        rounded = {2: [1], 4: [2], 5: [3, 4], 6: [5], 7: [6], 8: [7]}
         quantized = {
             3: [(0, 1), (0, 0)],
             4: [(1, 1), (1, 0)],
@@ -479,6 +480,8 @@ def tile_moe_bdx_glu_sigmoid_kernel(
             exact_da3(k, opening, span(k) // BANK)
             for j in copied.get(k, []):
                 copy_dx(j, nc.vector)
+            if k == 0:
+                round_da3(k)
             if k + 2 <= last:
                 sigmoid_minus(k + 2)
             for j in rounded.get(k, []):

@@ -45,7 +45,7 @@ PACKED = 5 * WIDE
 WORD_BYTES = 2 * SPAN
 Y_AT = (WORD_BYTES, 4 * WORD_BYTES)
 WORDS_IN_ROW = (3 * WORD_BYTES, 0, 6 * WORD_BYTES)
-DA3_PLACE = [(3, WORDS_AT), (6, WORDS_AT), (8, WORDS_AT), (9, WORDS_AT), (9, WORD_BYTES), (10, WORDS_AT), (7, WORDS_AT), (7, 0)]
+DA3_PLACE = [(3, 0), (6, WORDS_AT), (8, WORDS_AT), (9, WORDS_AT), (9, WORD_BYTES), (10, WORDS_AT), (7, WORDS_AT), (7, 0)]
 EXACT_PLACE = [0, 1, 2, None, 0, 1, 3, 2, 0]
 LEVELS = (E + 1) // 2
 
@@ -182,6 +182,8 @@ def tile_moe_bdx_glu_sigmoid_kernel(
         def a1_home(k):
             if k == 0:
                 return by_plane(sm(0))
+            if k == 1:
+                return by_plane(lodger("a1_sb", k, k + 2, 0, span(k), F32))
             return by_plane(lodger("a1_sb", k, k + 2, A1_AT, SPAN, F32)[:, : span(k)])
 
         def load_rows(place, rows, k, t0=0, t1=PACK):
@@ -414,8 +416,9 @@ def tile_moe_bdx_glu_sigmoid_kernel(
         load_a1(1)
         load_s2(1, range(2, 4))
         load_w2(2, 3)
+        load_a1(2, 0, 2)
         load_a3(1)
-        load_a1(2)
+        load_a1(2, 2, PACK)
         load_s13()
 
         sigmoid_minus(0, 0, 1)
@@ -457,7 +460,7 @@ def tile_moe_bdx_glu_sigmoid_kernel(
             5: [(2, 0)],
             6: [(2, 1), (3, 0)],
             7: [(3, 1), (4, 1), (4, 0)],
-            8: [(5, 1), (5, 0), (6, 1), (6, 0), (7, 1), (7, 0)],
+            8: [(5, 1), (5, 0), (6, 1), (6, 0), (7, 0), (7, 1)],
         }
         copied = {late: [1, 2], last: [3, 4]}
 
@@ -482,7 +485,9 @@ def tile_moe_bdx_glu_sigmoid_kernel(
                 copy_dx(j, nc.vector)
             if k == 0:
                 round_da3(k)
-            if k + 2 <= last:
+                sigmoid_minus(2, 0, 2)
+                sigmoid_minus(2, 2, PACK)
+            elif k + 2 <= last:
                 sigmoid_minus(k + 2)
             for j in rounded.get(k, []):
                 round_da3(j)
@@ -504,7 +509,6 @@ def tile_moe_bdx_glu_sigmoid_kernel(
                 quantize_da(j, m, code_place(k, n))
             if k == last:
                 round_da3(k)
-                quantize_da(k, 1, codes_of_step(last + 1, "sm_room")[:, PACKED:])
             if k + 1 < W2_TURN:
                 reorder_w2(k + 1, nc.vector)
             if k < last:
@@ -519,6 +523,7 @@ def tile_moe_bdx_glu_sigmoid_kernel(
                     gather(coming + 1, t, nc.scalar)
         copy_dx(late - 2, nc.scalar)
         copy_dx(late - 1, nc.scalar)
+        quantize_da(last, 1, codes_of_step(last + 1, "sm_room")[:, PACKED:])
         quantize_da(last, 0, codes_of_step(last + 1, "sm_room")[:, 2 * PACKED :])
         copy_dx(late, nc.vector)
         copy_dx(last, nc.vector)

from contextlib import ExitStack

import concourse.mybir as mybir
from concourse.masks import make_identity

K, T, E, C, H, N = 128, 1280, 15, 256, 512, 512
S = E * C
P = 128
PACK = 4
GROUP = 128
BANK = 512
FLOPS = 2 * S * (N * H + 2 * H * K)
BYTES = 4 * (N * T + 2 * H * S + S + K * T) + E * (N * H + 2 * H * K) * 17 // 32 + 2 * P * (S + 3 * T) // 16

F32 = mybir.dt.float32
BF16 = mybir.dt.bfloat16
I32 = mybir.dt.int32
U32 = mybir.dt.uint32
U16 = mybir.dt.uint16
U8 = mybir.dt.uint8
FP8X4 = mybir.dt.float8_e4m3fn_x4
FP4X4 = mybir.dt.float4_e2m1fn_x4
ACT = mybir.ActivationFunctionType
MULT = mybir.AluOpType.mult
ADD = mybir.AluOpType.add
SUB = mybir.AluOpType.subtract

UNITS = [1, 1, 2, 2, 2, 2, 2, 2, 1]
WIDE = 2 * C
SPAN = PACK * WIDE
OUT_CUTS = (256, 576, 1024)
RUN = 2
LINE = 8
LIVE = 100
LAG = 3
AHEAD = 3
HEAD = 3
W2_TURN = LAG + 2
HOMES = 4
WORDS_AT = 4 * SPAN
W2_AT = WORDS_AT + 2 * SPAN
ROOM = W2_AT + 4 * H
A1_AT = ROOM - 4 * SPAN
PACKED = 5 * WIDE
WORD_BYTES = 2 * SPAN
Y_AT = (WORD_BYTES, 4 * WORD_BYTES)
WORDS_IN_ROW = (3 * WORD_BYTES, 0, 6 * WORD_BYTES)
DA3_PLACE = [(3, 0), (6, WORDS_AT), (8, WORDS_AT), (9, WORDS_AT), (9, WORD_BYTES), (10, WORDS_AT), (7, WORDS_AT), (7, 0)]
EXACT_PLACE = [0, 1, 2, None, 0, 1, 3, 2, 0]
LEVELS = (E + 1) // 2


def planes_by_runs(ap):
    return ap.rearrange("p t (c i) -> p c t i", i=RUN)


def words_by_runs(ap):
    return ap.rearrange("p (c i t) -> p c t i", i=RUN, t=PACK)


def tile_moe_bdx_glu_sigmoid_kernel(
    tc, dyT, a1, a3, w2_words, w2_scales, w1_words, w1_scales, w3_words, w3_scales, gate, offs, pos1, pos2, pos3, out
):
    nc = tc.nc
    first = [sum(UNITS[:k]) for k in range(len(UNITS))]
    last = len(UNITS) - 1
    late = last - 1

    with ExitStack() as ctx:
        keep = ctx.enter_context(tc.tile_pool(name="keep", bufs=1))
        rooms = ctx.enter_context(tc.tile_pool(name="rooms", bufs=1))
        row = ctx.enter_context(tc.tile_pool(name="row", bufs=1))
        shelf = ctx.enter_context(tc.tile_pool(name="shelf", bufs=1))
        psum = ctx.enter_context(tc.psum_pool(name="psum", bufs=1))

        def ring(name, count, columns, dtype):
            return [keep.tile([P, columns], dtype, name="%s%d" % (name, r), align_bytes=64) for r in range(count)]

        exact_ring = ring("exact", LAG + 1, SPAN, F32)
        dh_bank = [psum.tile([P, BANK], F32, name="dh_bank%d" % r) for r in range(4)]
        gate_bank = psum.tile([P, BANK], F32, name="gate_bank")
        dx_bank = [psum.tile([P, BANK], F32, name="dx_bank%d" % r) for r in range(3)]

        offs_sb = keep.tile([P, S // 16], U16, name="offs_sb")
        pos_sb = [keep.tile([P, T // 16], U16, name="pos_sb%d" % r) for r in range(3)]
        dy = [keep.tile([P, T], F32, name="dy%d" % t) for t in range(PACK)]
        stacked = shelf.tile([P, 2, H], U8, name="stacked", offset=2 * WORD_BYTES, align_bytes=64)
        s2_levels = keep.tile([P, 2, H], U8, name="s2_levels", align_bytes=64)
        s2_all = keep.tile([P, (E - 2) * H], U8, name="s2_all", align_bytes=64)
        w13 = [keep.tile([P, E, 2 * K], U8, name="w13_%d" % m, align_bytes=64) for m in range(2)]
        s13 = keep.tile([P, E, 2, K], U8, name="s13", align_bytes=64)
        ident = keep.tile([P, P], F32, name="ident")
        gate_rows = keep.tile([P, GROUP], F32, name="gate_rows")
        gate_cols = keep.tile([P, S // GROUP], F32, name="gate_cols")

        nc.vector.memset(gate_rows[:], 0.0)
        nc.vector.memset(stacked[:, 1, :].bitcast(I32), 0)
        make_identity(nc, ident[:])
        nc.gpsimd.memset(s2_all[96:, :].bitcast(I32), 0)
        nc.gpsimd.memset(s13[:].bitcast(I32), 0)

        w2_raw, da_mx, tenants = {}, {}, {}

        def width(k):
            return UNITS[k] * C

        def span(k):
            return PACK * width(k)

        def slots(k):
            return slice(first[k] * C, (first[k] + UNITS[k]) * C)

        def home(tiles, k):
            return tiles[k % len(tiles)][:, : span(k)]

        def tenant(name, room, k, columns, dtype):
            if (name, room, k) not in tenants:
                tenants[name, room, k] = keep.tile(
                    [P, columns], dtype, tag="%s%d" % (room, k % AHEAD), name=name, align_bytes=64
                )
            return tenants[name, room, k][:]

        def lodger(name, k, room, start, columns, dtype):
            if (name, k) not in tenants:
                tenants[name, k] = rooms.tile(
                    [P, columns], dtype, name="%s%d" % (name, k), offset=room % HOMES * ROOM + start, align_bytes=64
                )
            return tenants[name, k][:]

        def in_row(name, k, start, columns, dtype):
            if (name, k) not in tenants:
                tenants[name, k] = row.tile([P, columns], dtype, name="%s%d" % (name, k), offset=start, align_bytes=64)
            return tenants[name, k][:]

        def on_shelf(name, start, columns, dtype):
            if name not in tenants:
                tenants[name] = shelf.tile([P, columns], dtype, name=name, offset=start, align_bytes=64)
            return tenants[name][:]

        def dx():
            return on_shelf("dx", 0, S, F32)

        def y_sb(k):
            return in_row("y", k, Y_AT[k % 2], span(k), F32)

        def word_pair(k):
            if k == LAG:
                return on_shelf("words_held", 0, SPAN, BF16)
            if k == 2 * LAG:
                return lodger("words", k, 2 * LAG + 2, WORDS_AT, SPAN, BF16)
            return in_row("words", k, WORDS_IN_ROW[0 if k == last else k % LAG], SPAN, BF16)

        def exact(k):
            return on_shelf("exact_held", WORD_BYTES, SPAN, F32) if k == LAG else exact_ring[EXACT_PLACE[k]][:, : span(k)]

        def w2_sb(k):
            if 1 <= k <= LAG:
                return codes_of_step(k - 1, "a3_room")[:, PACKED : PACKED + UNITS[k] * 2 * H]
            if LAG < k < W2_TURN:
                return tenant("w2_sb", "sm_room", k - 1, UNITS[k] * 2 * H, U8)
            return lodger("w2_sb", k, k + 1, W2_AT, UNITS[k] * 2 * H, U8)

        def sm(k):
            return tenant("sm", "sm_room", k, span(k), F32)

        def a3_sb(k):
            if k == 0:
                return on_shelf("a3_first", WORD_BYTES, span(0), F32)
            return tenant("a3_sb", "a3_room", k, span(k), F32)

        def codes_of_step(k, room):
            if k == 0:
                return on_shelf("codes_first", WORD_BYTES + WORD_BYTES // 2, 2 * PACKED, U8)
            return tenant("codes", room, k, 3 * PACKED, U8)

        def by_plane(ap):
            return ap.rearrange("p (t s) -> p t s", t=PACK)

        def load_dy(t):
            nc.sync.dma_start(dy[t][:], dyT.rearrange("(p t) c -> p t c", t=PACK)[:, t, :])

        def a1_home(k):
            if k == 0:
                return by_plane(sm(0))
            if k == 1:
                return by_plane(lodger("a1_sb", k, k + 2, 0, span(k), F32))
            return by_plane(lodger("a1_sb", k, k + 2, A1_AT, SPAN, F32)[:, : span(k)])

        def load_rows(place, rows, k, t0=0, t1=PACK):
            nc.sync.dma_start(place[:, t0:t1, :], rows.rearrange("(p t) s -> p t s", t=PACK)[:, t0:t1, slots(k)])

        def load_a1(k, t0=0, t1=PACK):
            load_rows(a1_home(k), a1, k, t0, t1)

        def load_a3(k):
            load_rows(by_plane(a3_sb(k)), a3, k)

        def load_w2(k0, k1):
            e0, e1 = first[k0], first[k1 - 1] + UNITS[k1 - 1]
            if 1 <= k0 <= LAG:
                flat = in_row("w2_raw", k0, WORDS_IN_ROW[k0 - 1], (e1 - e0) * 2 * H, U8)
            elif k0 == LAG + 1:
                flat = on_shelf("w2_raw_held", 0, (e1 - e0) * 2 * H, U8)
            else:
                flat = keep.tile([P, (e1 - e0) * 2 * H], U8, name="w2_raw%d" % e0, align_bytes=64)[:]
            raw = flat.rearrange("p (e b) -> p e b", b=2 * H)
            nc.sync.dma_start(raw.bitcast(I32), w2_words[e0:e1, 0, :, :].rearrange("e p b -> p e b").bitcast(I32))
            for k in range(k0, k1):
                w2_raw[k] = raw[:, first[k] - e0 : first[k] - e0 + UNITS[k], :]

        def load_w13():
            for m, packed in enumerate((w1_words, w3_words)):
                nc.sync.dma_start(w13[m][:].bitcast(I32), packed[:, 0, :, :].rearrange("e p b -> p e b").bitcast(I32))

        def load_s13():
            for m, scales in enumerate((w1_scales, w3_scales)):
                nc.gpsimd.dma_start(
                    s13[:16, :, m, :].bitcast(I32), scales[:, 0, :, :].rearrange("e f n -> f e n").bitcast(I32)
                )

        def spread_s13():
            rows = s13[:].rearrange("p e m n -> p (e m n)").bitcast(I32)
            for quad in range(1, 4):
                nc.sync.dma_start(rows[32 * quad : 32 * quad + 4, :], rows[4 * quad : 4 * quad + 4, :])

        def load_s2(b, quads):
            count = (E - b + 1) // 2
            for quad in quads:
                nc.sync.dma_start(
                    stacked[32 * quad : 32 * quad + 4 * count, b, :].bitcast(I32),
                    w2_scales[b::2, 0, 4 * quad : 4 * quad + 4, :].bitcast(I32),
                )

        def reorder_s2(b):
            nc.vector.tensor_copy(
                s2_levels[:, b, :].rearrange("p (t m) -> p t m", t=PACK),
                stacked[:, b, :].rearrange("p (m t) -> p t m", t=PACK),
            )

        def s2_plane(e):
            if e < 2:
                return s2_levels[:, e, :]
            return s2_all[:, (e - 2) * H : (e - 1) * H]

        def unstack_s2(level):
            count = min(2, E - 2 * level)
            nc.sync.dma_start(
                s2_all[:LIVE, (2 * level - 2) * H : (2 * level - 2 + count) * H].bitcast(I32),
                s2_levels[4 * level : 4 * level + LIVE, :count, :].rearrange("p b n -> p (b n)").bitcast(I32),
            )

        def turn_gate():
            nc.tensor.transpose(dx_bank[2][:, :GROUP], gate_rows[:], ident[:])
            nc.scalar.activation(gate_cols[:], dx_bank[2][:, : S // GROUP], ACT.Copy, scale=-1.0)

        def spread_gate(k):
            for j in range(width(k) // GROUP):
                col = first[k] * C // GROUP + j
                nc.tensor.transpose(
                    gate_bank[:, j * GROUP : (j + 1) * GROUP],
                    gate_cols[:, col : col + 1].to_broadcast([P, P]),
                    ident[:],
                )

        def picked(k):
            if k == 0:
                return by_plane(on_shelf("picked_first", 0, span(0), F32))
            if k in (HEAD - 1, HEAD):
                return by_plane(exact_ring[k][:])
            return by_plane(lodger("picked", k, k, 0, SPAN, F32)[:, : span(k)])

        def gather(k, t, engine, j0=0, j1=None):
            j1 = UNITS[k] if j1 is None else j1
            window = dy[t][:].indirect(offs_sb[:, (first[k] + j0) * C // 16 : (first[k] + j1) * C // 16])
            plane = picked(k)[:, t, j0 * C : j1 * C]
            if engine is nc.vector:
                nc.vector.tensor_copy(plane, window)
            else:
                nc.scalar.activation(plane, window, ACT.Copy)

        def g_words(k):
            return in_row("g_words", k, Y_AT[k % 2], span(k), BF16)

        def apply_gate(k):
            runs = width(k) // RUN
            row = gate_bank[:, : width(k)].rearrange("p (c i) -> p c i", i=RUN)
            nc.vector.tensor_tensor(
                words_by_runs(g_words(k)),
                planes_by_runs(picked(k)),
                row.unsqueeze(2).to_broadcast([P, runs, PACK, RUN]),
                MULT,
            )

        def sigmoid_minus(k, t0=0, t1=PACK):
            nc.scalar.activation(by_plane(sm(k))[:, t0:t1, :], a1_home(k)[:, t0:t1, :], ACT.Sigmoid, scale=-1.0)

        def factor_y(k):
            nc.gpsimd.tensor_tensor(y_sb(k), a3_sb(k), sm(k), MULT)

        def reorder_w2(k, engine):
            copy = nc.vector.tensor_copy if engine is nc.vector else nc.scalar.copy
            copy(
                w2_sb(k).bitcast(U16).rearrange("p (e t c i) -> p e c t i", t=PACK, i=LINE, c=P // LINE),
                w2_raw[k].bitcast(U16).rearrange("p e (c i t) -> p e c t i", t=PACK, i=LINE),
            )

        def quantize(packed, words, count):
            nc.vector.quantize_mx(
                out=packed[:, : 4 * count].bitcast(U32).bitcast(FP8X4), scales=packed[:, 4 * count : 5 * count], in_=words
            )

        def columns(packed, count, start):
            return (
                packed[:, 4 * start : 4 * (start + C)].bitcast(U32).bitcast(FP8X4),
                packed[:, 4 * count + start : 4 * count + start + C],
            )

        def g_mx(k):
            return codes_of_step(k - 1, "a3_room")[:, :PACKED]

        def dh_part(k, b):
            return dh_bank[(2 * (k == last) + b) % 4]

        def first_product(k):
            for t in range(PACK):
                for j in range(UNITS[k]):
                    place = t * width(k) + j * C
                    start = j * 2 * H + 2 * P * t
                    codes, scales = columns(g_mx(k), width(k), j * C)
                    nc.tensor.matmul_mx(
                        out=dh_part(k, place // BANK)[:, place % BANK : place % BANK + C],
                        lhsT=w2_sb(k)[:, start : start + 2 * P].bitcast(FP4X4),
                        lhsT_scale=s2_plane(first[k] + j)[:, P * t : P * (t + 1)],
                        rhs=codes,
                        rhs_scale=scales,
                        start=True,
                        stop=True,
                    )

        def exact_da3(k, b0, b1):
            for b in range(b0, b1):
                part = slice(b * BANK, (b + 1) * BANK)
                nc.vector.scalar_tensor_tensor(
                    exact(k)[:, part], sm(k)[:, part], 1.0, dh_part(k, b)[:], SUB, MULT
                )

        def da_words(k, m):
            if m == 1 and k < last:
                room, start = DA3_PLACE[k]
                return lodger("da3_words", k, room, start, span(k), BF16)
            return word_pair(k)[:, m * span(k) : (m + 1) * span(k)]

        def make_da1(k):
            nc.vector.tensor_tensor(
                words_by_runs(da_words(k, 0)), planes_by_runs(by_plane(exact(k))), planes_by_runs(by_plane(y_sb(k))), MULT
            )

        def round_da3(k):
            nc.scalar.copy(words_by_runs(da_words(k, 1)), planes_by_runs(by_plane(exact(k))))

        def da_operand(k, m, j):
            return columns(da_mx[k, m], width(k), j * C)

        def dx_ps(k):
            if k < 2:
                return dx_bank[0][:, slots(k)]
            if k == last:
                return gate_bank[:, : width(k)]
            return dx_bank[(k - 1) % 3][:, : width(k)]

        def second_product(k):
            for j in range(UNITS[k]):
                e = first[k] + j
                for m in (1, 0):
                    codes, scales = da_operand(k, m, j)
                    nc.tensor.matmul_mx(
                        out=dx_ps(k)[:, j * C : (j + 1) * C],
                        lhsT=w13[m][:, e, :].bitcast(FP4X4),
                        lhsT_scale=s13[:, e, m, :],
                        rhs=codes,
                        rhs_scale=scales,
                        start=(m == 1),
                        stop=(m == 0),
                    )

        def quantize_da(k, m, place):
            da_mx[k, m] = place
            quantize(place, da_words(k, m), width(k))
            if (k, 1 - m) in da_mx:
                second_product(k)

        def copy_dx(k, engine):
            copy = nc.vector.tensor_copy if engine is nc.vector else nc.scalar.copy
            if k == 1:
                copy(dx()[:, :BANK], dx_bank[0][:])
            else:
                copy(dx()[:, slots(k)], dx_ps(k))

        a1_middle = exact_ring[HEAD][:, 3 * WIDE - C : 3 * WIDE + C].rearrange("p (t s) -> p t s", s=C)
        a1_end = exact_ring[HEAD - 1][:, SPAN - C :]
        a1_rows = a1.rearrange("(p t) s -> p t s", t=PACK)[:, :, slots(0)]
        load_a1(0, 0, 1)
        nc.sync.dma_start(offs_sb[:], offs)
        load_dy(0)
        load_dy(1)
        load_s2(0, range(4))
        nc.sync.dma_start(gate_rows[: S // GROUP, :], gate[0, :].rearrange("(b s) -> b s", s=GROUP))
        load_dy(2)
        load_w2(0, 1)
        load_dy(3)
        nc.sync.dma_start(a1_middle, a1_rows[:, 1:3, :])
        nc.sync.dma_start(a1_end, a1_rows[:, 3, :])
        load_a3(0)
        load_w2(1, 2)
        load_s2(1, range(2))
        load_a1(1)
        load_s2(1, range(2, 4))
        load_w2(2, 3)
        load_a1(2, 0, 2)
        load_a3(1)
        load_a1(2, 2, PACK)
        load_s13()

        sigmoid_minus(0, 0, 1)
        for t in range(PACK - 1):
            gather(0, t, nc.vector)
            gather(1, t, nc.vector)
            if t < 2:
                gather(2, t, nc.scalar)
                gather(HEAD, t, nc.scalar)
            else:
                gather(2, t, nc.scalar, 0, 1)
                gather(2, t, nc.vector, 1, 2)
            if t == 1:
                turn_gate()
                spread_gate(0)
        reorder_w2(0, nc.vector)
        gather(0, PACK - 1, nc.vector)
        gather(1, PACK - 1, nc.scalar)
        apply_gate(0)
        spread_gate(1)
        reorder_s2(0)
        quantize(g_mx(0), g_words(0), width(0))
        first_product(0)
        nc.scalar.activation(by_plane(sm(0))[:, 1:3, :], a1_middle, ACT.Sigmoid, scale=-1.0)
        nc.scalar.activation(by_plane(sm(0))[:, 3, :], a1_end, ACT.Sigmoid, scale=-1.0)
        gather(2, PACK - 1, nc.scalar)
        factor_y(0)
        reorder_s2(1)
        unstack_s2(1)
        load_w2(3, 4)
        sigmoid_minus(1)
        gather(HEAD, PACK - 2, nc.scalar)
        gather(HEAD, PACK - 1, nc.scalar)

        rounded = {2: [1], 4: [2], 5: [3, 4], 6: [5], 7: [6], 8: [7]}
        quantized = {
            3: [(0, 1), (0, 0)],
            4: [(1, 1), (1, 0)],
            5: [(2, 0)],
            6: [(2, 1), (3, 0)],
            7: [(3, 1), (4, 1), (4, 0)],
            8: [(5, 1), (5, 0), (6, 1), (6, 0), (7, 0), (7, 1)],
        }
        copied = {late: [1, 2], last: [3, 4]}

        def code_place(k, n):
            part = n + (k < last)
            return codes_of_step(k, "a3_room" if part < 3 else "sm_room")[:, part % 3 * PACKED :]

        for k in range(len(UNITS)):
            coming = k + AHEAD
            opening = int(1 <= k < last)
            exact_da3(k, 0, opening)
            if k < last:
                apply_gate(k + 1)
            if k + 2 <= last:
                load_a3(k + 2)
            if k + HOMES - 1 <= last:
                load_a1(k + HOMES - 1)
            if k + 2 <= last:
                spread_gate(k + 2)
            exact_da3(k, opening, span(k) // BANK)
            for j in copied.get(k, []):
                copy_dx(j, nc.vector)
            if k == 0:
                round_da3(k)
                sigmoid_minus(2, 0, 2)
                sigmoid_minus(2, 2, PACK)
            elif k + 2 <= last:
                sigmoid_minus(k + 2)
            for j in rounded.get(k, []):
                round_da3(j)
            if k + 2 < LEVELS:
                unstack_s2(k + 2)
            if k == 0:
                load_w2(LAG + 1, LAG + 2)
            if k == 1:
                load_w2(W2_TURN, W2_TURN + 1)
            if k == 2:
                load_w2(W2_TURN + 1, last + 1)
            if k == 1:
                load_w13()
                spread_s13()
            if k == last - 3:
                for r, pos in enumerate((pos1, pos2, pos3)):
                    nc.sync.dma_start(pos_sb[r][:], pos)
            for n, (j, m) in enumerate(quantized.get(k, [])):
                quantize_da(j, m, code_place(k, n))
            if k == last:
                round_da3(k)
            if k + 1 < W2_TURN:
                reorder_w2(k + 1, nc.vector)
            if k < last:
                quantize(g_mx(k + 1), g_words(k + 1), width(k + 1))
                first_product(k + 1)
                factor_y(k + 1)
            make_da1(k)
            if W2_TURN <= coming <= last:
                reorder_w2(coming, nc.scalar)
            if coming < last:
                for t in range(PACK):
                    gather(coming + 1, t, nc.scalar)
        copy_dx(late - 2, nc.scalar)
        copy_dx(late - 1, nc.scalar)
        quantize_da(last, 1, codes_of_step(last + 1, "sm_room")[:, PACKED:])
        quantize_da(last, 0, codes_of_step(last + 1, "sm_room")[:, 2 * PACKED :])
        copy_dx(late, nc.vector)
        copy_dx(last, nc.vector)

        def fetch(r, c0, c1):
            return dx().indirect(pos_sb[r][:, c0 // 16 : c1 // 16])

        one, two, three = (lodger("part", r, r, 0, T, F32) for r in range(3))
        total = in_row("total", 0, Y_AT[1], T, F32)
        c1, c2, c3 = OUT_CUTS
        nc.vector.tensor_copy(two[:, :c1], fetch(1, 0, c1))
        for c0, c4 in ((c1, c2), (0, c1), (c2, c3), (c3, T)):
            nc.scalar.activation(one[:, c0:c4], fetch(0, c0, c4), ACT.Copy)
        for c0, c4 in ((c2, c3), (c3, T)):
            nc.scalar.activation(two[:, c0:c4], fetch(1, c0, c4), ACT.Copy)
        nc.vector.tensor_tensor(three[:, :c1], fetch(2, 0, c1), two[:, :c1], ADD)
        nc.vector.tensor_tensor(two[:, c1:c2], fetch(1, c1, c2), one[:, c1:c2], ADD)
        nc.vector.tensor_tensor(total[:, :c1], three[:, :c1], one[:, :c1], ADD)
        nc.vector.tensor_tensor(total[:, c1:c2], fetch(2, c1, c2), two[:, c1:c2], ADD)
        nc.sync.dma_start(out[:, :c2], total[:, :c2])
        for c0, c4 in ((c2, c3), (c3, T)):
            nc.vector.tensor_tensor(three[:, c0:c4], fetch(2, c0, c4), one[:, c0:c4], ADD)
        for c0, c4 in ((c2, c3), (c3, T)):
            nc.vector.tensor_tensor(total[:, c0:c4], three[:, c0:c4], two[:, c0:c4], ADD)
            nc.sync.dma_start(out[:, c0:c4], total[:, c0:c4])
